import numpy as np, ml_dtypes
CORES = [48,51,52,55]
N = 4
BF = ml_dtypes.bfloat16
W, C, RO, SH = 4096, 256, 6, 4
def parts(rng):
    cov = np.where(rng.random((N, 8, 1, W)) < 0.15, 0, rng.integers(0, 256, (N, 8, 16, W)))
    share = rng.choice(np.array([0.0, 0.1, 0.2, 0.3, 0.5, 0.8]), (N, 8, 1, C))
    tst = np.where(rng.random((N, 8, 16, C)) < share, 256, rng.integers(0, 256, (N, 8, 16, C)))
    return cov, tst, rng.integers(0, 160, (N, 8, 16, C)), rng.integers(200, 2000, (N, 8))
def pack(cov, tst, pr, th):
    return {"cov": np.ascontiguousarray(cov.reshape(N, 128, W)).astype(np.float32).astype(BF), "tst": np.ascontiguousarray(tst.reshape(N, 128, C)).astype(np.int32),
            "pr": np.ascontiguousarray(pr.reshape(N, 128, C)).astype(np.float32).astype(BF), "th": np.ascontiguousarray(th.reshape(N, 8, 1)).astype(np.int32)}
def setup_inputs(rng):
    return pack(*parts(rng))
def setup_inputs_corners(rng):
    cov, tst, pr, th = parts(rng)
    c = np.arange(C); lane = np.arange(16)[:, None]; full = rng.integers(0, 256, (N, 8, 16, C))
    th = rng.choice(np.array([0, 1, 500, 4080]), (N, 8))
    for r in range(N):
        for g in range(8):
            k = (g + r) % 8; x = full[r, g]
            if k == 1: x = np.full((16, C), 256)
            elif k == 2: x = np.where(lane == c % 16, 256, x)
            elif k == 3: x = np.where((lane + c) % 2 == 1, 256, x)
            elif k == 4:
                x = np.repeat(x[:, :1], C, axis=1); pr[r, g] = np.repeat(pr[r, g][:, :1], C, axis=1); th[r, g] = 0
            elif k == 5: x = np.where((lane == c % 16) | (lane == (c + 1) % 16), x, 256)
            elif k == 6:
                cov[r, g][:, rng.random(W) < 0.7] = 0; th[r, g] = 0
            elif k == 7: pr[r, g] = 255 * rng.integers(0, 2, (1, C))
            tst[r, g] = x
    q = rng.permutation(N); th[q[0]] = 0; th[q[1]] = 4080
    r = int(q[0]); g = (8 - r) % 8
    cov[r, g, 0] = 0; cov[r, g, 1:] = rng.integers(1, 256, (15, W))
    pr[r, g, :, 0::2] = 255; pr[r, g, :, 1::2] = 0
    k = np.arange(C // 2); p = 1 + k % 14; v = rng.integers(0, 256, (2, C // 2)); x = np.full((16, C), 256)
    for odd in range(2):
        x[p, 2 * k + odd] = v[0]; x[p + 1, 2 * k + odd] = v[1]
    tst[r, g] = x
    return pack(cov, tst, pr, th)
def pairs(rng, low):
    x = rng.integers(0, 256, 2 ** 15); y = rng.integers(0, 256, 2 ** 15); i = rng.integers(0, 16, 2 ** 15)
    col, at = np.unique(((((2 * x + 1) * (2 * y + 1)) >> 4) + 613 * i) & (W - 1), return_index=True)
    at = rng.permutation(at[col >= low])
    return x[at], y[at], i[at]
def lone(rng, x, y, i):
    k = len(x); c = np.arange(k); v = np.full((16, k), 256)
    v[i, c] = x; v[(i + 1) & 15, c] = y
    for d in range(3, 15, 2): v[(i + d) & 15, c] = rng.integers(0, 256, k)
    return v
def setup_inputs_crowd(rng):
    cov, tst, pr, th = parts(rng)
    a = int(rng.integers(0, N)); b = (a + 1) % N; d = (a + 2) % N
    v = rng.integers(0, 256, (8, 16, C)); v[:, [1, 5, 7, 9, 11, 13, 15]] = 256
    tst[a] = v; th[a] = rng.integers(511, 1500, 8); th[b] = 0; th[d] = 0
    cov[b] = rng.integers(1, 256, (8, 16, W)); cov[d] = rng.integers(1, 256, (8, 16, W))
    c = np.arange(C); second = ((c % 2 == 0) & (c > 0)) | (c == C - 1)
    for g in range(8):
        p = np.append(rng.permutation(C - 1)[:31], C - 1)
        few = ((((2 * v[g, 2, p] + 1) * (2 * v[g, 3, p] + 1)) >> 4) + 613 * 2) & (W - 1)
        most = ((((2 * v[g, 3, p] + 1) * (2 * v[g, 4, p] + 1)) >> 4) + 613 * 3) & (W - 1)
        cov[a, g][:, few] = 255; cov[a, g][int(rng.integers(0, 16)), few] = 254; cov[a, g][:, most] = 255
        x, y, i = pairs(rng, 0)
        tst[b, g] = lone(rng, x[:C], y[:C], i[:C])
        x, y, i = pairs(rng, W - 254 if g == 7 else 0)
        o = (c + 1) // 2; o[C - 1] = 0; o = np.where(o > 0, 1 + (o - 1) % (len(x) - 1), 0)
        tst[d, g] = lone(rng, x[o], y[o], i[o])
        lev = rng.integers(0, 16, C // 2)[o]; lev = np.where(second, (lev + rng.integers(1, 16, C)) & 15, lev)
        pr[d, g] = np.where(np.arange(16)[:, None] == lev[None, :], 0, 255)
    return pack(cov, tst, pr, th)
def setup_inputs_ties(rng):
    unit = np.where(np.arange(8) % 4 == 1, 1, 85).reshape(1, 8, 1, 1)
    cov = unit * np.where(rng.random((N, 8, 1, W)) < 0.5, rng.integers(0, 4, (N, 8, 1, W)), rng.integers(0, 4, (N, 8, 16, W)))
    pr = unit * np.where(rng.random((N, 8, 1, C)) < 0.5, rng.integers(0, 2, (N, 8, 1, C)), rng.integers(0, 2, (N, 8, 16, C)))
    few = rng.choice(np.array([0, 1, 64, 128, 255, 256]), (N, 8, 16, C)); many = np.where(rng.random((N, 8, 16, C)) < 0.2, 256, rng.integers(0, 256, (N, 8, 16, C)))
    tst = np.where(rng.random((N, 8, 1, C)) < 0.5, few, many)
    return pack(cov, tst, pr, unit[..., 0, 0] * rng.integers(0, 24, (N, 8)))
def setup_inputs_spread(rng):
    cov = np.minimum((np.exp2(8 * rng.random((N, 8, 1, W))) * rng.random((N, 8, 16, W)) * 1.01).astype(np.int64), 255)
    pr = np.minimum((np.exp2(8 * rng.random((N, 8, 16, C))) * rng.random((N, 8, 1, C))).astype(np.int64), 255)
    tst = np.minimum((256 * rng.random((N, 8, 16, C)) ** rng.choice(np.array([0.25, 1.0, 4.0]), (N, 8, 16, 1))).astype(np.int64), 255)
    tst = np.where(rng.random((N, 8, 16, C)) < rng.random((N, 8, 1, C)) * 0.6, 256, tst)
    th = np.minimum(np.exp2(12 * rng.random((N, 8))).astype(np.int64) - 1, 4080)
    return pack(cov, tst, pr, th)
def setup_inputs_ends(rng):
    kind = rng.integers(0, 3, (N, 8, 1, W)); cov = 255 * np.where(kind == 2, rng.integers(0, 2, (N, 8, 16, W)), kind)
    lane = np.arange(16)
    for t in range(RO):
        z = (613 * lane + 77 * t) & (W - 1); f = ((511 * 511 >> 4) + 613 * lane + 77 * t) & (W - 1)
        cov[..., z] = 255; cov[..., f] = 0; cov[..., f[15]] = 255; cov[:, ::2, :, f[6]] = 255
    u = rng.random((N, 8, 16, C))
    tst = np.where(u < 0.5, 0, np.where(u < 0.7, 256, np.where(u < 0.9, 255, rng.integers(0, 256, (N, 8, 16, C)))))
    tst[..., [2, C - 1]] = 0; tst[..., [5, C - 2]] = 255; tst[..., [1, C - 3]] = 256
    pr = 255 * rng.integers(0, 2, (N, 8, 16, C))
    pr[..., [2, 5, C - 2, C - 1]] = 255; pr[:, :, 15, [2, 5, C - 2, C - 1]] = 0; pr[:, 1::2, 4, [2, C - 1]] = 0
    o = np.argsort(rng.random((N, 8)), axis=1); th = 4080 * (o < rng.integers(3, 6, (N, 1))).astype(np.int64)
    th[N - 1, 7] = 4080; th[N - 1, 0] = 0
    return pack(cov, tst, pr, th)
def check_inputs(d):
    bad = []
    for k, lo, hi in (("cov", 0, 255), ("tst", 0, 256), ("pr", 0, 255), ("th", 0, 4080)):
        v = np.asarray(d[k]).astype(np.float64)
        if not (np.min(v) >= lo and np.max(v) <= hi): bad.append("range of " + k)
        elif np.any(v != np.floor(v)): bad.append("whole numbers in " + k)
    return bad
def reference(cov, tst, pr, th):
    U = cov.astype(np.float32).astype(np.int64).reshape(N, 8, 16, W); T = tst.astype(np.int64).reshape(N, 8, 16, C)
    price = pr.astype(np.float32).astype(np.int64).reshape(N, 8, 16, C); lim = th.astype(np.int64).reshape(N, 8, 1)
    lane = np.arange(16).reshape(1, 16, 1); last = np.zeros(N, np.int64)
    for t in range(RO):
        rho = (5 * t) & 15; now = np.zeros(N, np.int64)
        for r in range(N):
            s = (r + t) % N
            x = T[r]; y = np.roll(x, -(1 + t), axis=1)
            live = (x != 256) & (y != 256)
            code = ((((2 * x + 1) * (2 * y + 1)) >> 4) + 613 * lane + 77 * t) & (W - 1)
            got = np.take_along_axis(U[s], code.reshape(8, 1, 16 * C), 2).reshape(8, 16, 16, C)
            gain = np.add.reduce(np.where(live[:, None], np.maximum(got - price[s][:, :, None, :], 0), 0), axis=2)
            lev = np.argmax(gain, axis=1); best = np.max(gain, axis=1)
            useful = best >= lim[s] + (last[s] & 255); now[s] = np.sum(~useful)
            some = np.any(live, axis=1)
            vote = np.argmax(np.where(live, np.add.reduce(got, axis=1), -1), axis=1)
            taken = np.take_along_axis(code, vote[:, None, :], 1)[:, 0] >> SH
            most = np.argmax(np.where(live, np.take_along_axis(got, lev[:, None, None, :], 1)[:, 0], -1), axis=1)
            credit = np.take_along_axis(code, most[:, None, :], 1)[:, 0]
            none = x == 256; first = np.argmax(none, axis=1)
            new = np.array(x)
            g, c = np.nonzero(~useful & some & np.any(none, axis=1))
            new[g, first[g, c], c] = taken[g, c]
            new[:, rho] = np.where(useful, 16 * lev + (best & 15), 256)
            for g in range(8):
                c = np.nonzero(useful[g] & some[g])[0]
                col, at = np.unique(credit[g, c], return_index=True)
                U[s, g, lev[g, c[at]], col] = 0
            T[r] = new
        last = now
    left = np.add.reduce(U.reshape(N, 128, W // 16, 16), axis=3)
    return {"yt": T.reshape(N, 128, C).astype(np.float32), "yc": left.astype(np.float32)}

@@ -1,0 +1,566 @@
+from concourse.mybir import AluOpType as A, AxisListType, ActivationFunctionType as F
+
+N = 4
+RO = 6
+C = 256
+W = 4096
+UW = 4368
+VOID = 4096
+DUMMY = 4112
+FLAG = 2.0 ** 19
+BIG = 2.0 ** 25
+MAGIC = 1.5 * 2.0 ** 23
+CH = 4
+NT = C // CH
+RHO = [(5 * t) % 16 for t in range(RO)]
+
+SCRATCH = {}
+for _n, _w, _d in [
+    ("U", UW, "bfloat16"), ("PXP", W, "bfloat16"), ("R", W, "bfloat16"), ("M", W, "bfloat16"), ("PR", W, "bfloat16"),
+    ("P", C, "bfloat16"), ("TI", C, "int32"), ("NF", C, "bfloat16"), ("FN", C, "bfloat16"), ("QF", C, "float32"),
+    ("FI", C, "int32"), ("XI", C, "int32"), ("OFF", C, "uint16"), ("CM", C, "float32"), ("MG", C, "float32"), ("N4", C, "bfloat16"),
+    ("KT", C, "float32"), ("S1", C, "float32"), ("VT", C, "float32"), ("S2", C, "float32"), ("XT", C, "float32"), ("S3", C, "float32"),
+    ("WT", C, "float32"), ("W1", C, "bfloat16"), ("EA", C, "bfloat16"), ("EN", C, "bfloat16"), ("EB", C, "bfloat16"), ("VN", C, "bfloat16"),
+    ("VM", 2 * C, "bfloat16"), ("RV", C, "bfloat16"), ("JK", 4096, "bfloat16"), ("DL", C, "bfloat16"), ("UG", C, "bfloat16"),
+    ("TAU", 16, "int32"), ("LB", 16, "float32"), ("TV", 16, "float32"), ("KV", 16, "int32"), ("NB", 16, "int32"),
+    ("X1", 16, "int32"), ("X2", 16, "int32"), ("KI", 16, "int32"), ("D0", 16, "int32"), ("D1", 16, "int32"), ("D2", 16, "int32"),
+    ("YM", 16, "float32"), ("OL", 16, "uint16"), ("FL", 16, "float32"), ("FB", 64, "bfloat16"),
+    ("LIM", 16, "float32"), ("TH16", 16, "float32"), ("THI", 1, "int32"), ("THF", 1, "float32"), ("TH8", 16, "float32"), ("THQ", 16, "int32"),
+    ("MC", 1, "float32"), ("MA", 1, "float32"), ("MQ", 1, "float32"), ("MR", 1, "float32"), ("MF", 1, "float32"), ("MJK", 16, "float32"),
+    ("OUTT", C, "float32"), ("OUTC", C, "float32"), ("TS", C * RO, "bfloat16"),
+    ("cM", 128, "int32"), ("cD", 128, "int32"), ("cJ", 128, "int32"), ("cT", 128, "int32"), ("cG", 16, "int32"),
+    ("cP", 1, "int32"), ("cI", 8, "int32"), ("cF", 64, "float32"), ("cBM", 128, "bfloat16"), ("cMI", 128, "bfloat16"), ("cDD", 128, "bfloat16"),
+    ("cA", 128, "bfloat16"), ("cB", 128, "bfloat16"), ("mI", 128, "bfloat16"), ("mI16", 128, "bfloat16"), ("mP256", 128, "bfloat16"), ("mIF", 128, "float32"),
+    ("mPT", 128 * RO, "bfloat16"), ("mQT", 128 * RO, "bfloat16"), ("mKC", 128 * RO, "bfloat16"), ("iKC", 128 * RO, "int32"), ("jKC", 128 * RO, "int32"),
+    ("mE", 2048, "bfloat16"), ("mEX", 2048, "bfloat16"), ("mEL", 2048, "bfloat16"), ("mCH", 128, "bfloat16"), ("mCV", 128, "bfloat16"), ("mCX", 128, "bfloat16"),
+    ("mF0", 128, "bfloat16"), ("mFN", 128 * RO, "bfloat16"), ("mBR", 128 * RO, "bfloat16"), ("mNR", 128 * RO, "bfloat16"), ("mB0", 128, "bfloat16"), ("mON", C, "bfloat16"),
+    ("mXX", 128, "bfloat16"), ("mZ", 128, "bfloat16"), ("mLM", 512, "bfloat16"), ("mTH", 128, "float32"),
+    ("cMASK", C, "float32"), ("cNEG", C, "float32"), ("cBL", 16, "uint16"), ("cDUM", 16, "float32"),
+]:
+    SCRATCH[_n] = ("sbuf", [128, _w], _d)
+for _t in range(RO + 1):
+    SCRATCH["TB%d" % _t] = ("sbuf", [128, C], "bfloat16")
+for _b in range(8):
+    SCRATCH["bk%d" % _b] = ("psum", [128, 512], "float32")
+SEMAPHORES = ["v", "s", "p", "g", "snd"] + ["arr%d" % t for t in range(1, RO + 1)] + ["dma%d" % k for k in range(6)]
+AND, SHR = A.bitwise_and, A.arith_shift_right
+
+
+def rank_program(g, core, T, topo):
+    rank = T.rank_of(core)
+    if rank is None:
+        return
+    queue = {"v": g.vector, "s": g.scalar, "p": g.tensor, "g": g, "y": g.sync}
+    count = {}
+    known = {q: {} for q in queue}
+    done = {}
+    last = {}
+
+    def need(q, sem, val):
+        if known[q].get(sem, 0) >= val:
+            return
+        queue[q].wait_ge(T.sem[sem], val)
+        known[q][sem] = val
+        for k, x in done.get((sem, val), {}).items():
+            if known[q].get(k, 0) < x:
+                known[q][k] = x
+
+    def spans(views):
+        return [(x, 0, 1 << 20) if isinstance(x, str) else x for x in views]
+
+    def order(q, reads, writes):
+        todo = {}
+        reads, writes = spans(reads), spans(writes)
+        for views, wr in ((reads, False), (writes, True)):
+            for b, lo, hi in views:
+                for l2, h2, w2, q2, s2, v2 in last.get(b, []):
+                    if b.startswith("bk"):
+                        hit = q2 != q or (w2 and q != "p")
+                    else:
+                        hit = (wr or w2) and l2 < hi and lo < h2
+                    if hit and todo.get(s2, 0) < v2:
+                        todo[s2] = v2
+        for s2, v2 in sorted(todo.items(), key=lambda kv: -sum(done.get(kv, {}).values())):
+            need(q, s2, v2)
+        return reads, writes
+
+    def note(q, reads, writes, sem, val):
+        for views, wr in ((reads, False), (writes, True)):
+            for b, lo, hi in views:
+                keep = []
+                for e in last.get(b, []):
+                    if b.startswith("bk"):
+                        if e[3] != q or wr or not e[2]:
+                            continue
+                    elif wr and lo <= e[0] and e[1] <= hi:
+                        continue
+                    elif not wr and not e[2] and e[3] == q and lo <= e[0] and e[1] <= hi:
+                        continue
+                    keep.append(e)
+                keep.append((lo, hi, wr, q, sem, val))
+                last[b] = keep
+        know = dict(known[q])
+        know[sem] = val
+        done[(sem, val)] = know
+
+    def run(q, call, reads, writes):
+        reads, writes = order(q, reads, writes)
+        call(queue[q]).then_inc(T.sem[q], 1)
+        count[q] = count.get(q, 0) + 1
+        note(q, reads, writes, q, count[q])
+
+    def dma(q, k, out, in_, reads, writes):
+        sem = "dma%d" % k
+        reads, writes = order(q, reads, writes)
+        queue[q].dma_start(out, in_).then_inc(T.sem[sem], 16)
+        note(q, reads, writes, sem, 16)
+
+    def V(name, out, wr, rd, *a, **k):
+        run("v", lambda e: {"tt": e.tensor_tensor, "ts": e.tensor_scalar, "cp": e.tensor_copy, "tr": e.transpose, "sc": e.tensor_tensor_scan,
+                            "rd": e.tensor_reduce, "ms": e.memset}[name](out, *a, **k), rd, wr)
+
+    def S(out, in_, wr, rd, func=F.Identity, **k):
+        run("s", lambda e: e.activation(out, in_, func, **k), rd, wr)
+
+    def MM(out, lhsT, rhs, start, stop, bank, rd):
+        run("p", lambda e: e.matmul(out, lhsT, rhs, start, stop), rd, [bank])
+
+    def ts(out, wr, in0, rd, s1, s2, op0, op1=None):
+        if op1 is None:
+            V("ts", out, wr, rd, in0, s1, None, op0)
+        else:
+            V("ts", out, wr, rd, in0, s1, s2, op0, op1)
+
+    def tt(out, wr, a, b, rd, op):
+        V("tt", out, wr, rd, a, b, op)
+
+    def iota(out, wr, pattern, base, cm):
+        run("g", lambda e: e.iota(out, pattern, base, cm), [], [wr])
+
+    def fill(name, c0, pattern, base, cm, value, src=None, s0=0):
+        n = 1
+        for p in pattern:
+            n *= p[1]
+        if src is None:
+            src, s0 = name, c0
+        run("g", lambda e: e.affine_select(T[name][:, c0:c0 + n], T[src][:, s0:s0 + n], pattern, A.not_equal, value, base, cm),
+            [(src, s0, s0 + n)], [(name, c0, c0 + n)])
+
+    def cell(name, c0, row, column, value, src=None, s0=0):
+        fill(name, c0, [[-16, 8], [1000, 16]], -row - 1000 * column, 1, value, src, s0)
+
+    def col(k):
+        return T.cF[:, k:k + 1]
+
+    def fcol(k, src, s1, s2, op0, op1=None):
+        ts(col(k), [("cF", k, k + 1)], col(src), [("cF", src, src + 1)], s1, s2, op0, op1)
+
+    def icol(k, s1, s2, op0, op1=None):
+        ts(T.cI[:, k:k + 1], [("cI", k, k + 1)], T.cP[:], ["cP"], s1, s2, op0, op1)
+
+    EAS = ["EA%d" % r for r in range(6)]
+    E16 = lambda r: slice(r, C, 16)
+    blk = lambda name, k: (T[name][:, 128 * k:128 * k + 128], (name, 128 * k, 128 * k + 128))
+
+    dma("y", 0, T.TI[:], T.tst[:], [], ["TI"])
+    dma("s", 1, T.P[:], T.pr[:], [], ["P"])
+    dma("y", 3, T.U[:, 0:W], T.cov[:], [], [("U", 0, W)])
+    dma("s", 2, T.THI[0:8, :], T.th[:], [], ["THI"])
+
+    iota(T.cD[:], "cD", [[1, 128]], 256, -1)
+    iota(T.cM[:], "cM", [[1, 128]], 0, 0)
+    iota(T.cP[:], "cP", [[0, 1]], 0, 1)
+    V("ms", T.mON[:], ["mON"], [], 1.0)
+    for k, x in ((60, -511.0 * FLAG), (61, MAGIC), (62, -MAGIC), (63, -127.5), (59, BIG)):
+        V("ms", T.cF[:, k:k + 1], [("cF", k, k + 1)], [], x)
+
+    def icodes(t):
+        iota(blk("iKC", t)[0], blk("iKC", t)[1], [[0, 8], [613, 16]], 77 * t, 0)
+    icodes(0)
+    iota(T.cG[:], "cG", [[1, 16]], 0, 0)
+    icol(0, 4, None, SHR)
+    icol(1, 15, None, AND)
+    icol(2, 4, 1, SHR, AND)
+    icol(3, 1, None, AND)
+    icol(4, 31, 1, AND, SHR)
+    icol(5, 1, None, SHR)
+    icol(6, 5, None, SHR)
+    icol(7, 31, None, AND)
+    V("cp", T.cF[:, 0:8], [("cF", 0, 8)], ["cI"], T.cI[:])
+    ts(T.cJ[:], ["cJ"], T.cM[:], ["cM"], 4, None, SHR)
+    ts(T.cT[:], ["cT"], T.cD[:], ["cD"], 15, None, AND)
+    ts(T.cBM[:], ["cBM"], T.cJ[:], ["cJ", ("cF", 0, 1)], col(0), None, A.is_equal)
+    ts(T.cB[:], ["cB"], T.cT[:], ["cT"], 1.0, None, A.mult)
+    ts(T.cA[:], ["cA"], T.cBM[:], ["cBM"], -100.0, 100.0, A.mult, A.add)
+    tt(T.cDD[:], ["cDD"], T.cB[:], T.cA[:], ["cA", "cB"], A.add)
+
+    def eqm(name, k, val, scale):
+        ts(blk(name, k)[0], [blk(name, k)[1]], T.cDD[:], ["cDD"], float(val), float(scale), A.is_equal, A.mult)
+    eqm("mI", 0, 0, 1)
+
+    def const_t(t):
+        eqm("mPT", t, (-(1 + t)) % 16, 1)
+        if t == 0:
+            tt(blk("mQT", t)[0], [blk("mQT", t)[1]], blk("mPT", t)[0], T.mI[:], [blk("mPT", t)[1], "mI"], A.add)
+        x = slice(128 * t, 128 * t + 128)
+        part = ((0, "KCa%d" % t, 4080, 0.0), (64, "KCb%d" % t, 15, 1.0 / 64))
+        for p0, nm, bits, add in part:
+            ts(T.jKC[p0:p0 + 64, x], ["j" + nm], T.iKC[p0:p0 + 64, x], [blk("iKC", t)[1]], bits, None, AND)
+        for p0, nm, bits, add in part:
+            ts(T.mKC[p0:p0 + 64, x], [nm], T.jKC[p0:p0 + 64, x], ["j" + nm], 0.25, add, A.mult, A.add)
+
+    def const_g(t):
+        rho = RHO[t]
+        if t:
+            fill("mQT", 128 * t, [[-1, 128]], 0, 1, 1.0, "mPT", 128 * t)
+        fill("mFN", 128 * t, [[0, 8], [1, 16]], -rho, 0, 0.0, "mF0", 0)
+        cell("mNR", 128 * t, rho, rho, 0.0, "mI", 0)
+        for k, (r, x) in enumerate(((1, -32.0), (2, 2.0), (3, 32.0), (4, 480.0))):
+            if k == 0:
+                cell("mBR", 128 * t, r, rho, x, "mZ", 0)
+            else:
+                cell("mBR", 128 * t, r, rho, x)
+    const_t(0)
+    ts(T.TB0[:], ["TB0"], T.TI[:], ["TI"], 2.0, None, A.mult)
+
+    def codes(t):
+        TB = "TB%d" % t
+        tb = T[TB]
+        S(T.NF[:], tb[:], ["NF"], [TB, ("cF", 59, 64)], F.Relu, scale=FLAG, bias=col(60))
+        MM(T.bk0[:, 0:C], blk("mPT", t)[0], tb[:], True, True, "bk0", [blk("mPT", t)[1], TB])
+        MM(T.bk1[:, 0:C], blk("mKC", t)[0], T.mON[:], True, False, "bk1", ["KCa%d" % t, "KCb%d" % t, "mON"])
+        MM(T.bk1[:, 0:C], blk("mQT", t)[0], tb[:], False, False, "bk1", [blk("mQT", t)[1], TB])
+        MM(T.bk1[:, 0:C], blk("mQT", t)[0], T.NF[:], False, True, "bk1", [blk("mQT", t)[1], "NF"])
+
+    def codev(t, k):
+        if k == 0:
+            tt(T.QF[:], ["QF"], T["TB%d" % t][:], T.bk0[:, 0:C], ["TB%d" % t, "bk0"], A.mult)
+        elif k == 1:
+            tt(T.FI[:], ["FI"], T.QF[:], T.bk1[:, 0:C], ["QF", "bk1"], A.add)
+        elif k == 2:
+            ts(T.XI[:], ["XI"], T.FI[:], ["FI"], 4, 0x7FFF8FFF, SHR, AND)
+        elif k == 3:
+            ts(T.OFF[:], ["OFF"], T.XI[:], ["XI"], float(VOID), None, A.min)
+        else:
+            ts(T.CM[:], ["CM"], T.XI[:], ["XI"], float(VOID - 1), -7.5, A.min, A.add)
+
+    def codes2(t):
+        S(T.MG[:], T.CM[:], ["MG"], ["CM", ("cF", 59, 64)], scale=1.0 / 16, bias=col(61))
+        S(T.N4[:], T.MG[:], ["N4"], ["MG", ("cF", 59, 64)], bias=col(62))
+        MM(T.bk6[:, 0:C], blk("mFN", t)[0], T.NF[:], True, True, "bk6", [blk("mFN", t)[1], "NF"])
+        S(T.FN[:], T.bk6[:, 0:C], ["FN"], ["bk6"], F.Relu, scale=1.0 / FLAG)
+
+    codes(0)
+    V("ms", T.U[:, W:UW], [("U", W, UW)], [], -1.0)
+    V("ms", T.cMASK[:], ["cMASK"], [], 1.0)
+    codev(0, 0)
+    V("ms", T.cNEG[:], ["cNEG"], [], 0.0)
+    codev(0, 1)
+    V("ms", T.cMASK[:, E16(0)], ["cMASK"], [], 0.0)
+    V("ms", T.cNEG[:, E16(0)], ["cNEG"], [], -2.0 ** 26)
+    V("ms", T.EA[:], EAS, [], 0.0)
+    codev(0, 2)
+    V("ms", T.EB[:], ["EB"], [], 1.0)
+    V("ms", T.EA[:, E16(4)], ["EA4"], [], 1.0)
+    V("ms", T.mZ[:], ["mZ"], [], 0.0)
+    V("ms", T.mXX[:], ["mXX"], [], 0.0)
+    codev(0, 3)
+    codev(0, 4)
+    allpx = ["PXP%d" % i for i in range(16)]
+    for i in range(16):
+        if i < 11:
+            S(T.PXP[:, i:W:16], T.P[:], [allpx[i]], ["P"], F.Copy)
+        else:
+            V("cp", T.PXP[:, i:W:16], [allpx[i]], ["P"], T.P[:])
+
+    S(T.mI16[:], T.mI[:], ["mI16"], ["mI"], F.Copy, scale=16.0)
+    S(T.mP256[:], T.mI[:], ["mP256"], ["mI"], F.Copy, scale=-256.0)
+    ts(T.cJ[:], ["cJ"], T.cM[:], ["cM"], 15, None, AND)
+    ts(T.mCH[:], ["mCH"], T.cJ[:], ["cJ"], -1.0 / 128, 15.0 / 128, A.mult, A.add)
+    ts(T.mCV[:], ["mCV"], T.cJ[:], ["cJ"], -2.0, 30.0, A.mult, A.add)
+    S(T.mIF[:], T.mI[:], ["mIF"], ["mI"], F.Copy, scale=1.0 / 16)
+
+    def constants_0():
+        ts(T.cB[:], ["cB"], T.cJ[:], ["cJ"], 1.0, None, A.mult)
+        ts(T.cT[:], ["cT"], T.cD[:], ["cD"], 256.0, None, A.is_gt)
+        tt(T.cMI[:], ["cMI"], T.cB[:], T.cA[:], ["cB", "cA"], A.add)
+        tt(T.cB[:], ["cB"], T.cT[:], T.cBM[:], ["cT", "cBM"], A.mult)
+        for i in range(16):
+            ts(blk("mE", i)[0], [blk("mE", i)[1]], T.cMI[:], ["cMI"], float(i), 4096.0, A.is_equal, A.mult)
+        tt(T.mF0[:], ["mF0"], T.mI[:], T.cB[:], ["cB", "mI"], A.subtract)
+        const_g(0)
+        fill("mB0", 0, [[-16, 8], [0, 16]], 0, 1, 2.0, "mZ", 0)
+        fill("mB0", 0, [[-16, 8], [0, 16]], -5, 1, -512.0)
+        for r, m, x in [(k, k, 512.0) for k in range(3)] + [(3 + k, 8 + k, -256.0) for k in range(3)] + [(8 + k, 3 + k, -256.0) for k in range(3)] + \
+                [(6, 11, -1.0), (11, 6, 1.0), (7, 12, -16384.0)]:
+            cell("mXX", 0, r, m, x)
+
+    def constants_a():
+        V("cp", T.cBL[:], ["cBL"], ["cG"], T.cG[:])
+        V("cp", T.THF[0:8, :], ["THF"], ["THI"], T.THI[0:8, :])
+        ts(T.THQ[0:8, :], ["THQ"], T.cG[0:8, :], ["cG"], 1, None, AND)
+        ts(T.cT[:], ["cT"], T.cM[:], ["cM"], 5, None, SHR)
+        ts(T.TH8[0:8, :], ["TH8"], T.THQ[0:8, :], ["THQ", ("cF", 0, 8), "THF"], T.cF[0:8, 3:4], T.THF[0:8, :], A.is_equal, A.mult)
+        ts(T.mTH[0:8, :], ["mTH"], T.cT[0:8, :], ["cT", ("cF", 0, 8)], T.cF[0:8, 5:6], 16.0, A.is_equal, A.mult)
+        MM(T.bk6[:, 0:16], T.mTH[0:8, :], T.TH8[0:8, :], True, True, "bk6", ["mTH", "TH8"])
+        V("cp", T.TH16[:], ["TH16"], ["bk6"], T.bk6[:, 0:16])
+        V("cp", T.LIM[:], ["LIM"], ["bk6"], T.bk6[:, 0:16])
+        ts(T.mCX[0:64, :], ["mCX0"], T.mCV[0:64, :], ["mCV"], 2.0, None, A.mult)
+        V("ms", T.mCX[64:128, :], ["mCX1"], [], 15.0 / 2048)
+
+    def constants_b():
+        fcol(20, 1, 0.0, 1.0 / 4096, A.is_equal, A.mult)
+        for r, x in ((1, 16.0), (2, 256.0), (7, 8192.0)):
+            fcol(21 + r, 1, float(r), x / 4096, A.is_equal, A.mult)
+        for r in (1, 2, 7):
+            tt(col(20), [("cF", 20, 21)], col(20), col(21 + r), [("cF", 20, 29)], A.add)
+
+    def constants_c():
+        ts(T.X1[:], ["X1"], T.cG[:], ["cG"], 1, None, SHR)
+        fcol(30, 2, 0.0, None, A.is_equal)
+        ts(T.EB[:, E16(6)], ["EB"], T.X1[:], ["X1", ("cF", 7, 8)], 32.0, col(7), A.mult, A.add)
+        ts(T.cDUM[:], ["cDUM"], T.cG[:], ["cG", ("cF", 1, 2)], 16.0, col(1), A.mult, A.add)
+        fcol(33, 3, 16.0, col(4), A.mult, A.add)
+
+    def constants_d():
+        ts(T.cDUM[:], ["cDUM"], T.cDUM[:], ["cDUM"], float(DUMMY), None, A.add)
+        for a in range(1, 4):
+            fcol(33 + a, 33, 32.0 * a, None, A.add)
+        for s in range(4):
+            fcol(40 + s, 6, float(s), None, A.is_equal)
+        for a in range(4):
+            ts(blk("mLM", a)[0], [blk("mLM", a)[1]], T.cM[:], ["cM", ("cF", 33 + a, 34 + a)], col(33 + a), 8192.0, A.is_equal, A.mult)
+
+    def votes(k):
+        lo, hi = 1024 * k, 1024 * k + 1024
+        for i in range(16):
+            MM(T.bk2[:, NT * k:NT * (k + 1)], blk("mE", i)[0], T.R[:, lo + i:hi:16], False, False, "bk2", [blk("mE", i)[1], ("R", lo, hi)])
+
+    for t in range(RO):
+        first, more = t == 0, t < RO - 1
+        TB = "TB%d" % t
+        LBS = ["LB00", "LB10", "LB01", "LB11"]
+        l3 = T.EA[:, E16(3)]
+
+        def gather_v(c0, n):
+            lo, hi = 16 * c0, 16 * (c0 + n)
+            tt(T.M[:, lo:hi], [("M", lo, hi)], T.U[:].indirect(T.OFF[:, c0:c0 + n]), T.PXP[:, lo:hi], ["U", ("OFF", c0, c0 + n)] + allpx, A.max)
+
+        def gather_s(k):
+            lo, hi = 1024 * k, 1024 * k + 1024
+            S(T.R[:, lo:hi], T.U[:].indirect(T.OFF[:, NT * k:NT * k + NT]), [("R", lo, hi)], ["U", ("OFF", NT * k, NT * k + NT)], F.Copy)
+
+        def gains(k):
+            lo, hi, bank, c0 = 1024 * k, 1024 * k + 1024, ("bk0", "bk1")[k // 2], NT * (k % 2)
+            for i in range(16):
+                MM(T[bank][:, c0:c0 + NT], T.mI16[:], T.M[:, lo + i:hi:16], False, k % 2 == 1 and i == 15, bank, ["mI16", ("M", lo, hi)])
+
+        def level(h, step):
+            a, b, a8 = 128 * h, 128 * h + 128, 8 * h
+            kt, s1, tau, wt = ("KT", a, b), ("S1", a, b), ("TAU", a8, a8 + 8), ("WT", a, b)
+            gb, wb = ("bk0", "bk1")[h], ("bk3", "bk4")[h]
+            if step == 0:
+                V("tr", T.KT[:, a:b], [kt], [gb], T[gb][:, 0:128])
+            elif step == 1:
+                V("sc", T.S1[:, a:b], [s1], ["cMASK", kt], T.cMASK[:, 0:128], T.KT[:, a:b], 0.0, A.mult, A.max)
+            elif step == 2:
+                for gm in range(2):
+                    ts(T.LB[:, a8 + gm:a8 + 8:2], ["LB%d%d" % (gm, h)], T.S1[:, a + 15 + 16 * gm:b:32], [s1, "LIM"], T.LIM[:, gm:gm + 1], BIG, A.is_lt, A.mult)
+            elif step == 3:
+                tt(T.TAU[:, a8:a8 + 8], [tau], T.LB[:, a8:a8 + 8], T.S1[:, a + 15:b:16], ["LB0%d" % h, "LB1%d" % h, s1], A.max)
+            elif step == 4:
+                tt(T.WT[:, a:b], [wt], T.TAU[:, a8:a8 + 8].indirect(T.cBL[:, 0:8]), T.KT[:, a:b], [tau, "cBL", kt], A.is_le)
+            else:
+                V("tr", T[wb][:, 0:128], [wb], [wt], T.WT[:, a:b])
+
+        for h in range(2):
+            gb = ("bk0", "bk1")[h]
+            MM(T[gb][:, 0:128], T.mCH[:], T.mON[:, 0:128], True, False, gb, ["mCH", "mON"])
+            MM(T[gb][:, 0:128], T.mP256[:], T.P[:, 128 * h:128 * h + 128], False, False, gb, ["mP256", "P"])
+        MM(T.bk2[:, 0:C], T.mCV[:], T.mON[:], True, False, "bk2", ["mCV", "mON"])
+        for k in range(2):
+            gather_v(NT * k, NT)
+            gather_s(k)
+            if first and k == 0:
+                constants_a()
+                constants_0()
+            gains(k)
+        votes(0)
+        gather_v(128, 32)
+        gather_s(2)
+        level(0, 0)
+        gather_v(160, 32)
+        gains(2)
+        votes(1)
+        level(0, 1)
+        gather_s(3)
+        for k in range(4):
+            gather_v(192 + 16 * k, 16)
+            level(0, 2 + k)
+        gains(3)
+        votes(2)
+        if first:
+            codes2(0)
+        votes(3)
+        MM(T.bk2[:, 0:C], T.mI[:], T.N4[:], False, True, "bk2", ["mI", "N4"])
+        if first:
+            constants_b()
+
+        def pick(h, i):
+            pr, xb, wb = "PR%d_%d" % (h, i), ("bk5", "bk7")[h], ("bk3", "bk4")[h]
+            lo, hi = 2048 * h, 2048 * h + 2048
+            tt(T.PR[:, lo + i:hi:16], [pr], T.R[:, lo + i:hi:16], T[wb][:, 0:128], [("R", lo, hi), wb], A.mult)
+            MM(T[xb][:, 0:128], blk("mE", i)[0], T.PR[:, lo + i:hi:16], False, i == 15, xb, [blk("mE", i)[1], pr])
+
+        for h in range(2):
+            xb = ("bk5", "bk7")[h]
+            MM(T[xb][:, 0:128], T.mIF[:], T.CM[:, 128 * h:128 * h + 128], True, False, xb, ["mIF", "CM"])
+            MM(T[xb][:, 0:128], T.mCX[:], T.mON[:, 0:128], False, False, xb, ["mCX0", "mCX1", "mON"])
+        vote = {
+            9: lambda: ts(T.X1[:], ["X1"], T.TAU[:], ["TAU"], 15, None, AND),
+            10: lambda: V("tr", T.VT[:], ["VT"], ["bk2"], T.bk2[:, 0:C]),
+            12: lambda: V("sc", T.S2[:], ["S2"], ["cNEG", "VT"], T.cNEG[:], T.VT[:], 0.0, A.add, A.max),
+            13: lambda: ts(T.X2[:], ["X2"], T.TAU[:], ["TAU"], 4, 15, SHR, AND),
+            14: lambda: V("cp", T.KV[:], ["KV"], ["S2"], T.S2[:, 15:C:16]),
+            15: lambda: ts(T.NB[:], ["NB"], T.KV[:], ["KV"], 255, None, AND),
+        }
+        for i in range(16):
+            pick(0, i)
+            if i % 2 == 1 and i < 12:
+                level(1, i // 2)
+                if i // 2 == 2:
+                    S(T.TV[:], T.LB[:], ["TV"], LBS + [("cF", 59, 64)], scale=-1.0, bias=col(59))
+                    S(l3, T.LB[:], ["EA3"], LBS, F.Sign)
+            if i in vote:
+                vote[i]()
+        if more:
+            MM(T.bk6[:, 0:16], T.mON[:, 0:128], l3, True, True, "bk6", ["mON", "EA3"])
+            S(T.MJK[:], T.bk6[:, 0:16], ["MJK", "MC"], ["bk6"], scale=16.0, accum_out=T.MC[:])
+            S(T.MA[:], T.MC[:], ["MA"], ["MC", ("cF", 59, 64)], scale=1.0 / 16, bias=col(63))
+            S(T.MQ[:], T.MA[:], ["MQ"], ["MA", ("cF", 59, 64)], scale=1.0 / 256, bias=col(61))
+            S(T.MR[:], T.MQ[:], ["MR"], ["MQ", ("cF", 59, 64)], bias=col(62))
+            S(T.MF[:], T.MR[:], ["MF"], ["MR", "MC"], scale=-4096.0, bias=T.MC[:])
+
+        def claim(h, step):
+            x, s3, xb = ("XT", 128 * h, 128 * h + 128), ("S3", 128 * h, 128 * h + 128), ("bk5", "bk7")[h]
+            if step == 0:
+                V("tr", T.XT[:, x[1]:x[2]], [x], [xb], T[xb][:, 0:128])
+            else:
+                V("sc", T.S3[:, x[1]:x[2]], [s3], ["cNEG", x], T.cNEG[:, 0:128], T.XT[:, x[1]:x[2]], 0.0, A.add, A.max)
+        a, b = C * t, C * t + C
+
+        def spread():
+            V("tr", T.EN[:], ["EN"], EAS, T.EA[:])
+            MM(T.bk0[:, 0:C], T.mB0[:], T.EN[:], True, True, "bk0", ["mB0", "EN"])
+            MM(T.bk1[:, 0:C], blk("mNR", t)[0], T[TB][:], True, False, "bk1", [blk("mNR", t)[1], TB])
+            MM(T.bk1[:, 0:C], blk("mBR", t)[0], T.EN[:], False, True, "bk1", [blk("mBR", t)[1], "EN"])
+
+        def leave():
+            tt(T.TS[:, a:b], [("TS", a, b)], T.DL[:], T.bk1[:, 0:C], ["DL", "bk1"], A.add)
+            step = 1 if more else -(RO - 1)
+            dst, src = T.cores[(rank + step) % N], T.cores[(rank - step) % N]
+            rid, pid, _se = topo.addr(dst)
+            order("g", [("TS", a, b)], [])
+            g.remote_dma(T["TB%d" % (t + 1)][:], T.TS[:, a:b], T.sem["arr%d" % (t + 1)], T.sem["snd"], pid, rid, topo.mask(core, dst))
+            last["TB%d" % (t + 1)] = [(0, 1 << 20, True, "r", "arr%d" % (t + 1), len(topo.engines(src, core)))]
+            for u in range(1 if first else t + 2, min(t + 3, RO)):
+                icodes(u)
+        chain = [
+            lambda: tt(T.EA[:, E16(5)], ["EA5"], T.S2[:, 15:C:16], T.TV[:], ["S2", "TV"], A.is_ge),
+            lambda: V("cp", T.EA[:, E16(1)], ["EA1"], ["X1"], T.X1[:]),
+            lambda: V("cp", T.EA[:, E16(2)], ["EA2"], ["X2"], T.X2[:]),
+            lambda: tt(T.EA[:, E16(0)], ["EA0"], T.NB[:], T.EA[:, E16(5)], ["NB", "EA5"], A.mult),
+            None,
+            spread,
+            lambda: claim(0, 0),
+            None,
+            lambda: tt(T.DL[:], ["DL"], T.FN[:], T.bk0[:, 0:C], ["FN", "bk0"], A.mult),
+            lambda: claim(0, 1),
+            leave,
+        ]
+        for i in range(16):
+            pick(1, i)
+            if i < len(chain) and chain[i] is not None:
+                chain[i]()
+        for h, wb in enumerate(("bk3", "bk4")):
+            S(T.W1[:, 128 * h:128 * h + 128], T[wb][:, 0:128], [("W1", 128 * h, 128 * h + 128)], [wb], scale=-1.0, bias=1.0)
+        if more:
+            ts(T.LIM[:], ["LIM"], T.TH16[:], ["TH16", "MF"], T.MF[:], None, A.add)
+        if first:
+            S(T.mEL[:], T.mE[:], ["mEL"], ["mE", ("cF", 20, 21)], F.Copy, scale=col(20))
+            constants_c()
+
+        claim(1, 0)
+        claim(1, 1)
+        if more:
+            if first:
+                const_t(1)
+                const_g(1)
+            codes(t + 1)
+        ts(T.KI[:], ["KI"], T.S3[:, 15:C:16], ["S3"], 16.0, None, A.mult)
+        tt(T.EB[:, E16(7)], ["EBz"], T.S3[:, 15:C:16], T.LB[:], ["EB", "S3"] + LBS, A.is_lt)
+        for r in range(3):
+            ts(T["D%d" % r][:], ["D%d" % r], T.KI[:], ["KI"], 4 * r, 15, SHR, AND)
+        for r in range(3):
+            V("cp", T.EB[:, E16(r)], ["EBd%d" % r], ["EB", "D%d" % r], T["D%d" % r][:])
+        for r in range(3):
+            tt(T.EB[:, E16(3 + r)], ["EBs%d" % r], T["D%d" % r][:], T["D%d" % r][:], ["EB", "D%d" % r], A.mult)
+        V("tr", T.VN[:], ["VN"], ["EB", "EBz"] + ["EBd%d" % r for r in range(3)] + ["EBs%d" % r for r in range(3)], T.EB[:])
+        MM(T.bk2[:, 0:C], T.mXX[:], T.VN[:], True, True, "bk2", ["mXX", "VN"])
+        if more:
+            codev(t + 1, 0)
+        ts(T.VM[:, 0:2 * C:2], ["VM0"], T.VN[:], ["VN", ("cF", 30, 31)], col(30), None, A.mult)
+        ts(T.VM[:, 1:2 * C:2], ["VM1"], T.VN[:], ["VN", ("cF", 2, 3)], col(2), None, A.mult)
+        S(T.RV[:], T.bk2[:, 0:C], ["RV"], ["bk2"], F.Copy)
+        for k in range(16):
+            MM(T.bk6[:, 0:16], blk("mEL", k)[0], T.VN[:, k:C:16], k == 0, False, "bk6", ["mEL", "VN"])
+        if more:
+            codev(t + 1, 1)
+        if first:
+            constants_d()
+        if more:
+            codev(t + 1, 2)
+        banks = ["bk3", "bk4", "bk5", "bk7", "bk2"]
+        for j, (a4, pair) in enumerate(((0, (3, 2)), (0, (1, 0)), (1, (3, 2)), (3, (3, 2)), (2, (3, 2)), (1, (1, 0)), (2, (1, 0)), (3, (1, 0)))):
+            bank = banks[j % len(banks)]
+            rows = slice(32 * a4, 32 * a4 + 32)
+            part = []
+            for be in pair:
+                n = 64 * (be + 1)
+                c0 = 0 if be == pair[0] else 64 * (pair[0] + 1)
+                MM(T[bank][:, c0:c0 + n], T.VM[rows, 128 * be:128 * be + 128], T.RV[rows, 0:n], True, True, bank, ["VM0", "VM1", "RV"])
+                part.append((T[bank][:, c0:c0 + n], n, 4 * a4 + be))
+            for x, n, k in part:
+                if pair == (3, 2) and a4 < 3:
+                    S(T.JK[:, 256 * k:256 * k + n], x, ["JK%d" % k, ("FL", k, k + 1)], [bank], F.Relu, accum_out=T.FL[:, k:k + 1])
+                else:
+                    V("rd", T.FL[:, k:k + 1], [("FL", k, k + 1)], [bank], x, AxisListType.X, A.max)
+        for s in range(4):
+            if s < 2:
+                S(T.FB[:, s:64:4], T.FL[:], ["FB%d" % s], ["FL", ("cF", 40 + s, 41 + s)], F.Relu, scale=col(40 + s))
+            else:
+                ts(T.FB[:, s:64:4], ["FB%d" % s], T.FL[:], ["FL", ("cF", 40 + s, 41 + s)], 0.0, col(40 + s), A.is_gt, A.mult)
+        for a4 in range(4):
+            MM(T.bk6[:, 0:16], blk("mLM", a4)[0], T.FB[:, 16 * a4:16 * a4 + 16], False, a4 == 3, "bk6", ["mLM"] + ["FB%d" % s for s in range(4)])
+        if more:
+            codev(t + 1, 3)
+            codev(t + 1, 4)
+        tt(T.YM[:], ["YM"], T.cDUM[:], T.bk6[:, 0:16], ["cDUM", "bk6"], A.min)
+        V("cp", T.OL[:], ["OL"], ["YM"], T.YM[:])
+        S(T.UG[:], T.U[:].indirect(T.OL[:]), ["UG"], ["U", "OL"], F.Copy)
+        if more:
+            codes2(t + 1)
+        if t + 2 < RO:
+            const_t(t + 2)
+            const_g(t + 2)
+        tt(T.U[:].indirect(T.OL[:]), ["U"], T.UG[:], T.W1[:], ["UG", "W1", "OL"], A.mult)
+
+    S(T.OUTT[:], T["TB%d" % RO][:], ["OUTT"], ["TB%d" % RO], scale=0.5)
+    dma("s", 4, T.yt[:], T.OUTT[:], ["OUTT"], ["yt"])
+    for i in range(16):
+        MM(T.bk0[:, 0:C], T.mI[:], T.U[:, i:W:16], i == 0, i == 15, "bk0", ["mI", "U"])
+    V("cp", T.OUTC[:], ["OUTC"], ["bk0"], T.bk0[:, 0:C])
+    dma("y", 5, T.yc[:], T.OUTC[:], ["OUTC"], ["yc"])
+    need("y", "dma4", 16)
+    need("y", "dma5", 16)
+    g.wait_ge(T.sem["snd"], sum(len(topo.engines(core, T.cores[(rank + (1 if t < RO - 1 else 1 - RO)) % N])) for t in range(RO)))

@@ -3,47 +3,101 @@ from concourse.mybir import AluOpType as A, AxisListType, ActivationFunctionType
 N = 4
 RO = 6
 C = 256
+H = 128
 W = 4096
-UW = 4368
+UW = 5136
 VOID = 4096
-DUMMY = 4112
-FLAG = 2.0 ** 19
-BIG = 2.0 ** 25
-MAGIC = 1.5 * 2.0 ** 23
-CH = 4
-NT = C // CH
+SPARE = 4100
+NONE = 16384.0
+BIG = 2.0 ** 20
+KEEP = 2.0 ** 17
+RELU = 2
+PIECE = 32
+LEAD, SHORT = 4000.0, 3.0
 RHO = [(5 * t) % 16 for t in range(RO)]
+CYCLE, PE, GATHER, SCATTER, HOP, FAR, RATE = 0.83, 0.42, 1.3, 3.0, 240.0, 1500.0, 300.0
 
 SCRATCH = {}
 for _n, _w, _d in [
-    ("U", UW, "bfloat16"), ("PXP", W, "bfloat16"), ("R", W, "bfloat16"), ("M", W, "bfloat16"), ("PR", W, "bfloat16"),
-    ("P", C, "bfloat16"), ("TI", C, "int32"), ("NF", C, "bfloat16"), ("FN", C, "bfloat16"), ("QF", C, "float32"),
-    ("FI", C, "int32"), ("XI", C, "int32"), ("OFF", C, "uint16"), ("CM", C, "float32"), ("MG", C, "float32"), ("N4", C, "bfloat16"),
-    ("KT", C, "float32"), ("S1", C, "float32"), ("VT", C, "float32"), ("S2", C, "float32"), ("XT", C, "float32"), ("S3", C, "float32"),
-    ("WT", C, "float32"), ("W1", C, "bfloat16"), ("EA", C, "bfloat16"), ("EN", C, "bfloat16"), ("EB", C, "bfloat16"), ("VN", C, "bfloat16"),
-    ("VM", 2 * C, "bfloat16"), ("RV", C, "bfloat16"), ("JK", 4096, "bfloat16"), ("DL", C, "bfloat16"), ("UG", C, "bfloat16"),
-    ("TAU", 16, "int32"), ("LB", 16, "float32"), ("TV", 16, "float32"), ("KV", 16, "int32"), ("NB", 16, "int32"),
-    ("X1", 16, "int32"), ("X2", 16, "int32"), ("KI", 16, "int32"), ("D0", 16, "int32"), ("D1", 16, "int32"), ("D2", 16, "int32"),
-    ("YM", 16, "float32"), ("OL", 16, "uint16"), ("FL", 16, "float32"), ("FB", 64, "bfloat16"),
-    ("LIM", 16, "float32"), ("TH16", 16, "float32"), ("THI", 1, "int32"), ("THF", 1, "float32"), ("TH8", 16, "float32"), ("THQ", 16, "int32"),
-    ("MC", 1, "float32"), ("MA", 1, "float32"), ("MQ", 1, "float32"), ("MR", 1, "float32"), ("MF", 1, "float32"), ("MJK", 16, "float32"),
-    ("OUTT", C, "float32"), ("OUTC", C, "float32"), ("TS", C * RO, "bfloat16"),
-    ("cM", 128, "int32"), ("cD", 128, "int32"), ("cJ", 128, "int32"), ("cT", 128, "int32"), ("cG", 16, "int32"),
-    ("cP", 1, "int32"), ("cI", 8, "int32"), ("cF", 64, "float32"), ("cBM", 128, "bfloat16"), ("cMI", 128, "bfloat16"), ("cDD", 128, "bfloat16"),
-    ("cA", 128, "bfloat16"), ("cB", 128, "bfloat16"), ("mI", 128, "bfloat16"), ("mI16", 128, "bfloat16"), ("mP256", 128, "bfloat16"), ("mIF", 128, "float32"),
-    ("mPT", 128 * RO, "bfloat16"), ("mQT", 128 * RO, "bfloat16"), ("mKC", 128 * RO, "bfloat16"), ("iKC", 128 * RO, "int32"), ("jKC", 128 * RO, "int32"),
-    ("mE", 2048, "bfloat16"), ("mEX", 2048, "bfloat16"), ("mEL", 2048, "bfloat16"), ("mCH", 128, "bfloat16"), ("mCV", 128, "bfloat16"), ("mCX", 128, "bfloat16"),
-    ("mF0", 128, "bfloat16"), ("mFN", 128 * RO, "bfloat16"), ("mBR", 128 * RO, "bfloat16"), ("mNR", 128 * RO, "bfloat16"), ("mB0", 128, "bfloat16"), ("mON", C, "bfloat16"),
-    ("mXX", 128, "bfloat16"), ("mZ", 128, "bfloat16"), ("mLM", 512, "bfloat16"), ("mTH", 128, "float32"),
-    ("cMASK", C, "float32"), ("cNEG", C, "float32"), ("cBL", 16, "uint16"), ("cDUM", 16, "float32"),
+    ("U0", UW, "bfloat16"), ("U1", UW, "bfloat16"), ("R", W, "bfloat16"), ("M", W, "bfloat16"), ("KP", W, "float16"),
+    ("P", 2 * C, "bfloat16"), ("P1", C, "bfloat16"), ("TI", 2 * C, "int32"), ("QF", C, "float32"), ("FI", C, "int32"), ("XI", C, "int32"),
+    ("OFF", C, "uint16"), ("CM", C, "float16"), ("ZN", C, "float16"), ("TR", C, "float16"), ("WP", C, "float16"),
+    ("S1", C, "float32"), ("S2", C, "float32"), ("S3", C, "float32"), ("ST", C, "bfloat16"), ("VB", C, "float16"),
+    ("W1", 2 * C, "bfloat16"), ("UG", 2 * C, "bfloat16"), ("FE", C, "bfloat16"),
+    ("FT", 768, "float16"), ("FA", 800, "float16"),
+    ("KV", 16, "int32"), ("AV", 16, "int32"), ("KS", 16, "int32"), ("AG", 16, "int32"), ("H2", 16, "int32"), ("G2", 16, "int32"), ("GM", 16, "int32"),
+    ("ZZ", 16, "float32"), ("PX", W, "bfloat16"), ("P0", C, "bfloat16"), ("PU", 16, "float32"), ("PN", 16, "bfloat16"), ("PV", 16, "float32"), ("P2", 16, "bfloat16"),
+    ("WN", 32, "int32"), ("X", 16, "float32"), ("PR", 32, "float32"), ("RD", 16, "float32"),
+    ("OL0", 32, "uint16"), ("OL", 32, "uint16"),
+    ("LR", C, "float16"), ("L2", 16, "float32"), ("THR", C, "float32"), ("TH2", 16, "float32"), ("THI", 1, "int32"), ("THF", 1, "float32"), ("TH8", C, "float32"),
+    ("MC", 4, "float32"), ("MW", 1, "bfloat16"), ("MJ", 16, "float32"),
+    ("OUTT", C, "float32"), ("OUTC", C, "float32"), ("TS", C * RO, "float16"),
+    ("cM", 128, "int32"), ("cD", 128, "int32"), ("cJ", 128, "int32"), ("cH", 128, "int32"), ("cT", 128, "int32"), ("cG", 128, "int32"), ("cP", 1, "int32"), ("cI", 8, "int32"),
+    ("cF", 64, "float32"), ("cV", 16, "int32"), ("cW", 16, "int32"), ("cA", 128, "bfloat16"), ("cB", 128, "bfloat16"), ("cC", 128, "bfloat16"), ("cE", 128, "bfloat16"),
+    ("cDD", 128, "bfloat16"), ("cBM", 128, "bfloat16"),
+    ("mI", 128, "bfloat16"), ("mIG", 128, "bfloat16"), ("mI16", 128, "bfloat16"), ("mN16", 128, "bfloat16"), ("mN1", 128, "bfloat16"), ("mP", 128, "bfloat16"),
+    ("mI32", 128, "bfloat16"), ("mH", 128, "bfloat16"),
+    ("mPT", 128 * RO, "bfloat16"), ("mFN", 128 * RO, "bfloat16"), ("mF0", 128, "bfloat16"), ("mCR", 128 * RO, "float16"), ("mC0", 128, "float16"),
+    ("mD", 128, "bfloat16"), ("mV", 8, "bfloat16"), ("mL", 128, "float16"), ("mON", C, "bfloat16"), ("mOF", 128, "float32"),
+    ("mRF", 16, "float16"), ("mTR", 64, "bfloat16"), ("mS", 2048, "bfloat16"), ("mW", 128, "bfloat16"), ("cX", 128, "bfloat16"), ("cY", 128, "bfloat16"), ("cZ", 128, "bfloat16"),
+    ("cAG", 16 * PIECE, "bfloat16"), ("c32", 128, "bfloat16"), ("c1", 128, "bfloat16"), ("cPA", 128, "bfloat16"), ("cK", 128, "bfloat16"),
+    ("cBL", 128, "uint16"), ("cBR", 8 * RO, "uint16"),
 ]:
     SCRATCH[_n] = ("sbuf", [128, _w], _d)
 for _t in range(RO + 1):
-    SCRATCH["TB%d" % _t] = ("sbuf", [128, C], "bfloat16")
+    SCRATCH["TB%d" % _t] = ("sbuf", [128, C], "float16")
 for _b in range(8):
     SCRATCH["bk%d" % _b] = ("psum", [128, 512], "float32")
-SEMAPHORES = ["v", "s", "p", "g", "snd"] + ["arr%d" % t for t in range(1, RO + 1)] + ["dma%d" % k for k in range(6)]
+DMAS = 17
+SEMAPHORES = ["v", "s", "p", "g", "snd"] + ["arr%d_%d" % (t, e) for t in range(1, RO + 1) for e in range(2)] + ["dma%d" % k for k in range(DMAS)]
 AND, SHR = A.bitwise_and, A.arith_shift_right
+ALL, LOW, HIGH = slice(0, 128), slice(0, 64), slice(64, 128)
+HALF = (LOW, HIGH)
+
+
+def arrange(calls):
+    touch, before = {}, []
+    for k, c in enumerate(calls):
+        pre = {}
+        for views, wr in ((c["reads"], False), (c["writes"], True)):
+            for b, lo, hi in views:
+                keep = []
+                for e in touch.get(b, []):
+                    j, l2, h2, w2 = e
+                    if b.startswith("bk"):
+                        hit = wr or w2 or calls[j]["q"] != c["q"]
+                        gone = wr
+                    else:
+                        hit = (wr or w2) and l2 < hi and lo < h2
+                        gone = wr and lo <= l2 and h2 <= hi
+                    if hit and j != k:
+                        free = b.startswith("bk") and c["q"] == "p" and calls[j]["q"] == "p"
+                        pre[j] = max(pre.get(j, 0.0), 0.0 if free else HOP + calls[j]["late"])
+                    if not gone:
+                        keep.append(e)
+                keep.append((k, lo, hi, wr))
+                touch[b] = keep
+        before.append(pre)
+    way = [c["time"] + c["late"] + (LEAD if c["writes"][0][0] in ("yc0", "yt0") else 0.0) for c in calls]
+    after, left = [[] for c in calls], [len(pre) for pre in before]
+    for k in range(len(calls) - 1, -1, -1):
+        for j, gap in before[k].items():
+            way[j] = max(way[j], calls[j]["time"] + gap + way[k])
+            after[j].append(k)
+    ready, free, start = {q: {} for q in "vspgy"}, {q: 0.0 for q in "vspgy"}, {}
+    for k, c in enumerate(calls):
+        if not left[k]:
+            ready[c["q"]][k] = 0.0
+    while len(start) < len(calls):
+        t, q = min((max(free[q], min(r.values())), q) for q, r in ready.items() if r)
+        k = min((k for k, x in ready[q].items() if x <= t), key=lambda k: (SHORT * calls[k]["time"] - way[k], k))
+        del ready[q][k]
+        start[k], free[q] = t, t + calls[k]["time"]
+        for m in after[k]:
+            left[m] -= 1
+            if not left[m]:
+                ready[calls[m]["q"]][m] = max(start[j] + calls[j]["time"] + gap for j, gap in before[m].items())
+    return sorted(range(len(calls)), key=lambda k: (start[k], k))
 
 
 def rank_program(g, core, T, topo):
@@ -51,6 +105,362 @@ def rank_program(g, core, T, topo):
     if rank is None:
         return
     queue = {"v": g.vector, "s": g.scalar, "p": g.tensor, "g": g, "y": g.sync}
+    calls = []
+
+    def run(q, call, reads, writes, time, late=0.0, signal=None):
+        spans = lambda views: [(x, 0, 1 << 20) if isinstance(x, str) else x for x in views]
+        calls.append({"q": q, "call": call, "reads": spans(reads), "writes": spans(writes), "time": time, "late": late, "signal": signal})
+
+    dmas = []
+
+    def dma(q, out, in_, reads, writes, size):
+        sem = "dma%d" % len(dmas)
+        dmas.append(size)
+        run(q, lambda e: e.dma_start(out, in_).then_inc(T.sem[sem], 16), reads, writes, 60.0, FAR + sum(dmas[-13:]) / RATE, (sem, 16))
+        return sem
+
+    def v(name, lo=0, hi=None, step=1, tag=None, rows=ALL):
+        if hi is None:
+            hi = T[name].shape[1]
+        n = len(range(lo, hi, step))
+        if name.startswith("bk"):
+            return T[name][rows, lo:hi:step], [name], n, 0, False
+        return T[name][rows, lo:hi:step], [(name if tag is None else name + "." + str(tag), lo, hi)], n, 2 if "16" in SCRATCH[name][2] else 4, False
+
+    def ind(win, off):
+        return win[0].indirect(off[0]), win[1] + off[1], 16 * off[2], win[3], True
+
+    def also(view, *names):
+        return (view[0], view[1] + list(names)) + view[2:]
+
+    def sc(x):
+        return x if isinstance(x, tuple) else (x, [])
+
+    def vtime(out, ins, rate=None):
+        if out[4]:
+            return 50 + out[2] * SCATTER * CYCLE
+        if ins[0][4]:
+            return 50 + out[2] * GATHER * CYCLE
+        if rate is None:
+            rate = 0.5 if all(x[3] == 2 for x in [out] + ins) else 1.0
+        return max(64, ins[0][2] * rate) * CYCLE
+
+    def ts(out, in0, s1, s2, op0, op1=None):
+        s1, s2 = sc(s1), sc(s2)
+        more = () if op1 is None else (op1,)
+        run("v", lambda e: e.tensor_scalar(out[0], in0[0], s1[0], s2[0], op0, *more), in0[1] + s1[1] + s2[1], out[1], vtime(out, [in0]))
+
+    def tt(out, a, b, op):
+        run("v", lambda e: e.tensor_tensor(out[0], a[0], b[0], op), a[1] + b[1], out[1], vtime(out, [a, b], 2.0 if a[3] and b[3] else 1.0))
+
+    def cp(out, a):
+        run("v", lambda e: e.tensor_copy(out[0], a[0]), a[1], out[1], vtime(out, [a]))
+
+    def ms(out, x):
+        run("v", lambda e: e.memset(out[0], x), [], out[1], vtime(out, [out]))
+
+    def scan(out, d0, d1, op0, op1):
+        run("v", lambda e: e.tensor_tensor_scan(out[0], d0[0], d1[0], 0.0, op0, op1), d0[1] + d1[1], out[1], vtime(out, [d0, d1]))
+
+    def least(out, a):
+        run("v", lambda e: e.tensor_reduce(out[0], a[0], AxisListType.X, A.min, apply_absolute_value=True), a[1], out[1], vtime(out, [a], 1.0))
+
+    def S(out, in_, func=F.Identity, scale=1.0, bias=0.0, accum=None):
+        scale, bias = sc(scale), sc(bias)
+        k = {} if accum is None else {"accum_out": accum[0]}
+        run("s", lambda e: e.activation(out[0], in_[0], func, bias=bias[0], scale=scale[0], **k),
+            in_[1] + scale[1] + bias[1], out[1] + ([] if accum is None else accum[1]), 65 + out[2] * GATHER * CYCLE if in_[4] else max(64, out[2]) * CYCLE)
+
+    def MM(out, lhsT, rhs, start=True, stop=True):
+        run("p", lambda e: e.matmul(out[0], lhsT[0], rhs[0], start, stop), lhsT[1] + rhs[1], out[1], max(64, rhs[2]) * PE * (4 if rhs[3] == 4 else 1))
+
+    def iota(out, pattern, base, cm):
+        run("g", lambda e: e.iota(out[0], pattern, base, cm), [], out[1], 130 + 2 * out[2] * CYCLE)
+
+    def fill(out, src, pattern, base, cm, value, op=A.not_equal):
+        run("g", lambda e: e.affine_select(out[0], src[0], pattern, op, value, base, cm), src[1], out[1], 170 + 2 * out[2] * CYCLE)
+
+    def col(k, rows=ALL):
+        return v("cF", k, k + 1, rows=rows)
+
+    def blk(name, k, n=128, rows=ALL, tag=None):
+        return v(name, n * k, n * k + n, rows=rows, tag=tag)
+
+    for y in range(2):
+        for e in range(2):
+            dma("y", T.TI[HALF[e], C * y:C * y + C], T.tst[HALF[y], :], [], [("TI.%d" % e, C * y, C * y + C)], 65536)
+        for e in range(2):
+            dma("s", T.P[HALF[e], C * y:C * y + C], T.pr[HALF[y], :], [], [("P.%d" % e, C * y, C * y + C)], 32768)
+        if y == 0:
+            dma("s", T.THI[0:8, :], T.th[:], [], ["THI"], 32)
+        for e in range(2):
+            dma("y", T["U%d" % y][HALF[e], 0:W], T.cov[HALF[y], :], [], ["U%d.%d" % (y, e)], 524288)
+
+    iota(v("cD"), [[1, 128]], 256, -1)
+    iota(v("cM"), [[1, 128]], 0, 0)
+    iota(v("cP"), [[0, 1]], 0, 1)
+    iota(v("cV", 0, 8), [[77, 8]], 0, 0)
+    iota(v("cV", 8, 16), [[5, 8]], 0, 0)
+    ms(v("mON"), 1.0)
+    for k, (s1, op) in enumerate(((4, SHR), (15, AND), (31, AND), (3, SHR), (7, AND), (1, SHR))):
+        ts(v("cI", k, k + 1), v("cP"), s1, None, op)
+    ts(v("cH"), v("cM"), 4, None, SHR)
+    ts(v("cT"), v("cD"), 15, None, AND)
+    ts(v("cJ"), v("cM"), 15, None, AND)
+    ts(v("cG"), v("cM"), 4, 3, SHR, AND)
+    cp(v("cF", 0, 6), v("cI", 0, 6))
+    ts(v("cB"), v("cT"), 1.0, None, A.mult)
+    ts(v("cBM"), v("cH"), col(0), None, A.is_equal)
+    ts(col(6), col(1), 613.0, None, A.mult)
+    ts(v("cA"), v("cBM"), -100.0, 100.0, A.mult, A.add)
+    ts(v("cW", 0, 8), v("cV", 0, 8), col(6), None, A.add)
+    tt(v("cDD"), v("cB"), v("cA"), A.add)
+    ts(v("cW", 0, 8), v("cW", 0, 8), W - 1, None, AND)
+    ts(v("cW", 8, 16), v("cV", 8, 16), 15, None, AND)
+
+    def eqm(out, val, scale):
+        ts(out, v("cDD"), float(val), float(scale), A.is_equal, A.mult)
+    ts(v("cF", 8, 16), v("cW", 0, 8), -0.5, None, A.add)
+    eqm(v("mI"), 0, 1)
+    cp(v("cBL"), v("cM"))
+    for k, x in ((40, -8.0), (41, -128.0), (42, 1536.0), (45, -1024.0 * 32881), (46, 192.0 - 127.5 / 256), (47, 47104.0)):
+        ms(col(k), x)
+    for y in range(2):
+        ms(v("U%d" % y, W, UW), -1.0)
+        for e in range(2):
+            ti = v("TI", C * y + e, C * y + C, 2, tag=e, rows=HALF[e])
+            ts(blk("QF", y, rows=HALF[e], tag=e), ti, 1.0 / 32, 1.0 / 64, A.mult, A.add)
+            ts(blk("ZN", y, rows=HALF[e], tag=e), ti, 256.0, NONE, A.is_ge, A.mult)
+            ts(blk("bk0", y, rows=HALF[e]), v("P", C * y + e, C * y + C, 2, tag=e, rows=HALF[e]), -128.0, None, A.add)
+        tt(blk("TB0", y), also(blk("QF", y), "QF.0", "QF.1"), also(blk("ZN", y), "ZN.0", "ZN.1"), A.max)
+        cp(blk("P0", y), blk("bk0", y))
+        cp(v("P1", 128 * y + 32 * RELU, 128 * y + 128), v("bk0", 128 * y + 32 * RELU, 128 * y + 128))
+        if RELU:
+            ms(v("P1", 128 * y, 128 * y + 32 * RELU), 0.0)
+            S(blk("PX", y, 512 * RELU), ind(blk("P0", y), v("cBL", 0, 32 * RELU)), F.Copy)
+    ms(v("cAG"), 1.0 / 16)
+    ms(v("cAG", 0, 16 * PIECE, 16), -32768.0)
+    for name, x in (("mIG", 2048.0), ("mI16", 16.0), ("mN16", -16.0), ("mN1", -1.0), ("mP", -32768.0), ("mI32", 32.0)):
+        S(v(name), v("mI"), F.Copy, scale=x)
+    ms(v("mH"), -1.0 / 256)
+    eqm(v("cC"), 15, -1.0 / 64)
+    fill(v("cC"), v("cC"), [[0, 8], [1, 16]], -15, 0, 0.0)
+    eqm(v("cE"), 0, 1.0 / 64)
+    tt(v("mD"), v("cE"), v("cC"), A.add)
+    ts(v("mV"), v("cM", 0, 8), col(0), 16.0, A.is_equal, A.mult)
+    for name, x in (("c32", 32.0), ("c1", 1.0)):
+        ms(v(name), x)
+        ms(v(name, 0, 128, 16), -2.0 ** 26)
+    ts(v("cPA"), v("cJ"), -1.0, 15.0, A.mult, A.add)
+    top8 = slice(0, 8)
+    ms(v("mOF", rows=slice(0, 32)), 1.0)
+    cp(v("THF", rows=top8), v("THI", rows=top8))
+    ts(col(7, top8), col(1, top8), -4.0, None, A.add)
+    for y in range(2):
+        ts(blk("TH8", y, rows=top8), v("cG", rows=top8), col(7 if y else 1, top8), v("THF", rows=top8), A.is_equal, A.mult)
+    MM(v("bk7", 0, C), v("mOF", rows=top8), v("TH8", rows=top8))
+    S(v("THR"), v("bk7", 0, C), bias=col(47))
+    ms(v("LR", rows=HIGH, tag="c"), 64.0)
+    ts(v("LR", rows=LOW), v("THR", rows=LOW), -49152.0, None, A.add)
+    ts(v("TH2"), v("THR", 0, C, 16), 2048.0, 2048.0, A.add, A.mult)
+    ts(v("L2"), v("TH2"), -49152.0 * 2048, None, A.add)
+    ms(v("mL", rows=LOW, tag=0), -32.0)
+    ms(v("mL", rows=slice(64, 96), tag=1), -2048.0)
+    ms(v("mL", rows=slice(96, 128), tag=2), 25616.0 / 2048)
+    ts(v("cF", 16, 24), v("cW", 8, 16), col(1), 8.0, A.is_equal, A.mult)
+    ts(v("cF", 24, 32), v("cW", 8, 16), col(1), None, A.not_equal)
+    ts(v("cF", 32, 40), v("cW", 8, 16), col(1), NONE, A.is_equal, A.mult)
+    ts(col(49), col(1), -15.0, None, A.add)
+    tt(col(48), col(49), col(49), A.mult)
+    ts(v("cA"), v("cD"), 256.0, 2.0, A.is_gt, A.mult)
+    tt(v("cB"), v("cA"), v("cBM"), A.mult)
+    eqm(v("cE"), 0, 2)
+    tt(v("mF0"), v("cB"), v("cE"), A.subtract)
+    ms(v("mC0", rows=LOW, tag=0), 511.75)
+    ms(v("mC0", rows=HIGH, tag=1), 1.0 / 4096)
+    for t in range(RO):
+        eqm(blk("mPT", t), (-(1 + t)) % 16, 256)
+        ts(blk("cBR", t, 8), v("cM", 0, 8), col(16 + t), None, A.add)
+        fill(blk("mFN", t), v("mF0"), [[0, 8], [1, 16]], -RHO[t], 0, 0.0)
+        fill(blk("mCR", t), also(v("mC0", tag=0), "mC0.1"), [[0, 8], [1, 16]], -RHO[t], 0, (7.5 + 1.0 / 64) / 128)
+    ms(v("FT"), 0.0)
+    ts(col(50), col(2), 2.0, None, A.is_equal)
+    ts(col(51), col(2), 4.0, None, A.is_equal)
+    for y in range(2):
+        for lo, hi, x in ((4, 256, -1.0), (5, 256, -1.0), (252, 380, -1.0), (253, 380, -1.0), (6, 128, 1.0)):
+            ms(also(v("FT", 384 * y + lo, 384 * y + hi, 32, tag="c%d" % lo), "FT"), x)
+        ts(v("FA", 400 * y, 400 * y + 1), col(2), 6.0, None, A.is_equal)
+        for k, x in ((1, 32.0), (2, -33.0)):
+            ts(v("FA", 400 * y + k, 400 * y + k + 1), col(51), x, col(50), A.mult, A.add)
+    ts(v("mTR"), v("cM", 0, 64), col(5), 16384.0, A.is_ge, A.mult)
+    for e in range(2):
+        ts(col(52 + e), v("cP"), 4.0, SPARE + 512.0 * e, A.mult, A.add)
+        ts(blk("mRF", e, 8), v("cM", 0, 8), col(0), col(52 + e), A.is_equal, A.mult)
+    ts(v("cK"), v("cJ"), col(1), -1.0, A.is_equal, A.add)
+    ms(v("cZ"), 0.0)
+    fill(v("cX"), v("cZ"), [[0, 2], [-32, 4], [0, 16]], -2, 1, 64.0)
+    for k in range(16):
+        fill(blk("mS", k), v("cX"), [[0, 8], [1, 16]], -k, 0, 0.0, A.is_equal)
+    ts(v("cY"), v("cPA"), -2.0, None, A.mult)
+    fill(v("mW"), v("cY"), [[0, 2], [-32, 4], [0, 16]], -7, 1, 0.0, A.is_equal)
+    fill(v("mW"), v("mW"), [[0, 2], [-32, 4], [0, 16]], -8, 1, 1.0)
+
+    def codes(t, y):
+        tb = blk("TB%d" % t, y)
+        qf = also(blk("QF", y), "QF.0", "QF.1") if t == 0 else blk("QF", y)
+        turned = blk("bk7", 1)
+        MM(turned, blk("mPT", t), tb)
+        tt(qf, tb, turned, A.mult)
+        ts(blk("FI", y), blk("QF", y), col(8 + t), BIG, A.add, A.min)
+        ts(blk("XI", y), blk("FI", y), 0x7FFF8FFF, None, AND)
+        ts(blk("OFF", y), blk("XI", y), float(VOID), None, A.min)
+        ts(blk("CM", y), blk("OFF", y), -2048.0, None, A.add)
+        S(also(blk("ZN", y), "ZN.0", "ZN.1") if t == 0 else blk("ZN", y), tb, F.Relu, bias=col(40))
+        S(blk("TR", y), tb, scale=col(24 + t), bias=col(32 + t))
+
+    sent = [0]
+
+    def visit(t, y):
+        more = t < RO - 1
+        bx, by, bz = ("bk%d" % (k + 3 * y) for k in (1, 2, 3))
+        U = also(v("U%d" % y), "U%d.0" % y, "U%d.1" % y)
+        w = lambda name: blk(name, y, 8)
+        b = lambda name: blk(name, y)
+        top = lambda name: v(name, 128 * y + 15, 128 * y + 128, 16)
+        mi = lambda i, n=1: v("M", 2048 * y + 128 * i, 2048 * y + 128 * (i + n))
+        ri = lambda i: v("R", 2048 * y + i, 2048 * y + 2048, 16)
+        key = blk(bx, 2)
+        for c0 in range(H * y, H * y + H, PIECE):
+            r = v("R", 16 * c0, 16 * (c0 + PIECE))
+            S(r, ind(U, v("OFF", c0, c0 + PIECE)), bias=col(41))
+            scan(v("KP", 16 * c0, 16 * (c0 + PIECE)), v("cAG"), r, A.add, A.max)
+        for i in range(16):
+            MM(v("bk7", i, 128, 16), ri(i), v("mV"))
+        scan(b("S2"), v("c1"), blk("bk7", 0), A.add, A.max)
+        if t + y in range(1, RO):
+            codes(t + y, 1 - y)
+        cp(w("KV"), top("S2"))
+        S(w("PV"), top("S2"), F.Relu, scale=-1024.0, bias=col(45))
+        ts(w("AV"), w("KV"), 15, None, AND)
+        kp = v("KP", 2048 * y + 15, 2048 * y + 2048, 16)
+        S(b("WP"), kp, bias=col(42))
+        MM(key, b("P1"), v("mP"), True, False)
+        MM(key, also(v("mL", tag=0), "mL.1", "mL.2"), also(b("LR"), "LR.c"), False, False)
+        for k in range(RELU):
+            bank = (by, bz)[k % 2]
+            MM(v(bank), v("mI"), blk("R", 4 * y + k, 512), True, False)
+            MM(v(bank), v("mN1"), blk("PX", RELU * y + k, 512), False, True)
+            S(blk("M", 4 * y + k, 512), v(bank), F.Relu)
+        lo = 2048 * y + 512 * RELU
+        for i in range(16):
+            tt(v("M", lo + i, 2048 * y + 2048, 16, tag="%d.%d" % (y, i)), v("R", lo + i, 2048 * y + 2048, 16), v("bk0", 128 * y + 32 * RELU, 128 * y + 128), A.max)
+        MM(key, kp, v("mI16"), False, False)
+        MM(key, b("WP"), v("mN16"), False, False)
+        for i in range(16):
+            MM(key, also(v("M", 2048 * y + i, 2048 * y + 2048, 16), "M.%d.%d" % (y, i)), v("mIG"), False, i == 15)
+        k1 = top("S1")
+        scan(b("S1"), v("c32"), key, A.add, A.max)
+        tt(w("KS"), k1, w("AV"), A.max)
+        ts(w("PU"), k1, 0.0, KEEP, A.is_ge, A.mult)
+        ts(w("AG"), w("KS"), 15, None, AND)
+        tt(w("P2"), w("PU"), w("PV"), A.max)
+        MM(blk(bx, 0), b("CM"), v("mD"), True, False)
+        MM(v(bx, 15, 128, 16), v("mI"), w("P2"), False, True)
+        tt(b("ST"), ind(w("AG"), v("cBL", 0, 8)), v("cPA"), A.is_gt)
+        scan(b("S3"), b("ST"), blk(bx, 0), A.mult, A.add)
+        ft = lambda tag, lo, hi: v("FT", 384 * y + lo, 384 * y + hi, 32, tag="%d%s" % (y, tag))
+        x, x0, x1, pr = w("X"), v("X", 8 * y, 8 * y + 4), v("X", 8 * y + 4, 8 * y + 8), v("PR", 16 * y, 16 * y + 12)
+        ts(blk("WN", 2 * y, 8), top("S3"), 4.0, 128.0 - 7.5 / 16, A.mult, A.add)
+        ts(x, top("S3"), -KEEP, -33.0, A.add, A.max)
+        S(v("PR", 16 * y, 16 * y + 8), x, F.Square)
+        tt(v("PR", 16 * y + 8, 16 * y + 12), x0, x1, A.mult)
+        S(ft("a", 2, 256), x, F.Copy)
+        S(ft("b", 3, 256), x, F.Copy)
+        S(ft("c", 254, 380), x0, F.Copy)
+        S(ft("d", 255, 380), x1, F.Copy)
+        tt(ft("e", 134, 256), x1, x0, A.subtract)
+        cp(ft("f", 0, 384), pr)
+        tt(ft("g", 1, 384), pr, ft("f", 0, 384), A.subtract)
+        ts(w("H2"), w("KS"), 1, 0xF0, SHR, AND)
+        S(ft("h", 7, 256), w("H2"), F.Copy, scale=1.0 / 16)
+        S(ft("i", 8, 256), w("H2"), F.Square, scale=1.0 / 16)
+        rows = ["FT.c%d" % k for k in (4, 5, 252, 253, 6)] + ["FT.%d%s" % (y, k) for k in "abcdefghi"]
+        MM(blk(by, 0), also(v("FT", 384 * y + 252, 384 * y + 380), *rows), v("mI"))
+        for e in range(2):
+            MM(v(by, 128 + e, 384, 2), also(blk("FT", 3 * y + e), *rows), v("mI"))
+        S(v("FA", 400 * y + 3, 400 * y + 387), v(by, 0, 384), F.Copy)
+        tt(w("G2"), w("KS"), w("L2"), A.add)
+        ts(w("GM"), w("G2"), 11, 15, SHR, AND)
+        ts(w("PN"), k1, 0.0, BIG, A.is_lt, A.mult)
+        tt(w("ZZ"), w("GM"), w("H2"), A.subtract)
+        tt(blk("WN", 2 * y + 1, 8), w("ZZ"), w("PN"), A.add)
+        if more and y == 1:
+            MM(v("bk7", 0, 16), blk("mON", 0), v("PN"))
+            S(v("MJ"), v("bk7", 0, 16), scale=1.0 / BIG, accum=v("MC", 0, 1))
+            S(v("MW"), v("MC", 0, 1), scale=1.0 / 256, bias=col(46))
+            S(v("MC", 1, 2), v("MW"), scale=-256.0, bias=v("MC", 0, 1))
+            S(v("LR", rows=LOW), v("THR", rows=LOW), bias=v("MC", 1, 2, rows=LOW))
+            S(v("MC", 2, 3), v("MC", 1, 2), scale=2048.0)
+            S(v("L2"), v("TH2"), bias=v("MC", 2, 3))
+        S(b("VB"), ind(blk("WN", y, 16), blk("cBR", t, 8)), scale=1.0 / 32)
+        MM(blk(bz, 0), blk("mCR", t), blk("mON", 0), True, False)
+        MM(blk(bz, 0), blk("mFN", t), b("ZN"), False, False)
+        MM(blk(bz, 0), b("VB"), v("mI"), False, True)
+        out, land = blk("TS", 2 * t + y), blk("TB%d" % (t + 1), y)
+        tt(out, b("TR"), blk(bz, 0), A.min)
+        step = 1 if more else -(RO - 1)
+        dst, src = T.cores[(rank + step) % N], T.cores[(rank - step) % N]
+        rid, pid, _se = topo.addr(dst)
+        arr = "arr%d_%d" % (t + 1, y)
+        run("g", lambda e: e.remote_dma(land[0], out[0], T.sem[arr], T.sem["snd"], pid, rid, topo.mask(core, dst)), out[1], land[1], 100.0, FAR,
+            (arr, len(topo.engines(src, core))))
+        sent[0] += len(topo.engines(core, dst))
+        fa = lambda lo, hi, step=1, rows=ALL: v("FA", 400 * y + lo, 400 * y + hi, step, rows=rows)
+        todo = []
+        for gr in range(4):
+            bank, rows = (bz, bx)[gr % 2], slice(32 * gr, 32 * gr + 7)
+            for be in range(2):
+                c0, n = 198 * (gr // 2) + 67 * be, 64 * be + 67
+                tile = ("tile" + bank, be, be + 1) if gr < 2 else ("tile" + bank, 0, 2 - 2 * be)
+                MM(also(v(bank, c0, c0 + n), tile), fa(131 + 128 * be, 259 + 128 * be, rows=rows), fa(0, n, rows=rows), True, False)
+                MM(v(bank, c0 + n - 64, c0 + n), v("mI"), v("mTR"), False, True)
+                todo.append((gr % 2, v("RD", 8 * y + 4 * be + gr, 8 * y + 4 * be + gr + 1), v(bank, c0, c0 + n)))
+        for side, out1, a in sorted(todo, key=lambda x: x[0]):
+            least(out1, a)
+        l16 = lambda name: blk(name, y, 16)
+        for k in range(16):
+            MM(v(by, 0, 16), blk("mS", k), fa(131 + k, 387, 16), k == 0, k == 15)
+        MM(blk(by, 1, C), v("mW"), fa(131, 387))
+        ts(l16("OL0"), v(by, 0, 16), 2048.0, 0.0, A.add, A.max)
+        S(blk("UG", y, C), ind(U, l16("OL0")), F.Copy)
+        S(blk("W1", y, C), blk(by, 1, C), F.Sign, bias=col(48))
+        tt(b("FE"), ind(w("RD"), v("cBL", 0, 8)), v("cK"), A.is_le)
+        for half in HALF:
+            for be in range(2):
+                MM(v(bz, 8 * be, 8 * be + 8, rows=half), blk("FE", 2 * y + be, 64), blk("mRF", be, 8))
+        tt(l16("OL"), l16("OL0"), v(bz, 0, 16), A.max)
+        run("v", lambda e: e.tensor_tensor(U[0].indirect(l16("OL")[0]), blk("UG", y, C)[0], blk("W1", y, C)[0], A.mult),
+            l16("OL")[1] + blk("UG", y, C)[1] + blk("W1", y, C)[1], U[1], 50 + C * SCATTER * CYCLE)
+
+    codes(0, 0)
+    codes(0, 1)
+    for t in range(RO):
+        visit(t, 0)
+        visit(t, 1)
+
+    ends = []
+    for y in range(2):
+        bx, by, half = "bk%d" % (1 + 3 * y), "bk%d" % (2 + 3 * y), HALF[y]
+        MM(v(by, 0, C, rows=half), v("mH", 0, 64), v("mON"), True, False)
+        for e in range(2):
+            MM(v(by, e, C, 2, rows=half), blk("mI32", e, 64), blk("TB%d" % RO, y), False, e == 1)
+        ts(v("OUTT", rows=half, tag=y), v(by, 0, C, rows=half), 256.0, None, A.min)
+        ends.append(dma("s", T.yt[half, :], T.OUTT[half, :], ["OUTT.%d" % y], ["yt%d" % y], 0))
+        for i in range(16):
+            MM(v(bx, 0, C, rows=half), v("mI", 0, 64), v("U%d" % y, i, W, 16), i == 0, i == 15)
+        cp(v("OUTC", rows=half, tag=y), v(bx, 0, C, rows=half))
+        ends.append(dma("y", T.yc[half, :], T.OUTC[half, :], ["OUTC.%d" % y], ["yc%d" % y], 0))
+
     count = {}
     known = {q: {} for q in queue}
     done = {}
@@ -65,13 +475,11 @@ def rank_program(g, core, T, topo):
             if known[q].get(k, 0) < x:
                 known[q][k] = x
 
-    def spans(views):
-        return [(x, 0, 1 << 20) if isinstance(x, str) else x for x in views]
-
-    def order(q, reads, writes):
+    for k in arrange(calls):
+        c = calls[k]
+        q = c["q"]
         todo = {}
-        reads, writes = spans(reads), spans(writes)
-        for views, wr in ((reads, False), (writes, True)):
+        for views, wr in ((c["reads"], False), (c["writes"], True)):
             for b, lo, hi in views:
                 for l2, h2, w2, q2, s2, v2 in last.get(b, []):
                     if b.startswith("bk"):
@@ -82,10 +490,15 @@ def rank_program(g, core, T, topo):
                         todo[s2] = v2
         for s2, v2 in sorted(todo.items(), key=lambda kv: -sum(done.get(kv, {}).values())):
             need(q, s2, v2)
-        return reads, writes
-
-    def note(q, reads, writes, sem, val):
-        for views, wr in ((reads, False), (writes, True)):
+        if c["signal"] is None:
+            c["call"](queue[q]).then_inc(T.sem[q], 1)
+            count[q] = count.get(q, 0) + 1
+            sem, val = q, count[q]
+        else:
+            c["call"](queue[q])
+            sem, val = c["signal"]
+        far = sem.startswith("arr")
+        for views, wr in (([] if far else c["reads"], False), (c["writes"], True)):
             for b, lo, hi in views:
                 keep = []
                 for e in last.get(b, []):
@@ -99,468 +512,7 @@ def rank_program(g, core, T, topo):
                     keep.append(e)
                 keep.append((lo, hi, wr, q, sem, val))
                 last[b] = keep
-        know = dict(known[q])
-        know[sem] = val
-        done[(sem, val)] = know
-
-    def run(q, call, reads, writes):
-        reads, writes = order(q, reads, writes)
-        call(queue[q]).then_inc(T.sem[q], 1)
-        count[q] = count.get(q, 0) + 1
-        note(q, reads, writes, q, count[q])
-
-    def dma(q, k, out, in_, reads, writes):
-        sem = "dma%d" % k
-        reads, writes = order(q, reads, writes)
-        queue[q].dma_start(out, in_).then_inc(T.sem[sem], 16)
-        note(q, reads, writes, sem, 16)
-
-    def V(name, out, wr, rd, *a, **k):
-        run("v", lambda e: {"tt": e.tensor_tensor, "ts": e.tensor_scalar, "cp": e.tensor_copy, "tr": e.transpose, "sc": e.tensor_tensor_scan,
-                            "rd": e.tensor_reduce, "ms": e.memset}[name](out, *a, **k), rd, wr)
-
-    def S(out, in_, wr, rd, func=F.Identity, **k):
-        run("s", lambda e: e.activation(out, in_, func, **k), rd, wr)
-
-    def MM(out, lhsT, rhs, start, stop, bank, rd):
-        run("p", lambda e: e.matmul(out, lhsT, rhs, start, stop), rd, [bank])
-
-    def ts(out, wr, in0, rd, s1, s2, op0, op1=None):
-        if op1 is None:
-            V("ts", out, wr, rd, in0, s1, None, op0)
-        else:
-            V("ts", out, wr, rd, in0, s1, s2, op0, op1)
-
-    def tt(out, wr, a, b, rd, op):
-        V("tt", out, wr, rd, a, b, op)
-
-    def iota(out, wr, pattern, base, cm):
-        run("g", lambda e: e.iota(out, pattern, base, cm), [], [wr])
-
-    def fill(name, c0, pattern, base, cm, value, src=None, s0=0):
-        n = 1
-        for p in pattern:
-            n *= p[1]
-        if src is None:
-            src, s0 = name, c0
-        run("g", lambda e: e.affine_select(T[name][:, c0:c0 + n], T[src][:, s0:s0 + n], pattern, A.not_equal, value, base, cm),
-            [(src, s0, s0 + n)], [(name, c0, c0 + n)])
-
-    def cell(name, c0, row, column, value, src=None, s0=0):
-        fill(name, c0, [[-16, 8], [1000, 16]], -row - 1000 * column, 1, value, src, s0)
-
-    def col(k):
-        return T.cF[:, k:k + 1]
-
-    def fcol(k, src, s1, s2, op0, op1=None):
-        ts(col(k), [("cF", k, k + 1)], col(src), [("cF", src, src + 1)], s1, s2, op0, op1)
-
-    def icol(k, s1, s2, op0, op1=None):
-        ts(T.cI[:, k:k + 1], [("cI", k, k + 1)], T.cP[:], ["cP"], s1, s2, op0, op1)
-
-    EAS = ["EA%d" % r for r in range(6)]
-    E16 = lambda r: slice(r, C, 16)
-    blk = lambda name, k: (T[name][:, 128 * k:128 * k + 128], (name, 128 * k, 128 * k + 128))
-
-    dma("y", 0, T.TI[:], T.tst[:], [], ["TI"])
-    dma("s", 1, T.P[:], T.pr[:], [], ["P"])
-    dma("y", 3, T.U[:, 0:W], T.cov[:], [], [("U", 0, W)])
-    dma("s", 2, T.THI[0:8, :], T.th[:], [], ["THI"])
-
-    iota(T.cD[:], "cD", [[1, 128]], 256, -1)
-    iota(T.cM[:], "cM", [[1, 128]], 0, 0)
-    iota(T.cP[:], "cP", [[0, 1]], 0, 1)
-    V("ms", T.mON[:], ["mON"], [], 1.0)
-    for k, x in ((60, -511.0 * FLAG), (61, MAGIC), (62, -MAGIC), (63, -127.5), (59, BIG)):
-        V("ms", T.cF[:, k:k + 1], [("cF", k, k + 1)], [], x)
-
-    def icodes(t):
-        iota(blk("iKC", t)[0], blk("iKC", t)[1], [[0, 8], [613, 16]], 77 * t, 0)
-    icodes(0)
-    iota(T.cG[:], "cG", [[1, 16]], 0, 0)
-    icol(0, 4, None, SHR)
-    icol(1, 15, None, AND)
-    icol(2, 4, 1, SHR, AND)
-    icol(3, 1, None, AND)
-    icol(4, 31, 1, AND, SHR)
-    icol(5, 1, None, SHR)
-    icol(6, 5, None, SHR)
-    icol(7, 31, None, AND)
-    V("cp", T.cF[:, 0:8], [("cF", 0, 8)], ["cI"], T.cI[:])
-    ts(T.cJ[:], ["cJ"], T.cM[:], ["cM"], 4, None, SHR)
-    ts(T.cT[:], ["cT"], T.cD[:], ["cD"], 15, None, AND)
-    ts(T.cBM[:], ["cBM"], T.cJ[:], ["cJ", ("cF", 0, 1)], col(0), None, A.is_equal)
-    ts(T.cB[:], ["cB"], T.cT[:], ["cT"], 1.0, None, A.mult)
-    ts(T.cA[:], ["cA"], T.cBM[:], ["cBM"], -100.0, 100.0, A.mult, A.add)
-    tt(T.cDD[:], ["cDD"], T.cB[:], T.cA[:], ["cA", "cB"], A.add)
-
-    def eqm(name, k, val, scale):
-        ts(blk(name, k)[0], [blk(name, k)[1]], T.cDD[:], ["cDD"], float(val), float(scale), A.is_equal, A.mult)
-    eqm("mI", 0, 0, 1)
-
-    def const_t(t):
-        eqm("mPT", t, (-(1 + t)) % 16, 1)
-        if t == 0:
-            tt(blk("mQT", t)[0], [blk("mQT", t)[1]], blk("mPT", t)[0], T.mI[:], [blk("mPT", t)[1], "mI"], A.add)
-        x = slice(128 * t, 128 * t + 128)
-        part = ((0, "KCa%d" % t, 4080, 0.0), (64, "KCb%d" % t, 15, 1.0 / 64))
-        for p0, nm, bits, add in part:
-            ts(T.jKC[p0:p0 + 64, x], ["j" + nm], T.iKC[p0:p0 + 64, x], [blk("iKC", t)[1]], bits, None, AND)
-        for p0, nm, bits, add in part:
-            ts(T.mKC[p0:p0 + 64, x], [nm], T.jKC[p0:p0 + 64, x], ["j" + nm], 0.25, add, A.mult, A.add)
-
-    def const_g(t):
-        rho = RHO[t]
-        if t:
-            fill("mQT", 128 * t, [[-1, 128]], 0, 1, 1.0, "mPT", 128 * t)
-        fill("mFN", 128 * t, [[0, 8], [1, 16]], -rho, 0, 0.0, "mF0", 0)
-        cell("mNR", 128 * t, rho, rho, 0.0, "mI", 0)
-        for k, (r, x) in enumerate(((1, -32.0), (2, 2.0), (3, 32.0), (4, 480.0))):
-            if k == 0:
-                cell("mBR", 128 * t, r, rho, x, "mZ", 0)
-            else:
-                cell("mBR", 128 * t, r, rho, x)
-    const_t(0)
-    ts(T.TB0[:], ["TB0"], T.TI[:], ["TI"], 2.0, None, A.mult)
-
-    def codes(t):
-        TB = "TB%d" % t
-        tb = T[TB]
-        S(T.NF[:], tb[:], ["NF"], [TB, ("cF", 59, 64)], F.Relu, scale=FLAG, bias=col(60))
-        MM(T.bk0[:, 0:C], blk("mPT", t)[0], tb[:], True, True, "bk0", [blk("mPT", t)[1], TB])
-        MM(T.bk1[:, 0:C], blk("mKC", t)[0], T.mON[:], True, False, "bk1", ["KCa%d" % t, "KCb%d" % t, "mON"])
-        MM(T.bk1[:, 0:C], blk("mQT", t)[0], tb[:], False, False, "bk1", [blk("mQT", t)[1], TB])
-        MM(T.bk1[:, 0:C], blk("mQT", t)[0], T.NF[:], False, True, "bk1", [blk("mQT", t)[1], "NF"])
-
-    def codev(t, k):
-        if k == 0:
-            tt(T.QF[:], ["QF"], T["TB%d" % t][:], T.bk0[:, 0:C], ["TB%d" % t, "bk0"], A.mult)
-        elif k == 1:
-            tt(T.FI[:], ["FI"], T.QF[:], T.bk1[:, 0:C], ["QF", "bk1"], A.add)
-        elif k == 2:
-            ts(T.XI[:], ["XI"], T.FI[:], ["FI"], 4, 0x7FFF8FFF, SHR, AND)
-        elif k == 3:
-            ts(T.OFF[:], ["OFF"], T.XI[:], ["XI"], float(VOID), None, A.min)
-        else:
-            ts(T.CM[:], ["CM"], T.XI[:], ["XI"], float(VOID - 1), -7.5, A.min, A.add)
-
-    def codes2(t):
-        S(T.MG[:], T.CM[:], ["MG"], ["CM", ("cF", 59, 64)], scale=1.0 / 16, bias=col(61))
-        S(T.N4[:], T.MG[:], ["N4"], ["MG", ("cF", 59, 64)], bias=col(62))
-        MM(T.bk6[:, 0:C], blk("mFN", t)[0], T.NF[:], True, True, "bk6", [blk("mFN", t)[1], "NF"])
-        S(T.FN[:], T.bk6[:, 0:C], ["FN"], ["bk6"], F.Relu, scale=1.0 / FLAG)
-
-    codes(0)
-    V("ms", T.U[:, W:UW], [("U", W, UW)], [], -1.0)
-    V("ms", T.cMASK[:], ["cMASK"], [], 1.0)
-    codev(0, 0)
-    V("ms", T.cNEG[:], ["cNEG"], [], 0.0)
-    codev(0, 1)
-    V("ms", T.cMASK[:, E16(0)], ["cMASK"], [], 0.0)
-    V("ms", T.cNEG[:, E16(0)], ["cNEG"], [], -2.0 ** 26)
-    V("ms", T.EA[:], EAS, [], 0.0)
-    codev(0, 2)
-    V("ms", T.EB[:], ["EB"], [], 1.0)
-    V("ms", T.EA[:, E16(4)], ["EA4"], [], 1.0)
-    V("ms", T.mZ[:], ["mZ"], [], 0.0)
-    V("ms", T.mXX[:], ["mXX"], [], 0.0)
-    codev(0, 3)
-    codev(0, 4)
-    allpx = ["PXP%d" % i for i in range(16)]
-    for i in range(16):
-        if i < 11:
-            S(T.PXP[:, i:W:16], T.P[:], [allpx[i]], ["P"], F.Copy)
-        else:
-            V("cp", T.PXP[:, i:W:16], [allpx[i]], ["P"], T.P[:])
-
-    S(T.mI16[:], T.mI[:], ["mI16"], ["mI"], F.Copy, scale=16.0)
-    S(T.mP256[:], T.mI[:], ["mP256"], ["mI"], F.Copy, scale=-256.0)
-    ts(T.cJ[:], ["cJ"], T.cM[:], ["cM"], 15, None, AND)
-    ts(T.mCH[:], ["mCH"], T.cJ[:], ["cJ"], -1.0 / 128, 15.0 / 128, A.mult, A.add)
-    ts(T.mCV[:], ["mCV"], T.cJ[:], ["cJ"], -2.0, 30.0, A.mult, A.add)
-    S(T.mIF[:], T.mI[:], ["mIF"], ["mI"], F.Copy, scale=1.0 / 16)
-
-    def constants_0():
-        ts(T.cB[:], ["cB"], T.cJ[:], ["cJ"], 1.0, None, A.mult)
-        ts(T.cT[:], ["cT"], T.cD[:], ["cD"], 256.0, None, A.is_gt)
-        tt(T.cMI[:], ["cMI"], T.cB[:], T.cA[:], ["cB", "cA"], A.add)
-        tt(T.cB[:], ["cB"], T.cT[:], T.cBM[:], ["cT", "cBM"], A.mult)
-        for i in range(16):
-            ts(blk("mE", i)[0], [blk("mE", i)[1]], T.cMI[:], ["cMI"], float(i), 4096.0, A.is_equal, A.mult)
-        tt(T.mF0[:], ["mF0"], T.mI[:], T.cB[:], ["cB", "mI"], A.subtract)
-        const_g(0)
-        fill("mB0", 0, [[-16, 8], [0, 16]], 0, 1, 2.0, "mZ", 0)
-        fill("mB0", 0, [[-16, 8], [0, 16]], -5, 1, -512.0)
-        for r, m, x in [(k, k, 512.0) for k in range(3)] + [(3 + k, 8 + k, -256.0) for k in range(3)] + [(8 + k, 3 + k, -256.0) for k in range(3)] + \
-                [(6, 11, -1.0), (11, 6, 1.0), (7, 12, -16384.0)]:
-            cell("mXX", 0, r, m, x)
-
-    def constants_a():
-        V("cp", T.cBL[:], ["cBL"], ["cG"], T.cG[:])
-        V("cp", T.THF[0:8, :], ["THF"], ["THI"], T.THI[0:8, :])
-        ts(T.THQ[0:8, :], ["THQ"], T.cG[0:8, :], ["cG"], 1, None, AND)
-        ts(T.cT[:], ["cT"], T.cM[:], ["cM"], 5, None, SHR)
-        ts(T.TH8[0:8, :], ["TH8"], T.THQ[0:8, :], ["THQ", ("cF", 0, 8), "THF"], T.cF[0:8, 3:4], T.THF[0:8, :], A.is_equal, A.mult)
-        ts(T.mTH[0:8, :], ["mTH"], T.cT[0:8, :], ["cT", ("cF", 0, 8)], T.cF[0:8, 5:6], 16.0, A.is_equal, A.mult)
-        MM(T.bk6[:, 0:16], T.mTH[0:8, :], T.TH8[0:8, :], True, True, "bk6", ["mTH", "TH8"])
-        V("cp", T.TH16[:], ["TH16"], ["bk6"], T.bk6[:, 0:16])
-        V("cp", T.LIM[:], ["LIM"], ["bk6"], T.bk6[:, 0:16])
-        ts(T.mCX[0:64, :], ["mCX0"], T.mCV[0:64, :], ["mCV"], 2.0, None, A.mult)
-        V("ms", T.mCX[64:128, :], ["mCX1"], [], 15.0 / 2048)
-
-    def constants_b():
-        fcol(20, 1, 0.0, 1.0 / 4096, A.is_equal, A.mult)
-        for r, x in ((1, 16.0), (2, 256.0), (7, 8192.0)):
-            fcol(21 + r, 1, float(r), x / 4096, A.is_equal, A.mult)
-        for r in (1, 2, 7):
-            tt(col(20), [("cF", 20, 21)], col(20), col(21 + r), [("cF", 20, 29)], A.add)
-
-    def constants_c():
-        ts(T.X1[:], ["X1"], T.cG[:], ["cG"], 1, None, SHR)
-        fcol(30, 2, 0.0, None, A.is_equal)
-        ts(T.EB[:, E16(6)], ["EB"], T.X1[:], ["X1", ("cF", 7, 8)], 32.0, col(7), A.mult, A.add)
-        ts(T.cDUM[:], ["cDUM"], T.cG[:], ["cG", ("cF", 1, 2)], 16.0, col(1), A.mult, A.add)
-        fcol(33, 3, 16.0, col(4), A.mult, A.add)
-
-    def constants_d():
-        ts(T.cDUM[:], ["cDUM"], T.cDUM[:], ["cDUM"], float(DUMMY), None, A.add)
-        for a in range(1, 4):
-            fcol(33 + a, 33, 32.0 * a, None, A.add)
-        for s in range(4):
-            fcol(40 + s, 6, float(s), None, A.is_equal)
-        for a in range(4):
-            ts(blk("mLM", a)[0], [blk("mLM", a)[1]], T.cM[:], ["cM", ("cF", 33 + a, 34 + a)], col(33 + a), 8192.0, A.is_equal, A.mult)
-
-    def votes(k):
-        lo, hi = 1024 * k, 1024 * k + 1024
-        for i in range(16):
-            MM(T.bk2[:, NT * k:NT * (k + 1)], blk("mE", i)[0], T.R[:, lo + i:hi:16], False, False, "bk2", [blk("mE", i)[1], ("R", lo, hi)])
-
-    for t in range(RO):
-        first, more = t == 0, t < RO - 1
-        TB = "TB%d" % t
-        LBS = ["LB00", "LB10", "LB01", "LB11"]
-        l3 = T.EA[:, E16(3)]
-
-        def gather_v(c0, n):
-            lo, hi = 16 * c0, 16 * (c0 + n)
-            tt(T.M[:, lo:hi], [("M", lo, hi)], T.U[:].indirect(T.OFF[:, c0:c0 + n]), T.PXP[:, lo:hi], ["U", ("OFF", c0, c0 + n)] + allpx, A.max)
-
-        def gather_s(k):
-            lo, hi = 1024 * k, 1024 * k + 1024
-            S(T.R[:, lo:hi], T.U[:].indirect(T.OFF[:, NT * k:NT * k + NT]), [("R", lo, hi)], ["U", ("OFF", NT * k, NT * k + NT)], F.Copy)
-
-        def gains(k):
-            lo, hi, bank, c0 = 1024 * k, 1024 * k + 1024, ("bk0", "bk1")[k // 2], NT * (k % 2)
-            for i in range(16):
-                MM(T[bank][:, c0:c0 + NT], T.mI16[:], T.M[:, lo + i:hi:16], False, k % 2 == 1 and i == 15, bank, ["mI16", ("M", lo, hi)])
-
-        def level(h, step):
-            a, b, a8 = 128 * h, 128 * h + 128, 8 * h
-            kt, s1, tau, wt = ("KT", a, b), ("S1", a, b), ("TAU", a8, a8 + 8), ("WT", a, b)
-            gb, wb = ("bk0", "bk1")[h], ("bk3", "bk4")[h]
-            if step == 0:
-                V("tr", T.KT[:, a:b], [kt], [gb], T[gb][:, 0:128])
-            elif step == 1:
-                V("sc", T.S1[:, a:b], [s1], ["cMASK", kt], T.cMASK[:, 0:128], T.KT[:, a:b], 0.0, A.mult, A.max)
-            elif step == 2:
-                for gm in range(2):
-                    ts(T.LB[:, a8 + gm:a8 + 8:2], ["LB%d%d" % (gm, h)], T.S1[:, a + 15 + 16 * gm:b:32], [s1, "LIM"], T.LIM[:, gm:gm + 1], BIG, A.is_lt, A.mult)
-            elif step == 3:
-                tt(T.TAU[:, a8:a8 + 8], [tau], T.LB[:, a8:a8 + 8], T.S1[:, a + 15:b:16], ["LB0%d" % h, "LB1%d" % h, s1], A.max)
-            elif step == 4:
-                tt(T.WT[:, a:b], [wt], T.TAU[:, a8:a8 + 8].indirect(T.cBL[:, 0:8]), T.KT[:, a:b], [tau, "cBL", kt], A.is_le)
-            else:
-                V("tr", T[wb][:, 0:128], [wb], [wt], T.WT[:, a:b])
-
-        for h in range(2):
-            gb = ("bk0", "bk1")[h]
-            MM(T[gb][:, 0:128], T.mCH[:], T.mON[:, 0:128], True, False, gb, ["mCH", "mON"])
-            MM(T[gb][:, 0:128], T.mP256[:], T.P[:, 128 * h:128 * h + 128], False, False, gb, ["mP256", "P"])
-        MM(T.bk2[:, 0:C], T.mCV[:], T.mON[:], True, False, "bk2", ["mCV", "mON"])
-        for k in range(2):
-            gather_v(NT * k, NT)
-            gather_s(k)
-            if first and k == 0:
-                constants_a()
-                constants_0()
-            gains(k)
-        votes(0)
-        gather_v(128, 32)
-        gather_s(2)
-        level(0, 0)
-        gather_v(160, 32)
-        gains(2)
-        votes(1)
-        level(0, 1)
-        gather_s(3)
-        for k in range(4):
-            gather_v(192 + 16 * k, 16)
-            level(0, 2 + k)
-        gains(3)
-        votes(2)
-        if first:
-            codes2(0)
-        votes(3)
-        MM(T.bk2[:, 0:C], T.mI[:], T.N4[:], False, True, "bk2", ["mI", "N4"])
-        if first:
-            constants_b()
-
-        def pick(h, i):
-            pr, xb, wb = "PR%d_%d" % (h, i), ("bk5", "bk7")[h], ("bk3", "bk4")[h]
-            lo, hi = 2048 * h, 2048 * h + 2048
-            tt(T.PR[:, lo + i:hi:16], [pr], T.R[:, lo + i:hi:16], T[wb][:, 0:128], [("R", lo, hi), wb], A.mult)
-            MM(T[xb][:, 0:128], blk("mE", i)[0], T.PR[:, lo + i:hi:16], False, i == 15, xb, [blk("mE", i)[1], pr])
-
-        for h in range(2):
-            xb = ("bk5", "bk7")[h]
-            MM(T[xb][:, 0:128], T.mIF[:], T.CM[:, 128 * h:128 * h + 128], True, False, xb, ["mIF", "CM"])
-            MM(T[xb][:, 0:128], T.mCX[:], T.mON[:, 0:128], False, False, xb, ["mCX0", "mCX1", "mON"])
-        vote = {
-            9: lambda: ts(T.X1[:], ["X1"], T.TAU[:], ["TAU"], 15, None, AND),
-            10: lambda: V("tr", T.VT[:], ["VT"], ["bk2"], T.bk2[:, 0:C]),
-            12: lambda: V("sc", T.S2[:], ["S2"], ["cNEG", "VT"], T.cNEG[:], T.VT[:], 0.0, A.add, A.max),
-            13: lambda: ts(T.X2[:], ["X2"], T.TAU[:], ["TAU"], 4, 15, SHR, AND),
-            14: lambda: V("cp", T.KV[:], ["KV"], ["S2"], T.S2[:, 15:C:16]),
-            15: lambda: ts(T.NB[:], ["NB"], T.KV[:], ["KV"], 255, None, AND),
-        }
-        for i in range(16):
-            pick(0, i)
-            if i % 2 == 1 and i < 12:
-                level(1, i // 2)
-                if i // 2 == 2:
-                    S(T.TV[:], T.LB[:], ["TV"], LBS + [("cF", 59, 64)], scale=-1.0, bias=col(59))
-                    S(l3, T.LB[:], ["EA3"], LBS, F.Sign)
-            if i in vote:
-                vote[i]()
-        if more:
-            MM(T.bk6[:, 0:16], T.mON[:, 0:128], l3, True, True, "bk6", ["mON", "EA3"])
-            S(T.MJK[:], T.bk6[:, 0:16], ["MJK", "MC"], ["bk6"], scale=16.0, accum_out=T.MC[:])
-            S(T.MA[:], T.MC[:], ["MA"], ["MC", ("cF", 59, 64)], scale=1.0 / 16, bias=col(63))
-            S(T.MQ[:], T.MA[:], ["MQ"], ["MA", ("cF", 59, 64)], scale=1.0 / 256, bias=col(61))
-            S(T.MR[:], T.MQ[:], ["MR"], ["MQ", ("cF", 59, 64)], bias=col(62))
-            S(T.MF[:], T.MR[:], ["MF"], ["MR", "MC"], scale=-4096.0, bias=T.MC[:])
-
-        def claim(h, step):
-            x, s3, xb = ("XT", 128 * h, 128 * h + 128), ("S3", 128 * h, 128 * h + 128), ("bk5", "bk7")[h]
-            if step == 0:
-                V("tr", T.XT[:, x[1]:x[2]], [x], [xb], T[xb][:, 0:128])
-            else:
-                V("sc", T.S3[:, x[1]:x[2]], [s3], ["cNEG", x], T.cNEG[:, 0:128], T.XT[:, x[1]:x[2]], 0.0, A.add, A.max)
-        a, b = C * t, C * t + C
-
-        def spread():
-            V("tr", T.EN[:], ["EN"], EAS, T.EA[:])
-            MM(T.bk0[:, 0:C], T.mB0[:], T.EN[:], True, True, "bk0", ["mB0", "EN"])
-            MM(T.bk1[:, 0:C], blk("mNR", t)[0], T[TB][:], True, False, "bk1", [blk("mNR", t)[1], TB])
-            MM(T.bk1[:, 0:C], blk("mBR", t)[0], T.EN[:], False, True, "bk1", [blk("mBR", t)[1], "EN"])
-
-        def leave():
-            tt(T.TS[:, a:b], [("TS", a, b)], T.DL[:], T.bk1[:, 0:C], ["DL", "bk1"], A.add)
-            step = 1 if more else -(RO - 1)
-            dst, src = T.cores[(rank + step) % N], T.cores[(rank - step) % N]
-            rid, pid, _se = topo.addr(dst)
-            order("g", [("TS", a, b)], [])
-            g.remote_dma(T["TB%d" % (t + 1)][:], T.TS[:, a:b], T.sem["arr%d" % (t + 1)], T.sem["snd"], pid, rid, topo.mask(core, dst))
-            last["TB%d" % (t + 1)] = [(0, 1 << 20, True, "r", "arr%d" % (t + 1), len(topo.engines(src, core)))]
-            for u in range(1 if first else t + 2, min(t + 3, RO)):
-                icodes(u)
-        chain = [
-            lambda: tt(T.EA[:, E16(5)], ["EA5"], T.S2[:, 15:C:16], T.TV[:], ["S2", "TV"], A.is_ge),
-            lambda: V("cp", T.EA[:, E16(1)], ["EA1"], ["X1"], T.X1[:]),
-            lambda: V("cp", T.EA[:, E16(2)], ["EA2"], ["X2"], T.X2[:]),
-            lambda: tt(T.EA[:, E16(0)], ["EA0"], T.NB[:], T.EA[:, E16(5)], ["NB", "EA5"], A.mult),
-            None,
-            spread,
-            lambda: claim(0, 0),
-            None,
-            lambda: tt(T.DL[:], ["DL"], T.FN[:], T.bk0[:, 0:C], ["FN", "bk0"], A.mult),
-            lambda: claim(0, 1),
-            leave,
-        ]
-        for i in range(16):
-            pick(1, i)
-            if i < len(chain) and chain[i] is not None:
-                chain[i]()
-        for h, wb in enumerate(("bk3", "bk4")):
-            S(T.W1[:, 128 * h:128 * h + 128], T[wb][:, 0:128], [("W1", 128 * h, 128 * h + 128)], [wb], scale=-1.0, bias=1.0)
-        if more:
-            ts(T.LIM[:], ["LIM"], T.TH16[:], ["TH16", "MF"], T.MF[:], None, A.add)
-        if first:
-            S(T.mEL[:], T.mE[:], ["mEL"], ["mE", ("cF", 20, 21)], F.Copy, scale=col(20))
-            constants_c()
-
-        claim(1, 0)
-        claim(1, 1)
-        if more:
-            if first:
-                const_t(1)
-                const_g(1)
-            codes(t + 1)
-        ts(T.KI[:], ["KI"], T.S3[:, 15:C:16], ["S3"], 16.0, None, A.mult)
-        tt(T.EB[:, E16(7)], ["EBz"], T.S3[:, 15:C:16], T.LB[:], ["EB", "S3"] + LBS, A.is_lt)
-        for r in range(3):
-            ts(T["D%d" % r][:], ["D%d" % r], T.KI[:], ["KI"], 4 * r, 15, SHR, AND)
-        for r in range(3):
-            V("cp", T.EB[:, E16(r)], ["EBd%d" % r], ["EB", "D%d" % r], T["D%d" % r][:])
-        for r in range(3):
-            tt(T.EB[:, E16(3 + r)], ["EBs%d" % r], T["D%d" % r][:], T["D%d" % r][:], ["EB", "D%d" % r], A.mult)
-        V("tr", T.VN[:], ["VN"], ["EB", "EBz"] + ["EBd%d" % r for r in range(3)] + ["EBs%d" % r for r in range(3)], T.EB[:])
-        MM(T.bk2[:, 0:C], T.mXX[:], T.VN[:], True, True, "bk2", ["mXX", "VN"])
-        if more:
-            codev(t + 1, 0)
-        ts(T.VM[:, 0:2 * C:2], ["VM0"], T.VN[:], ["VN", ("cF", 30, 31)], col(30), None, A.mult)
-        ts(T.VM[:, 1:2 * C:2], ["VM1"], T.VN[:], ["VN", ("cF", 2, 3)], col(2), None, A.mult)
-        S(T.RV[:], T.bk2[:, 0:C], ["RV"], ["bk2"], F.Copy)
-        for k in range(16):
-            MM(T.bk6[:, 0:16], blk("mEL", k)[0], T.VN[:, k:C:16], k == 0, False, "bk6", ["mEL", "VN"])
-        if more:
-            codev(t + 1, 1)
-        if first:
-            constants_d()
-        if more:
-            codev(t + 1, 2)
-        banks = ["bk3", "bk4", "bk5", "bk7", "bk2"]
-        for j, (a4, pair) in enumerate(((0, (3, 2)), (0, (1, 0)), (1, (3, 2)), (3, (3, 2)), (2, (3, 2)), (1, (1, 0)), (2, (1, 0)), (3, (1, 0)))):
-            bank = banks[j % len(banks)]
-            rows = slice(32 * a4, 32 * a4 + 32)
-            part = []
-            for be in pair:
-                n = 64 * (be + 1)
-                c0 = 0 if be == pair[0] else 64 * (pair[0] + 1)
-                MM(T[bank][:, c0:c0 + n], T.VM[rows, 128 * be:128 * be + 128], T.RV[rows, 0:n], True, True, bank, ["VM0", "VM1", "RV"])
-                part.append((T[bank][:, c0:c0 + n], n, 4 * a4 + be))
-            for x, n, k in part:
-                if pair == (3, 2) and a4 < 3:
-                    S(T.JK[:, 256 * k:256 * k + n], x, ["JK%d" % k, ("FL", k, k + 1)], [bank], F.Relu, accum_out=T.FL[:, k:k + 1])
-                else:
-                    V("rd", T.FL[:, k:k + 1], [("FL", k, k + 1)], [bank], x, AxisListType.X, A.max)
-        for s in range(4):
-            if s < 2:
-                S(T.FB[:, s:64:4], T.FL[:], ["FB%d" % s], ["FL", ("cF", 40 + s, 41 + s)], F.Relu, scale=col(40 + s))
-            else:
-                ts(T.FB[:, s:64:4], ["FB%d" % s], T.FL[:], ["FL", ("cF", 40 + s, 41 + s)], 0.0, col(40 + s), A.is_gt, A.mult)
-        for a4 in range(4):
-            MM(T.bk6[:, 0:16], blk("mLM", a4)[0], T.FB[:, 16 * a4:16 * a4 + 16], False, a4 == 3, "bk6", ["mLM"] + ["FB%d" % s for s in range(4)])
-        if more:
-            codev(t + 1, 3)
-            codev(t + 1, 4)
-        tt(T.YM[:], ["YM"], T.cDUM[:], T.bk6[:, 0:16], ["cDUM", "bk6"], A.min)
-        V("cp", T.OL[:], ["OL"], ["YM"], T.YM[:])
-        S(T.UG[:], T.U[:].indirect(T.OL[:]), ["UG"], ["U", "OL"], F.Copy)
-        if more:
-            codes2(t + 1)
-        if t + 2 < RO:
-            const_t(t + 2)
-            const_g(t + 2)
-        tt(T.U[:].indirect(T.OL[:]), ["U"], T.UG[:], T.W1[:], ["UG", "W1", "OL"], A.mult)
-
-    S(T.OUTT[:], T["TB%d" % RO][:], ["OUTT"], ["TB%d" % RO], scale=0.5)
-    dma("s", 4, T.yt[:], T.OUTT[:], ["OUTT"], ["yt"])
-    for i in range(16):
-        MM(T.bk0[:, 0:C], T.mI[:], T.U[:, i:W:16], i == 0, i == 15, "bk0", ["mI", "U"])
-    V("cp", T.OUTC[:], ["OUTC"], ["bk0"], T.bk0[:, 0:C])
-    dma("y", 5, T.yc[:], T.OUTC[:], ["OUTC"], ["yc"])
-    need("y", "dma4", 16)
-    need("y", "dma5", 16)
-    g.wait_ge(T.sem["snd"], sum(len(topo.engines(core, T.cores[(rank + (1 if t < RO - 1 else 1 - RO)) % N])) for t in range(RO)))
+        done[(sem, val)] = {sem: val} if far else dict(known[q], **{sem: val})
+    for sem in ends:
+        need("y", sem, 16)
+    g.wait_ge(T.sem["snd"], sent[0])

@@ -13,7 +13,10 @@ BIG = 2.0 ** 20
 KEEP = 2.0 ** 17
 RELU = 2
 PIECE = 32
-LEAD, SHORT = 4000.0, 3.0
+LEAD, SHORT = 2000.0, 3.0
+ONV = "qA"
+TURNS = 1
+AHEAD, FIT = 0.0, 60.0
 RHO = [(5 * t) % 16 for t in range(RO)]
 CYCLE, PE, GATHER, SCATTER, HOP, FAR, RATE = 0.83, 0.42, 1.3, 3.0, 240.0, 1500.0, 300.0
 
@@ -40,7 +43,7 @@ for _n, _w, _d in [
     ("mPT", 128 * RO, "bfloat16"), ("mFN", 128 * RO, "bfloat16"), ("mF0", 128, "bfloat16"), ("mCR", 128 * RO, "float16"), ("mC0", 128, "float16"),
     ("mD", 128, "bfloat16"), ("mV", 8, "bfloat16"), ("mL", 128, "float16"), ("mON", C, "bfloat16"), ("mOF", 128, "float32"),
     ("mRF", 16, "float16"), ("mTR", 64, "bfloat16"), ("mS", 2048, "bfloat16"), ("mW", 128, "bfloat16"), ("cX", 128, "bfloat16"), ("cY", 128, "bfloat16"), ("cZ", 128, "bfloat16"),
-    ("cAG", 16 * PIECE, "bfloat16"), ("c32", 128, "bfloat16"), ("c1", 128, "bfloat16"), ("cPA", 128, "bfloat16"), ("cK", 128, "bfloat16"),
+    ("cAG", 1024, "bfloat16"), ("c32", 128, "bfloat16"), ("c1", 128, "bfloat16"), ("cPA", 128, "bfloat16"), ("cK", 128, "bfloat16"),
     ("cBL", 128, "uint16"), ("cBR", 8 * RO, "uint16"),
 ]:
     SCRATCH[_n] = ("sbuf", [128, _w], _d)
@@ -90,14 +93,41 @@ def arrange(calls):
             ready[c["q"]][k] = 0.0
     while len(start) < len(calls):
         t, q = min((max(free[q], min(r.values())), q) for q, r in ready.items() if r)
-        k = min((k for k, x in ready[q].items() if x <= t), key=lambda k: (SHORT * calls[k]["time"] - way[k], k))
+        rank = lambda k: (SHORT * calls[k]["time"] - way[k], k)
+        k = min((k for k, x in ready[q].items() if x <= t), key=rank)
+        soon = [m for m, x in ready[q].items() if t < x < t + calls[k]["time"] - FIT and way[m] > way[k] + AHEAD]
+        if soon and AHEAD:
+            m = min(soon, key=rank)
+            k = min((n for n, x in ready[q].items() if max(x, t) + calls[n]["time"] <= ready[q][m] + FIT), key=rank, default=m)
+            t = max(t, ready[q][k])
         del ready[q][k]
         start[k], free[q] = t, t + calls[k]["time"]
         for m in after[k]:
             left[m] -= 1
             if not left[m]:
                 ready[calls[m]["q"]][m] = max(start[j] + calls[j]["time"] + gap for j, gap in before[m].items())
-    return sorted(range(len(calls)), key=lambda k: (start[k], k))
+
+    def place(order, links, least):
+        start, busy = {}, {}
+        for k in order:
+            d, line = calls[k]["time"], busy.setdefault(calls[k]["q"], [])
+            t = max([start[j] + calls[j]["time"] + gap for j, gap in links[k].items()] + [least[k]])
+            at = len(line)
+            while at and line[at - 1][1] > t:
+                at -= 1
+            while at < len(line) and line[at][0] < t + d:
+                t = max(t, line[at][1])
+                at += 1
+            line.insert(at, (t, t + d))
+            start[k] = t
+        return start
+    every = range(len(calls))
+    behind = [{m: before[m][k] for m in after[k]} for k in every]
+    for turn in range(TURNS):
+        late = [0.0 if after[k] else calls[k]["late"] for k in every]
+        start = place(sorted(every, key=lambda k: (-start[k] - calls[k]["time"] - late[k], -k)), behind, late)
+        start = place(sorted(every, key=lambda k: (-start[k] - calls[k]["time"], k)), before, [0.0] * len(calls))
+    return sorted(every, key=lambda k: (start[k], k))
 
 
 def rank_program(g, core, T, topo):
@@ -116,7 +146,7 @@ def rank_program(g, core, T, topo):
     def dma(q, out, in_, reads, writes, size):
         sem = "dma%d" % len(dmas)
         dmas.append(size)
-        run(q, lambda e: e.dma_start(out, in_).then_inc(T.sem[sem], 16), reads, writes, 60.0, FAR + sum(dmas[-13:]) / RATE, (sem, 16))
+        run(q, lambda e: e.dma_start(out, in_).then_inc(T.sem[sem], 16), reads, writes, 60.0, FAR + (sum(dmas) if size else 0) / RATE, (sem, 16))
         return sem
 
     def v(name, lo=0, hi=None, step=1, tag=None, rows=ALL):
@@ -175,7 +205,7 @@ def rank_program(g, core, T, topo):
         run("p", lambda e: e.matmul(out[0], lhsT[0], rhs[0], start, stop), lhsT[1] + rhs[1], out[1], max(64, rhs[2]) * PE * (4 if rhs[3] == 4 else 1))
 
     def iota(out, pattern, base, cm):
-        run("g", lambda e: e.iota(out[0], pattern, base, cm), [], out[1], 130 + 2 * out[2] * CYCLE)
+        run("g", lambda e: e.iota(out[0], pattern, base, cm, allow_small_or_imprecise_dtypes=out[3] == 2), [], out[1], 130 + 2 * out[2] * CYCLE)
 
     def fill(out, src, pattern, base, cm, value, op=A.not_equal):
         run("g", lambda e: e.affine_select(out[0], src[0], pattern, op, value, base, cm), src[1], out[1], 170 + 2 * out[2] * CYCLE)
@@ -238,7 +268,7 @@ def rank_program(g, core, T, topo):
         if RELU:
             ms(v("P1", 128 * y, 128 * y + 32 * RELU), 0.0)
             S(blk("PX", y, 512 * RELU), ind(blk("P0", y), v("cBL", 0, 32 * RELU)), F.Copy)
-    ms(v("cAG"), 1.0 / 16)
+    ms(v("cAG", 0, 16 * PIECE), 1.0 / 16)
     ms(v("cAG", 0, 16 * PIECE, 16), -32768.0)
     for name, x in (("mIG", 2048.0), ("mI16", 16.0), ("mN16", -16.0), ("mN1", -1.0), ("mP", -32768.0), ("mI32", 32.0)):
         S(v(name), v("mI"), F.Copy, scale=x)
@@ -297,7 +327,7 @@ def rank_program(g, core, T, topo):
         ts(col(52 + e), v("cP"), 4.0, SPARE + 512.0 * e, A.mult, A.add)
         ts(blk("mRF", e, 8), v("cM", 0, 8), col(0), col(52 + e), A.is_equal, A.mult)
     ts(v("cK"), v("cJ"), col(1), -1.0, A.is_equal, A.add)
-    ms(v("cZ"), 0.0)
+    iota(v("cZ"), [[0, 128]], 0, 0)
     fill(v("cX"), v("cZ"), [[0, 2], [-32, 4], [0, 16]], -2, 1, 64.0)
     for k in range(16):
         fill(blk("mS", k), v("cX"), [[0, 8], [1, 16]], -k, 0, 0.0, A.is_equal)
@@ -308,7 +338,7 @@ def rank_program(g, core, T, topo):
     def codes(t, y):
         tb = blk("TB%d" % t, y)
         qf = also(blk("QF", y), "QF.0", "QF.1") if t == 0 else blk("QF", y)
-        turned = blk("bk7", 1)
+        turned = blk("bk%d" % (1 + 3 * y), 0)
         MM(turned, blk("mPT", t), tb)
         tt(qf, tb, turned, A.mult)
         ts(blk("FI", y), blk("QF", y), col(8 + t), BIG, A.add, A.min)
@@ -333,12 +363,10 @@ def rank_program(g, core, T, topo):
         for c0 in range(H * y, H * y + H, PIECE):
             r = v("R", 16 * c0, 16 * (c0 + PIECE))
             S(r, ind(U, v("OFF", c0, c0 + PIECE)), bias=col(41))
-            scan(v("KP", 16 * c0, 16 * (c0 + PIECE)), v("cAG"), r, A.add, A.max)
+            scan(v("KP", 16 * c0, 16 * (c0 + PIECE)), v("cAG", 0, 16 * PIECE), r, A.add, A.max)
         for i in range(16):
             MM(v("bk7", i, 128, 16), ri(i), v("mV"))
         scan(b("S2"), v("c1"), blk("bk7", 0), A.add, A.max)
-        if t + y in range(1, RO):
-            codes(t + y, 1 - y)
         cp(w("KV"), top("S2"))
         S(w("PV"), top("S2"), F.Relu, scale=-1024.0, bias=col(45))
         ts(w("AV"), w("KV"), 15, None, AND)
@@ -355,9 +383,9 @@ def rank_program(g, core, T, topo):
         for i in range(16):
             tt(v("M", lo + i, 2048 * y + 2048, 16, tag="%d.%d" % (y, i)), v("R", lo + i, 2048 * y + 2048, 16), v("bk0", 128 * y + 32 * RELU, 128 * y + 128), A.max)
         MM(key, kp, v("mI16"), False, False)
-        MM(key, b("WP"), v("mN16"), False, False)
         for i in range(16):
-            MM(key, also(v("M", 2048 * y + i, 2048 * y + 2048, 16), "M.%d.%d" % (y, i)), v("mIG"), False, i == 15)
+            MM(key, also(v("M", 2048 * y + i, 2048 * y + 2048, 16), "M.%d.%d" % (y, i)), v("mIG"), False, False)
+        MM(key, b("WP"), v("mN16"), False, True)
         k1 = top("S1")
         scan(b("S1"), v("c32"), key, A.add, A.max)
         tt(w("KS"), k1, w("AV"), A.max)
@@ -372,14 +400,22 @@ def rank_program(g, core, T, topo):
         x, x0, x1, pr = w("X"), v("X", 8 * y, 8 * y + 4), v("X", 8 * y + 4, 8 * y + 8), v("PR", 16 * y, 16 * y + 12)
         ts(blk("WN", 2 * y, 8), top("S3"), 4.0, 128.0 - 7.5 / 16, A.mult, A.add)
         ts(x, top("S3"), -KEEP, -33.0, A.add, A.max)
-        S(v("PR", 16 * y, 16 * y + 8), x, F.Square)
+        if "q" in ONV:
+            tt(v("PR", 16 * y, 16 * y + 8), x, x, A.mult)
+        else:
+            S(v("PR", 16 * y, 16 * y + 8), x, F.Square)
         tt(v("PR", 16 * y + 8, 16 * y + 12), x0, x1, A.mult)
-        S(ft("a", 2, 256), x, F.Copy)
-        S(ft("b", 3, 256), x, F.Copy)
-        S(ft("c", 254, 380), x0, F.Copy)
-        S(ft("d", 255, 380), x1, F.Copy)
+        for tag, lo, hi, a in (("a", 2, 256, x), ("b", 3, 256, x), ("c", 254, 380, x0), ("d", 255, 380, x1)):
+            if tag in ONV:
+                cp(ft(tag, lo, hi), a)
+            else:
+                S(ft(tag, lo, hi), a, F.Copy)
         tt(ft("e", 134, 256), x1, x0, A.subtract)
-        cp(ft("f", 0, 384), pr)
+        if "p" in ONV:
+            tt(ft("f", 0, 256), x, x, A.mult)
+            tt(ft("f", 256, 384), x0, x1, A.mult)
+        else:
+            cp(ft("f", 0, 384), pr)
         tt(ft("g", 1, 384), pr, ft("f", 0, 384), A.subtract)
         ts(w("H2"), w("KS"), 1, 0xF0, SHR, AND)
         S(ft("h", 7, 256), w("H2"), F.Copy, scale=1.0 / 16)
@@ -388,7 +424,10 @@ def rank_program(g, core, T, topo):
         MM(blk(by, 0), also(v("FT", 384 * y + 252, 384 * y + 380), *rows), v("mI"))
         for e in range(2):
             MM(v(by, 128 + e, 384, 2), also(blk("FT", 3 * y + e), *rows), v("mI"))
-        S(v("FA", 400 * y + 3, 400 * y + 387), v(by, 0, 384), F.Copy)
+        if "A" in ONV:
+            cp(v("FA", 400 * y + 3, 400 * y + 387), v(by, 0, 384))
+        else:
+            S(v("FA", 400 * y + 3, 400 * y + 387), v(by, 0, 384), F.Copy)
         tt(w("G2"), w("KS"), w("L2"), A.add)
         ts(w("GM"), w("G2"), 11, 15, SHR, AND)
         ts(w("PN"), k1, 0.0, BIG, A.is_lt, A.mult)
@@ -402,7 +441,10 @@ def rank_program(g, core, T, topo):
             S(v("LR", rows=LOW), v("THR", rows=LOW), bias=v("MC", 1, 2, rows=LOW))
             S(v("MC", 2, 3), v("MC", 1, 2), scale=2048.0)
             S(v("L2"), v("TH2"), bias=v("MC", 2, 3))
-        S(b("VB"), ind(blk("WN", y, 16), blk("cBR", t, 8)), scale=1.0 / 32)
+        if "B" in ONV:
+            ts(b("VB"), ind(blk("WN", y, 16), blk("cBR", t, 8)), 1.0 / 32, None, A.mult)
+        else:
+            S(b("VB"), ind(blk("WN", y, 16), blk("cBR", t, 8)), scale=1.0 / 32)
         MM(blk(bz, 0), blk("mCR", t), blk("mON", 0), True, False)
         MM(blk(bz, 0), blk("mFN", t), b("ZN"), False, False)
         MM(blk(bz, 0), b("VB"), v("mI"), False, True)
@@ -425,7 +467,7 @@ def rank_program(g, core, T, topo):
                 MM(also(v(bank, c0, c0 + n), tile), fa(131 + 128 * be, 259 + 128 * be, rows=rows), fa(0, n, rows=rows), True, False)
                 MM(v(bank, c0 + n - 64, c0 + n), v("mI"), v("mTR"), False, True)
                 todo.append((gr % 2, v("RD", 8 * y + 4 * be + gr, 8 * y + 4 * be + gr + 1), v(bank, c0, c0 + n)))
-        for side, out1, a in sorted(todo, key=lambda x: x[0]):
+        for side, out1, a in sorted(todo, key=lambda x: -x[0]):
             least(out1, a)
         l16 = lambda name: blk(name, y, 16)
         for k in range(16):
@@ -441,6 +483,8 @@ def rank_program(g, core, T, topo):
         tt(l16("OL"), l16("OL0"), v(bz, 0, 16), A.max)
         run("v", lambda e: e.tensor_tensor(U[0].indirect(l16("OL")[0]), blk("UG", y, C)[0], blk("W1", y, C)[0], A.mult),
             l16("OL")[1] + blk("UG", y, C)[1] + blk("W1", y, C)[1], U[1], 50 + C * SCATTER * CYCLE)
+        if more:
+            codes(t + 1, y)
 
     codes(0, 0)
     codes(0, 1)

@@ -11,39 +11,41 @@ SPARE = 4100
 NONE = 16384.0
 BIG = 2.0 ** 20
 KEEP = 2.0 ** 17
-RELU = 2
+PLAN = "SNII"
 PIECE = 32
 LEAD, SHORT = 2000.0, 3.0
-ONV = "qA"
+ONV = "PTWCF"
 TURNS = 1
+TURN = (0, 1, 0, 1)
+BOTH, SFIX, FIRST = 1.0, 0.0, 2000.0
 AHEAD, FIT = 0.0, 60.0
 RHO = [(5 * t) % 16 for t in range(RO)]
-CYCLE, PE, GATHER, SCATTER, HOP, FAR, RATE = 0.83, 0.42, 1.3, 3.0, 240.0, 1500.0, 300.0
+CYCLE, PE, GATHER, SCATTER, HOP, FAR, RATE = 0.83, 0.42, 1.4, 3.8, 200.0, 1500.0, 300.0
 
 SCRATCH = {}
 for _n, _w, _d in [
     ("U0", UW, "bfloat16"), ("U1", UW, "bfloat16"), ("R", W, "bfloat16"), ("M", W, "bfloat16"), ("KP", W, "float16"),
-    ("P", 2 * C, "bfloat16"), ("P1", C, "bfloat16"), ("TI", 2 * C, "int32"), ("QF", C, "float32"), ("FI", C, "int32"), ("XI", C, "int32"),
+    ("P", C, "bfloat16"), ("P1", C, "bfloat16"), ("TI", C, "int32"), ("QF", C, "float32"), ("FI", C, "int32"), ("XI", C, "int32"),
     ("OFF", C, "uint16"), ("CM", C, "float16"), ("ZN", C, "float16"), ("TR", C, "float16"), ("WP", C, "float16"),
-    ("S1", C, "float32"), ("S2", C, "float32"), ("S3", C, "float32"), ("ST", C, "bfloat16"), ("VB", C, "float16"),
+    ("S1", 272, "int32"), ("S2", C, "int32"), ("S3", C, "float32"), ("ST", C, "bfloat16"), ("VB", C, "float16"),
     ("W1", 2 * C, "bfloat16"), ("UG", 2 * C, "bfloat16"), ("FE", C, "bfloat16"),
     ("FT", 768, "float16"), ("FA", 800, "float16"),
-    ("KV", 16, "int32"), ("AV", 16, "int32"), ("KS", 16, "int32"), ("AG", 16, "int32"), ("H2", 16, "int32"), ("G2", 16, "int32"), ("GM", 16, "int32"),
-    ("ZZ", 16, "float32"), ("PX", W, "bfloat16"), ("P0", C, "bfloat16"), ("PU", 16, "float32"), ("PN", 16, "bfloat16"), ("PV", 16, "float32"), ("P2", 16, "bfloat16"),
+    ("AV", 16, "int32"), ("AB", 16, "bfloat16"), ("AG", 16, "int32"), ("H2", 16, "int32"), ("GM", 16, "int32"),
+    ("PX", W, "bfloat16"), ("P0", C, "bfloat16"), ("PU", 16, "bfloat16"), ("RN", C * RO, "bfloat16"), ("PV", 16, "bfloat16"),
     ("WN", 32, "int32"), ("X", 16, "float32"), ("PR", 32, "float32"), ("RD", 16, "float32"),
     ("OL0", 32, "uint16"), ("OL", 32, "uint16"),
-    ("LR", C, "float16"), ("L2", 16, "float32"), ("THR", C, "float32"), ("TH2", 16, "float32"), ("THI", 1, "int32"), ("THF", 1, "float32"), ("TH8", C, "float32"),
+    ("LR", 272, "float16"), ("L2", 32, "float32"), ("TH2", 32, "float32"), ("THI", 1, "int32"), ("THF", 1, "float32"), ("TH8", 16, "float32"),
     ("MC", 4, "float32"), ("MW", 1, "bfloat16"), ("MJ", 16, "float32"),
     ("OUTT", C, "float32"), ("OUTC", C, "float32"), ("TS", C * RO, "float16"),
-    ("cM", 128, "int32"), ("cD", 128, "int32"), ("cJ", 128, "int32"), ("cH", 128, "int32"), ("cT", 128, "int32"), ("cG", 128, "int32"), ("cP", 1, "int32"), ("cI", 8, "int32"),
+    ("cM", 128, "int32"), ("cD", 128, "int32"), ("cJ", 128, "int32"), ("cH", 128, "int32"), ("cT", 128, "int32"), ("cG", 16, "int32"), ("cP", 1, "int32"), ("cI", 8, "int32"),
     ("cF", 64, "float32"), ("cV", 16, "int32"), ("cW", 16, "int32"), ("cA", 128, "bfloat16"), ("cB", 128, "bfloat16"), ("cC", 128, "bfloat16"), ("cE", 128, "bfloat16"),
     ("cDD", 128, "bfloat16"), ("cBM", 128, "bfloat16"),
-    ("mI", 128, "bfloat16"), ("mIG", 128, "bfloat16"), ("mI16", 128, "bfloat16"), ("mN16", 128, "bfloat16"), ("mN1", 128, "bfloat16"), ("mP", 128, "bfloat16"),
-    ("mI32", 128, "bfloat16"), ("mH", 128, "bfloat16"),
+    ("mI", 128, "bfloat16"), ("mI17", 136, "bfloat16"), ("mIG", 136, "bfloat16"), ("mI16", 136, "bfloat16"), ("mN16", 136, "bfloat16"), ("mN1", 128, "bfloat16"), ("mP", 136, "bfloat16"),
+    ("mI32", 128, "bfloat16"), ("mIK", 128, "bfloat16"), ("mIN", 128, "bfloat16"), ("mH", 128, "bfloat16"),
     ("mPT", 128 * RO, "bfloat16"), ("mFN", 128 * RO, "bfloat16"), ("mF0", 128, "bfloat16"), ("mCR", 128 * RO, "float16"), ("mC0", 128, "float16"),
     ("mD", 128, "bfloat16"), ("mV", 8, "bfloat16"), ("mL", 128, "float16"), ("mON", C, "bfloat16"), ("mOF", 128, "float32"),
-    ("mRF", 16, "float16"), ("mTR", 64, "bfloat16"), ("mS", 2048, "bfloat16"), ("mW", 128, "bfloat16"), ("cX", 128, "bfloat16"), ("cY", 128, "bfloat16"), ("cZ", 128, "bfloat16"),
-    ("cAG", 1024, "bfloat16"), ("c32", 128, "bfloat16"), ("c1", 128, "bfloat16"), ("cPA", 128, "bfloat16"), ("cK", 128, "bfloat16"),
+    ("mRF", 16, "float16"), ("mTR", 64, "bfloat16"), ("mS", 2048, "bfloat16"), ("mW", 128, "bfloat16"), ("cX", 128, "bfloat16"), ("cY", 128, "bfloat16"), ("cZ", 136, "bfloat16"),
+    ("cAG", 1024, "bfloat16"), ("c32", 136, "bfloat16"), ("c1", 128, "bfloat16"), ("cPA", 128, "bfloat16"), ("cK", 128, "bfloat16"),
     ("cBL", 128, "uint16"), ("cBR", 8 * RO, "uint16"),
 ]:
     SCRATCH[_n] = ("sbuf", [128, _w], _d)
@@ -51,7 +53,7 @@ for _t in range(RO + 1):
     SCRATCH["TB%d" % _t] = ("sbuf", [128, C], "float16")
 for _b in range(8):
     SCRATCH["bk%d" % _b] = ("psum", [128, 512], "float32")
-DMAS = 17
+DMAS = 11
 SEMAPHORES = ["v", "s", "p", "g", "snd"] + ["arr%d_%d" % (t, e) for t in range(1, RO + 1) for e in range(2)] + ["dma%d" % k for k in range(DMAS)]
 AND, SHR = A.bitwise_and, A.arith_shift_right
 ALL, LOW, HIGH = slice(0, 128), slice(0, 64), slice(64, 128)
@@ -80,6 +82,8 @@ def arrange(calls):
                         keep.append(e)
                 keep.append((k, lo, hi, wr))
                 touch[b] = keep
+        if c["q"] == "y":
+            pre.update({j: pre.get(j, 0.0) for j in range(k) if calls[j]["q"] == "y"})
         before.append(pre)
     way = [c["time"] + c["late"] + (LEAD if c["writes"][0][0] in ("yc0", "yt0") else 0.0) for c in calls]
     after, left = [[] for c in calls], [len(pre) for pre in before]
@@ -155,7 +159,7 @@ def rank_program(g, core, T, topo):
         n = len(range(lo, hi, step))
         if name.startswith("bk"):
             return T[name][rows, lo:hi:step], [name], n, 0, False
-        return T[name][rows, lo:hi:step], [(name if tag is None else name + "." + str(tag), lo, hi)], n, 2 if "16" in SCRATCH[name][2] else 4, False
+        return T[name][rows, lo:hi:step], [(name if tag is None else name + "." + str(tag), lo, hi)], n, 2 if "16" in SCRATCH[name][2] else 4, False, rows
 
     def ind(win, off):
         return win[0].indirect(off[0]), win[1] + off[1], 16 * off[2], win[3], True
@@ -181,7 +185,7 @@ def rank_program(g, core, T, topo):
         run("v", lambda e: e.tensor_scalar(out[0], in0[0], s1[0], s2[0], op0, *more), in0[1] + s1[1] + s2[1], out[1], vtime(out, [in0]))
 
     def tt(out, a, b, op):
-        run("v", lambda e: e.tensor_tensor(out[0], a[0], b[0], op), a[1] + b[1], out[1], vtime(out, [a, b], 2.0 if a[3] and b[3] else 1.0))
+        run("v", lambda e: e.tensor_tensor(out[0], a[0], b[0], op), a[1] + b[1], out[1], vtime(out, [a, b], (BOTH if a[3] == b[3] == out[3] == 2 else 2.0) if a[3] and b[3] else 1.0))
 
     def cp(out, a):
         run("v", lambda e: e.tensor_copy(out[0], a[0]), a[1], out[1], vtime(out, [a]))
@@ -199,7 +203,10 @@ def rank_program(g, core, T, topo):
         scale, bias = sc(scale), sc(bias)
         k = {} if accum is None else {"accum_out": accum[0]}
         run("s", lambda e: e.activation(out[0], in_[0], func, bias=bias[0], scale=scale[0], **k),
-            in_[1] + scale[1] + bias[1], out[1] + ([] if accum is None else accum[1]), 65 + out[2] * GATHER * CYCLE if in_[4] else max(64, out[2]) * CYCLE)
+            in_[1] + scale[1] + bias[1], out[1] + ([] if accum is None else accum[1]), 65 + out[2] * GATHER * CYCLE if in_[4] else SFIX + max(64, out[2]) * CYCLE)
+
+    def put(out, x):
+        S(out, v("cM", 0, out[2], rows=out[5]), scale=0.0, bias=x)
 
     def MM(out, lhsT, rhs, start=True, stop=True):
         run("p", lambda e: e.matmul(out[0], lhsT[0], rhs[0], start, stop), lhsT[1] + rhs[1], out[1], max(64, rhs[2]) * PE * (4 if rhs[3] == 4 else 1))
@@ -216,12 +223,10 @@ def rank_program(g, core, T, topo):
     def blk(name, k, n=128, rows=ALL, tag=None):
         return v(name, n * k, n * k + n, rows=rows, tag=tag)
 
+    dma("y", T.TI[:], T.tst[:], [], ["TI"], 131072)
+    dma("s", T.P[:], T.pr[:], [], ["P"], 65536)
     for y in range(2):
-        for e in range(2):
-            dma("y", T.TI[HALF[e], C * y:C * y + C], T.tst[HALF[y], :], [], [("TI.%d" % e, C * y, C * y + C)], 65536)
-        for e in range(2):
-            dma("s", T.P[HALF[e], C * y:C * y + C], T.pr[HALF[y], :], [], [("P.%d" % e, C * y, C * y + C)], 32768)
-        if y == 0:
+        if y:
             dma("s", T.THI[0:8, :], T.th[:], [], ["THI"], 32)
         for e in range(2):
             dma("y", T["U%d" % y][HALF[e], 0:W], T.cov[HALF[y], :], [], ["U%d.%d" % (y, e)], 524288)
@@ -237,7 +242,6 @@ def rank_program(g, core, T, topo):
     ts(v("cH"), v("cM"), 4, None, SHR)
     ts(v("cT"), v("cD"), 15, None, AND)
     ts(v("cJ"), v("cM"), 15, None, AND)
-    ts(v("cG"), v("cM"), 4, 3, SHR, AND)
     cp(v("cF", 0, 6), v("cI", 0, 6))
     ts(v("cB"), v("cT"), 1.0, None, A.mult)
     ts(v("cBM"), v("cH"), col(0), None, A.is_equal)
@@ -253,151 +257,175 @@ def rank_program(g, core, T, topo):
     ts(v("cF", 8, 16), v("cW", 0, 8), -0.5, None, A.add)
     eqm(v("mI"), 0, 1)
     cp(v("cBL"), v("cM"))
-    for k, x in ((40, -8.0), (41, -128.0), (42, 1536.0), (45, -1024.0 * 32881), (46, 192.0 - 127.5 / 256), (47, 47104.0)):
-        ms(col(k), x)
+    S(v("VB"), v("TI"), scale=1.0 / 32, bias=1.0 / 64)
+    S(v("ZN"), v("TI"), F.Relu, scale=NONE - 8, bias=-255.0 * (NONE - 8))
+    for names, bank in ((("VB", "ZN"), "bk2"), (("P",), "bk3")):
+        for y in range(2):
+            for e in range(2):
+                for name in names:
+                    MM(blk(bank, y, rows=HALF[e]), blk("mI", y, 64), v(name, e, C, 2), name == names[0], name == names[-1])
+    cp(v("TB0"), v("bk2", 0, C))
+    S(v("P0"), v("bk3", 0, C), bias=-128.0)
+    n = 32 * PLAN.count("S")
     for y in range(2):
         ms(v("U%d" % y, W, UW), -1.0)
-        for e in range(2):
-            ti = v("TI", C * y + e, C * y + C, 2, tag=e, rows=HALF[e])
-            ts(blk("QF", y, rows=HALF[e], tag=e), ti, 1.0 / 32, 1.0 / 64, A.mult, A.add)
-            ts(blk("ZN", y, rows=HALF[e], tag=e), ti, 256.0, NONE, A.is_ge, A.mult)
-            ts(blk("bk0", y, rows=HALF[e]), v("P", C * y + e, C * y + C, 2, tag=e, rows=HALF[e]), -128.0, None, A.add)
-        tt(blk("TB0", y), also(blk("QF", y), "QF.0", "QF.1"), also(blk("ZN", y), "ZN.0", "ZN.1"), A.max)
-        cp(blk("P0", y), blk("bk0", y))
-        cp(v("P1", 128 * y + 32 * RELU, 128 * y + 128), v("bk0", 128 * y + 32 * RELU, 128 * y + 128))
-        if RELU:
-            ms(v("P1", 128 * y, 128 * y + 32 * RELU), 0.0)
-            S(blk("PX", y, 512 * RELU), ind(blk("P0", y), v("cBL", 0, 32 * RELU)), F.Copy)
+        if n:
+            put(v("P1", H * y, H * y + n), 0.0)
+        S(v("P1", H * y + n, H * y + H), v("P0", H * y + n, H * y + H), F.Copy)
+        n2 = 32 * (4 - PLAN.count("I"))
+        S(v("PX", 2048 * y, 2048 * y + 16 * n2), ind(blk("P0", y), v("cBL", 0, n2)), F.Copy)
     ms(v("cAG", 0, 16 * PIECE), 1.0 / 16)
-    ms(v("cAG", 0, 16 * PIECE, 16), -32768.0)
-    for name, x in (("mIG", 2048.0), ("mI16", 16.0), ("mN16", -16.0), ("mN1", -1.0), ("mP", -32768.0), ("mI32", 32.0)):
+    put(v("cAG", 0, 16 * PIECE, 16), -32768.0)
+    iota(v("cZ"), [[0, 136]], 0, 0)
+    fill(v("mI17"), v("cZ"), [[-16, 8], [-1, 17]], 1, 1, 1.0)
+    fill(v("mI17"), v("mI17"), [[0, 8], [1, 17]], 0, 0, 0.0)
+    for name, x in (("mIG", 2048.0), ("mI16", 16.0), ("mN16", -16.0), ("mP", -32768.0)):
+        S(v(name), v("mI17"), F.Copy, scale=x)
+    for name, x in (("mN1", -1.0), ("mI32", 32.0), ("mIK", KEEP), ("mIN", NONE)):
         S(v(name), v("mI"), F.Copy, scale=x)
-    ms(v("mH"), -1.0 / 256)
+    put(v("mH"), -1.0 / 256)
     eqm(v("cC"), 15, -1.0 / 64)
     fill(v("cC"), v("cC"), [[0, 8], [1, 16]], -15, 0, 0.0)
     eqm(v("cE"), 0, 1.0 / 64)
     tt(v("mD"), v("cE"), v("cC"), A.add)
     ts(v("mV"), v("cM", 0, 8), col(0), 16.0, A.is_equal, A.mult)
-    for name, x in (("c32", 32.0), ("c1", 1.0)):
+    for name, x, n in (("c32", 32.0, 17), ("c1", 1.0, 16)):
         ms(v(name), x)
-        ms(v(name, 0, 128, 16), -2.0 ** 26)
-    ts(v("cPA"), v("cJ"), -1.0, 15.0, A.mult, A.add)
+        put(v(name, 0, 8 * n, n), -2.0 ** 26)
+    S(v("cPA"), v("cJ"), scale=-1.0, bias=15.0)
     top8 = slice(0, 8)
-    ms(v("mOF", rows=slice(0, 32)), 1.0)
+    put(v("mOF", rows=slice(0, 32)), 1.0)
     cp(v("THF", rows=top8), v("THI", rows=top8))
-    ts(col(7, top8), col(1, top8), -4.0, None, A.add)
-    for y in range(2):
-        ts(blk("TH8", y, rows=top8), v("cG", rows=top8), col(7 if y else 1, top8), v("THF", rows=top8), A.is_equal, A.mult)
-    MM(v("bk7", 0, C), v("mOF", rows=top8), v("TH8", rows=top8))
-    S(v("THR"), v("bk7", 0, C), bias=col(47))
-    ms(v("LR", rows=HIGH, tag="c"), 64.0)
-    ts(v("LR", rows=LOW), v("THR", rows=LOW), -49152.0, None, A.add)
-    ts(v("TH2"), v("THR", 0, C, 16), 2048.0, 2048.0, A.add, A.mult)
-    ts(v("L2"), v("TH2"), -49152.0 * 2048, None, A.add)
-    ms(v("mL", rows=LOW, tag=0), -32.0)
-    ms(v("mL", rows=slice(64, 96), tag=1), -2048.0)
-    ms(v("mL", rows=slice(96, 128), tag=2), 25616.0 / 2048)
+    iota(v("cG"), [[4, 2], [0, 2], [1, 4]], 0, 0)
+    ts(v("TH8", rows=top8), v("cG", rows=top8), col(1, top8), v("THF", rows=top8), A.is_equal, A.mult)
+    MM(v("bk7", 0, 16), v("mOF", rows=top8), v("TH8", rows=top8))
+    quarter = [slice(32 * k, 32 * k + 32) for k in range(4)]
+    ms(v("LR", rows=slice(0, 96), tag=0), 0.0)
+    S(v("LR", 0, 272, 17, rows=quarter[0], tag=0), v("bk7", 0, 16, rows=quarter[0]), bias=-2048.0)
+    for name in ("TH2", "L2"):
+        S(v(name, 0, 16), v("bk7", 0, 16), F.Copy, scale=2048.0)
+        S(v(name, 16, 32), v("bk7", 0, 16), scale=2048.0, bias=-512.0)
+    ms(v("LR", rows=quarter[3], tag=3), 768.5)
+    for k, (first, left) in enumerate(((None, 64.0), (64.0, 0.0), (64.0, 2048.0), (-48.0, 1.0))):
+        if k:
+            put(also(v("LR", 0, 272, 17, rows=quarter[k], tag=k), "LR.0"), first)
+        ms(v("mL", rows=quarter[k], tag=k), left)
     ts(v("cF", 16, 24), v("cW", 8, 16), col(1), 8.0, A.is_equal, A.mult)
     ts(v("cF", 24, 32), v("cW", 8, 16), col(1), None, A.not_equal)
     ts(v("cF", 32, 40), v("cW", 8, 16), col(1), NONE, A.is_equal, A.mult)
-    ts(col(49), col(1), -15.0, None, A.add)
-    tt(col(48), col(49), col(49), A.mult)
+    S(col(48), col(1), F.Square, bias=-15.0)
     ts(v("cA"), v("cD"), 256.0, 2.0, A.is_gt, A.mult)
     tt(v("cB"), v("cA"), v("cBM"), A.mult)
     eqm(v("cE"), 0, 2)
     tt(v("mF0"), v("cB"), v("cE"), A.subtract)
-    ms(v("mC0", rows=LOW, tag=0), 511.75)
-    ms(v("mC0", rows=HIGH, tag=1), 1.0 / 4096)
+    put(v("mC0", rows=LOW, tag=0), 511.75)
+    put(v("mC0", rows=HIGH, tag=1), 1.0 / 4096)
     for t in range(RO):
         eqm(blk("mPT", t), (-(1 + t)) % 16, 256)
+        iota(blk("RN", t, C), [[0, C]], 0, 0)
         ts(blk("cBR", t, 8), v("cM", 0, 8), col(16 + t), None, A.add)
         fill(blk("mFN", t), v("mF0"), [[0, 8], [1, 16]], -RHO[t], 0, 0.0)
         fill(blk("mCR", t), also(v("mC0", tag=0), "mC0.1"), [[0, 8], [1, 16]], -RHO[t], 0, (7.5 + 1.0 / 64) / 128)
-    ms(v("FT"), 0.0)
+    ms(also(v("FT"), *["FT.%d%s" % (y, k) for y in range(2) for k in "abcdefghi"]), 0.0)
     ts(col(50), col(2), 2.0, None, A.is_equal)
     ts(col(51), col(2), 4.0, None, A.is_equal)
+    for lo, x in ((4, -1.0), (5, -1.0), (28, -1.0), (29, -1.0), (6, 1.0)):
+        put(also(v("FT", lo, 768, 32), "FT.0e", "FT.1e"), x)
     for y in range(2):
-        for lo, hi, x in ((4, 256, -1.0), (5, 256, -1.0), (252, 380, -1.0), (253, 380, -1.0), (6, 128, 1.0)):
-            ms(also(v("FT", 384 * y + lo, 384 * y + hi, 32, tag="c%d" % lo), "FT"), x)
         ts(v("FA", 400 * y, 400 * y + 1), col(2), 6.0, None, A.is_equal)
         for k, x in ((1, 32.0), (2, -33.0)):
-            ts(v("FA", 400 * y + k, 400 * y + k + 1), col(51), x, col(50), A.mult, A.add)
+            S(v("FA", 400 * y + k, 400 * y + k + 1), col(51), scale=x, bias=col(50))
     ts(v("mTR"), v("cM", 0, 64), col(5), 16384.0, A.is_ge, A.mult)
     for e in range(2):
         ts(col(52 + e), v("cP"), 4.0, SPARE + 512.0 * e, A.mult, A.add)
         ts(blk("mRF", e, 8), v("cM", 0, 8), col(0), col(52 + e), A.is_equal, A.mult)
     ts(v("cK"), v("cJ"), col(1), -1.0, A.is_equal, A.add)
-    iota(v("cZ"), [[0, 128]], 0, 0)
-    fill(v("cX"), v("cZ"), [[0, 2], [-32, 4], [0, 16]], -2, 1, 64.0)
+    fill(v("cX"), v("cZ", 0, 128), [[0, 2], [-32, 4], [0, 16]], -2, 1, 64.0)
     for k in range(16):
         fill(blk("mS", k), v("cX"), [[0, 8], [1, 16]], -k, 0, 0.0, A.is_equal)
-    ts(v("cY"), v("cPA"), -2.0, None, A.mult)
+    S(v("cY"), v("cPA"), F.Copy, scale=-2.0)
     fill(v("mW"), v("cY"), [[0, 2], [-32, 4], [0, 16]], -7, 1, 0.0, A.is_equal)
     fill(v("mW"), v("mW"), [[0, 2], [-32, 4], [0, 16]], -8, 1, 1.0)
 
     def codes(t, y):
         tb = blk("TB%d" % t, y)
-        qf = also(blk("QF", y), "QF.0", "QF.1") if t == 0 else blk("QF", y)
-        turned = blk("bk%d" % (1 + 3 * y), 0)
+        qf = blk("QF", y)
+        turned = blk("bk%d" % (4 * y), 0)
         MM(turned, blk("mPT", t), tb)
         tt(qf, tb, turned, A.mult)
         ts(blk("FI", y), blk("QF", y), col(8 + t), BIG, A.add, A.min)
         ts(blk("XI", y), blk("FI", y), 0x7FFF8FFF, None, AND)
         ts(blk("OFF", y), blk("XI", y), float(VOID), None, A.min)
-        ts(blk("CM", y), blk("OFF", y), -2048.0, None, A.add)
-        S(also(blk("ZN", y), "ZN.0", "ZN.1") if t == 0 else blk("ZN", y), tb, F.Relu, bias=col(40))
-        S(blk("TR", y), tb, scale=col(24 + t), bias=col(32 + t))
+        if "C" in ONV:
+            ts(blk("CM", y), blk("OFF", y), -2048.0, None, A.add)
+        else:
+            S(blk("CM", y), blk("OFF", y), bias=-2048.0)
+        if "Z" in ONV:
+            ts(blk("ZN", y), tb, -8.0, 0.0, A.add, A.max)
+        else:
+            S(blk("ZN", y), tb, F.Relu, bias=-8.0)
+        if "T" in ONV:
+            ts(blk("TR", y), tb, col(32 + t), None, A.max)
+        else:
+            S(blk("TR", y), tb, scale=col(24 + t), bias=col(32 + t))
 
     sent = [0]
 
     def visit(t, y):
         more = t < RO - 1
-        bx, by, bz = ("bk%d" % (k + 3 * y) for k in (1, 2, 3))
+        bx, by, bz, bw = ("bk%d" % (k + 4 * y) for k in range(4))
         U = also(v("U%d" % y), "U%d.0" % y, "U%d.1" % y)
         w = lambda name: blk(name, y, 8)
         b = lambda name: blk(name, y)
         top = lambda name: v(name, 128 * y + 15, 128 * y + 128, 16)
         mi = lambda i, n=1: v("M", 2048 * y + 128 * i, 2048 * y + 128 * (i + n))
         ri = lambda i: v("R", 2048 * y + i, 2048 * y + 2048, 16)
-        key = blk(bx, 2)
+        key = v(bx, 256, 392)
         for c0 in range(H * y, H * y + H, PIECE):
             r = v("R", 16 * c0, 16 * (c0 + PIECE))
-            S(r, ind(U, v("OFF", c0, c0 + PIECE)), bias=col(41))
+            S(r, ind(U, v("OFF", c0, c0 + PIECE)), bias=-128.0)
             scan(v("KP", 16 * c0, 16 * (c0 + PIECE)), v("cAG", 0, 16 * PIECE), r, A.add, A.max)
         for i in range(16):
-            MM(v("bk7", i, 128, 16), ri(i), v("mV"))
-        scan(b("S2"), v("c1"), blk("bk7", 0), A.add, A.max)
-        cp(w("KV"), top("S2"))
-        S(w("PV"), top("S2"), F.Relu, scale=-1024.0, bias=col(45))
-        ts(w("AV"), w("KV"), 15, None, AND)
+            MM(v(bz, i, 128, 16), ri(i), v("mV"))
+        scan(b("S2"), v("c1"), blk(bz, 0), A.add, A.max)
+        S(w("PV"), top("S2"), F.Relu, scale=-4.0, bias=-4.0 * 32881)
+        ts(w("AV"), top("S2"), 15, None, AND)
+        S(w("AB"), w("AV"), F.Copy)
         kp = v("KP", 2048 * y + 15, 2048 * y + 2048, 16)
-        S(b("WP"), kp, bias=col(42))
+        if "W" in ONV:
+            ts(b("WP"), kp, 1536.0, None, A.add)
+        else:
+            S(b("WP"), kp, bias=1536.0)
         MM(key, b("P1"), v("mP"), True, False)
-        MM(key, also(v("mL", tag=0), "mL.1", "mL.2"), also(b("LR"), "LR.c"), False, False)
-        for k in range(RELU):
-            bank = (by, bz)[k % 2]
-            MM(v(bank), v("mI"), blk("R", 4 * y + k, 512), True, False)
-            MM(v(bank), v("mN1"), blk("PX", RELU * y + k, 512), False, True)
-            S(blk("M", 4 * y + k, 512), v(bank), F.Relu)
-        lo = 2048 * y + 512 * RELU
-        for i in range(16):
-            tt(v("M", lo + i, 2048 * y + 2048, 16, tag="%d.%d" % (y, i)), v("R", lo + i, 2048 * y + 2048, 16), v("bk0", 128 * y + 32 * RELU, 128 * y + 128), A.max)
+        MM(key, also(v("mL", tag=0), "mL.1", "mL.2", "mL.3"), also(blk("LR", y, 136, tag=0), "LR.1", "LR.2", "LR.3"), False, False)
+        for k, how in enumerate(PLAN):
+            if how == "S":
+                bank = (by, bw)[k % 2]
+                MM(v(bank), v("mI"), blk("R", 4 * y + k, 512), True, False)
+                MM(v(bank), v("mN1"), blk("PX", 4 * y + k, 512), False, True)
+                S(blk("M", 4 * y + k, 512), v(bank), F.Relu)
+            elif how == "N":
+                tt(blk("M", 4 * y + k, 512), blk("R", 4 * y + k, 512), blk("PX", 4 * y + k, 512), A.max)
+        lo = 32 * (4 - PLAN.count("I"))
+        for i in range(16 if lo < H else 0):
+            tt(v("M", 2048 * y + 16 * lo + i, 2048 * y + 2048, 16, tag="%d.%d" % (y, i)), v("R", 2048 * y + 16 * lo + i, 2048 * y + 2048, 16),
+               v("P0", 128 * y + lo, 128 * y + 128), A.max)
         MM(key, kp, v("mI16"), False, False)
         for i in range(16):
             MM(key, also(v("M", 2048 * y + i, 2048 * y + 2048, 16), "M.%d.%d" % (y, i)), v("mIG"), False, False)
+        MM(v(bx, 256, 392, 17), v("mI"), w("PV"), False, False)
+        MM(v(bx, 256, 392, 17), v("mI"), w("AB"), False, False)
         MM(key, b("WP"), v("mN16"), False, True)
-        k1 = top("S1")
-        scan(b("S1"), v("c32"), key, A.add, A.max)
-        tt(w("KS"), k1, w("AV"), A.max)
-        ts(w("PU"), k1, 0.0, KEEP, A.is_ge, A.mult)
-        ts(w("AG"), w("KS"), 15, None, AND)
-        tt(w("P2"), w("PU"), w("PV"), A.max)
+        k1 = v("S1", 136 * y + 16, 136 * y + 136, 17)
+        scan(blk("S1", y, 136), v("c32"), key, A.add, A.max)
+        ts(w("AG"), k1, 15, None, AND)
+        tt(w("PU"), k1, blk("L2", 2 + y, 8), A.is_ge)
         MM(blk(bx, 0), b("CM"), v("mD"), True, False)
-        MM(v(bx, 15, 128, 16), v("mI"), w("P2"), False, True)
+        MM(v(bx, 15, 128, 16), v("mIK"), w("PU"), False, True)
         tt(b("ST"), ind(w("AG"), v("cBL", 0, 8)), v("cPA"), A.is_gt)
         scan(b("S3"), b("ST"), blk(bx, 0), A.mult, A.add)
         ft = lambda tag, lo, hi: v("FT", 384 * y + lo, 384 * y + hi, 32, tag="%d%s" % (y, tag))
-        x, x0, x1, pr = w("X"), v("X", 8 * y, 8 * y + 4), v("X", 8 * y + 4, 8 * y + 8), v("PR", 16 * y, 16 * y + 12)
+        x, x0, x1, pr = ft("a", 2, 256), ft("a", 2, 128), ft("a", 130, 256), v("PR", 16 * y, 16 * y + 12)
         ts(blk("WN", 2 * y, 8), top("S3"), 4.0, 128.0 - 7.5 / 16, A.mult, A.add)
         ts(x, top("S3"), -KEEP, -33.0, A.add, A.max)
         if "q" in ONV:
@@ -405,7 +433,7 @@ def rank_program(g, core, T, topo):
         else:
             S(v("PR", 16 * y, 16 * y + 8), x, F.Square)
         tt(v("PR", 16 * y + 8, 16 * y + 12), x0, x1, A.mult)
-        for tag, lo, hi, a in (("a", 2, 256, x), ("b", 3, 256, x), ("c", 254, 380, x0), ("d", 255, 380, x1)):
+        for tag, lo, hi, a in (("b", 3, 256, x), ("c", 254, 380, x0), ("d", 255, 380, x1)):
             if tag in ONV:
                 cp(ft(tag, lo, hi), a)
             else:
@@ -414,31 +442,38 @@ def rank_program(g, core, T, topo):
         if "p" in ONV:
             tt(ft("f", 0, 256), x, x, A.mult)
             tt(ft("f", 256, 384), x0, x1, A.mult)
+        elif "P" in ONV:
+            S(ft("f", 0, 256), x, F.Square)
+            tt(ft("f", 256, 384), x0, x1, A.mult)
         else:
             cp(ft("f", 0, 384), pr)
         tt(ft("g", 1, 384), pr, ft("f", 0, 384), A.subtract)
-        ts(w("H2"), w("KS"), 1, 0xF0, SHR, AND)
+        ts(w("H2"), k1, 1, 0xF0, SHR, AND)
         S(ft("h", 7, 256), w("H2"), F.Copy, scale=1.0 / 16)
         S(ft("i", 8, 256), w("H2"), F.Square, scale=1.0 / 16)
-        rows = ["FT.c%d" % k for k in (4, 5, 252, 253, 6)] + ["FT.%d%s" % (y, k) for k in "abcdefghi"]
-        MM(blk(by, 0), also(v("FT", 384 * y + 252, 384 * y + 380), *rows), v("mI"))
+        rows = ["FT.%d%s" % (y, k) for k in "abcdefghi"]
         for e in range(2):
             MM(v(by, 128 + e, 384, 2), also(blk("FT", 3 * y + e), *rows), v("mI"))
-        if "A" in ONV:
+        MM(blk(bx if "F" in ONV else by, 0), also(v("FT", 384 * y + 252, 384 * y + 380), *rows), v("mI"))
+        if "F" in ONV:
+            S(v("FA", 400 * y + 131, 400 * y + 387), v(by, 128, 384), F.Copy)
+            cp(v("FA", 400 * y + 3, 400 * y + 131), v(bx, 0, 128))
+        elif "A" in ONV:
             cp(v("FA", 400 * y + 3, 400 * y + 387), v(by, 0, 384))
         else:
             S(v("FA", 400 * y + 3, 400 * y + 387), v(by, 0, 384), F.Copy)
-        tt(w("G2"), w("KS"), w("L2"), A.add)
-        ts(w("GM"), w("G2"), 11, 15, SHR, AND)
-        ts(w("PN"), k1, 0.0, BIG, A.is_lt, A.mult)
-        tt(w("ZZ"), w("GM"), w("H2"), A.subtract)
-        tt(blk("WN", 2 * y + 1, 8), w("ZZ"), w("PN"), A.add)
+        useless = lambda z: v("RN", 128 * (2 * t + z) + RHO[t], 128 * (2 * t + z) + 128, 16)
+        ts(w("GM"), k1, 11, 15, SHR, AND)
+        tt(useless(y), k1, w("L2"), A.is_lt)
+        tt(blk("WN", 2 * y + 1, 8), w("GM"), w("H2"), A.subtract)
+        yield
         if more and y == 1:
-            MM(v("bk7", 0, 16), blk("mON", 0), v("PN"))
-            S(v("MJ"), v("bk7", 0, 16), scale=1.0 / BIG, accum=v("MC", 0, 1))
-            S(v("MW"), v("MC", 0, 1), scale=1.0 / 256, bias=col(46))
+            for z in range(2):
+                MM(blk(bw, z, 8), blk("mON", 0), useless(z))
+            S(v("MJ"), v(bw, 0, 16), bias=3072.0, accum=v("MC", 0, 1))
+            S(v("MW"), v("MC", 0, 1), scale=1.0 / 256, bias=-127.5 / 256)
             S(v("MC", 1, 2), v("MW"), scale=-256.0, bias=v("MC", 0, 1))
-            S(v("LR", rows=LOW), v("THR", rows=LOW), bias=v("MC", 1, 2, rows=LOW))
+            S(v("mL", rows=quarter[1], tag=1), v("mI", rows=quarter[1]), scale=0.0, bias=v("MC", 1, 2, rows=quarter[1]))
             S(v("MC", 2, 3), v("MC", 1, 2), scale=2048.0)
             S(v("L2"), v("TH2"), bias=v("MC", 2, 3))
         if "B" in ONV:
@@ -447,6 +482,7 @@ def rank_program(g, core, T, topo):
             S(b("VB"), ind(blk("WN", y, 16), blk("cBR", t, 8)), scale=1.0 / 32)
         MM(blk(bz, 0), blk("mCR", t), blk("mON", 0), True, False)
         MM(blk(bz, 0), blk("mFN", t), b("ZN"), False, False)
+        MM(blk(bz, 0), blk("RN", 2 * t + y), v("mIN"), False, False)
         MM(blk(bz, 0), b("VB"), v("mI"), False, True)
         out, land = blk("TS", 2 * t + y), blk("TB%d" % (t + 1), y)
         tt(out, b("TR"), blk(bz, 0), A.min)
@@ -454,28 +490,29 @@ def rank_program(g, core, T, topo):
         dst, src = T.cores[(rank + step) % N], T.cores[(rank - step) % N]
         rid, pid, _se = topo.addr(dst)
         arr = "arr%d_%d" % (t + 1, y)
-        run("g", lambda e: e.remote_dma(land[0], out[0], T.sem[arr], T.sem["snd"], pid, rid, topo.mask(core, dst)), out[1], land[1], 100.0, FAR,
+        run("g", lambda e: e.remote_dma(land[0], out[0], T.sem[arr], T.sem["snd"], pid, rid, topo.mask(core, dst)), out[1], land[1], 100.0, FAR if sent[0] else FAR + FIRST,
             (arr, len(topo.engines(src, core))))
         sent[0] += len(topo.engines(core, dst))
         fa = lambda lo, hi, step=1, rows=ALL: v("FA", 400 * y + lo, 400 * y + hi, step, rows=rows)
-        todo = []
-        for gr in range(4):
-            bank, rows = (bz, bx)[gr % 2], slice(32 * gr, 32 * gr + 7)
+        for gr, bank in enumerate((by, bx, bz, by)):
+            rows = slice(32 * gr, 32 * gr + 7)
             for be in range(2):
-                c0, n = 198 * (gr // 2) + 67 * be, 64 * be + 67
-                tile = ("tile" + bank, be, be + 1) if gr < 2 else ("tile" + bank, 0, 2 - 2 * be)
-                MM(also(v(bank, c0, c0 + n), tile), fa(131 + 128 * be, 259 + 128 * be, rows=rows), fa(0, n, rows=rows), True, False)
+                c0, n = 67 * be, 64 * be + 67
+                MM(v(bank, c0, c0 + n), fa(131 + 128 * be, 259 + 128 * be, rows=rows), fa(0, n, rows=rows), True, False)
                 MM(v(bank, c0 + n - 64, c0 + n), v("mI"), v("mTR"), False, True)
-                todo.append((gr % 2, v("RD", 8 * y + 4 * be + gr, 8 * y + 4 * be + gr + 1), v(bank, c0, c0 + n)))
-        for side, out1, a in sorted(todo, key=lambda x: -x[0]):
-            least(out1, a)
+            for be in range(2):
+                c0, n = 67 * be, 64 * be + 67
+                least(v("RD", 8 * y + 4 * be + gr, 8 * y + 4 * be + gr + 1), v(bank, c0, c0 + n))
         l16 = lambda name: blk(name, y, 16)
         for k in range(16):
-            MM(v(by, 0, 16), blk("mS", k), fa(131 + k, 387, 16), k == 0, k == 15)
-        MM(blk(by, 1, C), v("mW"), fa(131, 387))
-        ts(l16("OL0"), v(by, 0, 16), 2048.0, 0.0, A.add, A.max)
+            MM(v(bw, 0, 16), blk("mS", k), fa(131 + k, 387, 16), k == 0, k == 15)
+        MM(blk(bw, 1, C), v("mW"), fa(131, 387))
+        if "O" in ONV:
+            ts(l16("OL0"), v(bw, 0, 16), 2048.0, 0.0, A.add, A.max)
+        else:
+            S(l16("OL0"), v(bw, 0, 16), F.Relu, bias=2048.0)
         S(blk("UG", y, C), ind(U, l16("OL0")), F.Copy)
-        S(blk("W1", y, C), blk(by, 1, C), F.Sign, bias=col(48))
+        S(blk("W1", y, C), blk(bw, 1, C), F.Sign, bias=col(48))
         tt(b("FE"), ind(w("RD"), v("cBL", 0, 8)), v("cK"), A.is_le)
         for half in HALF:
             for be in range(2):
@@ -489,12 +526,13 @@ def rank_program(g, core, T, topo):
     codes(0, 0)
     codes(0, 1)
     for t in range(RO):
-        visit(t, 0)
-        visit(t, 1)
+        parts = [visit(t, 0), visit(t, 1)]
+        for part in [parts[k] for k in TURN]:
+            next(part, None)
 
     ends = []
     for y in range(2):
-        bx, by, half = "bk%d" % (1 + 3 * y), "bk%d" % (2 + 3 * y), HALF[y]
+        bx, by, half = "bk%d" % (4 * y), "bk%d" % (4 * y + 1), HALF[y]
         MM(v(by, 0, C, rows=half), v("mH", 0, 64), v("mON"), True, False)
         for e in range(2):
             MM(v(by, e, C, 2, rows=half), blk("mI32", e, 64), blk("TB%d" % RO, y), False, e == 1)

from concourse.mybir import AluOpType as A, AxisListType, ActivationFunctionType as F

N = 4
RO = 6
C = 256
H = 128
W = 4096
UW = 5136
VOID = 4096
SPARE = 4100
NONE = 16384.0
BIG = 2.0 ** 20
KEEP = 2.0 ** 17
PLAN = "SNII"
PIECE = 32
LEAD, SHORT = 2000.0, 3.0
ONV = "PTWCF"
TURNS = 1
TURN = (0, 1, 0, 1)
BOTH, SFIX, FIRST = 1.0, 0.0, 2000.0
AHEAD, FIT = 0.0, 60.0
RHO = [(5 * t) % 16 for t in range(RO)]
CYCLE, PE, GATHER, SCATTER, HOP, FAR, RATE = 0.83, 0.42, 1.4, 3.8, 200.0, 1500.0, 300.0

SCRATCH = {}
for _n, _w, _d in [
    ("U0", UW, "bfloat16"), ("U1", UW, "bfloat16"), ("R", W, "bfloat16"), ("M", W, "bfloat16"), ("KP", W, "float16"),
    ("P", C, "bfloat16"), ("P1", C, "bfloat16"), ("TI", C, "int32"), ("QF", C, "float32"), ("FI", C, "int32"), ("XI", C, "int32"),
    ("OFF", C, "uint16"), ("CM", C, "float16"), ("ZN", C, "float16"), ("TR", C, "float16"), ("WP", C, "float16"),
    ("S1", 272, "int32"), ("S2", C, "int32"), ("S3", C, "float32"), ("ST", C, "bfloat16"), ("VB", C, "float16"),
    ("W1", 2 * C, "bfloat16"), ("UG", 2 * C, "bfloat16"), ("FE", C, "bfloat16"),
    ("FT", 768, "float16"), ("FA", 800, "float16"),
    ("AV", 16, "int32"), ("AB", 16, "bfloat16"), ("AG", 16, "int32"), ("H2", 16, "int32"), ("GM", 16, "int32"),
    ("PX", W, "bfloat16"), ("P0", C, "bfloat16"), ("PU", 16, "bfloat16"), ("RN", C * RO, "bfloat16"), ("PV", 16, "bfloat16"),
    ("WN", 32, "int32"), ("X", 16, "float32"), ("PR", 32, "float32"), ("RD", 16, "float32"),
    ("OL0", 32, "uint16"), ("OL", 32, "uint16"),
    ("LR", 272, "float16"), ("L2", 32, "float32"), ("TH2", 32, "float32"), ("THI", 1, "int32"), ("THF", 1, "float32"), ("TH8", 16, "float32"),
    ("MC", 4, "float32"), ("MW", 1, "bfloat16"), ("MJ", 16, "float32"),
    ("OUTT", C, "float32"), ("OUTC", C, "float32"), ("TS", C * RO, "float16"),
    ("cM", 128, "int32"), ("cD", 128, "int32"), ("cJ", 128, "int32"), ("cH", 128, "int32"), ("cT", 128, "int32"), ("cG", 16, "int32"), ("cP", 1, "int32"), ("cI", 8, "int32"),
    ("cF", 64, "float32"), ("cV", 16, "int32"), ("cW", 16, "int32"), ("cA", 128, "bfloat16"), ("cB", 128, "bfloat16"), ("cC", 128, "bfloat16"), ("cE", 128, "bfloat16"),
    ("cDD", 128, "bfloat16"), ("cBM", 128, "bfloat16"),
    ("mI", 128, "bfloat16"), ("mI17", 136, "bfloat16"), ("mIG", 136, "bfloat16"), ("mI16", 136, "bfloat16"), ("mN16", 136, "bfloat16"), ("mN1", 128, "bfloat16"), ("mP", 136, "bfloat16"),
    ("mI32", 128, "bfloat16"), ("mIK", 128, "bfloat16"), ("mIN", 128, "bfloat16"), ("mH", 128, "bfloat16"),
    ("mPT", 128 * RO, "bfloat16"), ("mFN", 128 * RO, "bfloat16"), ("mF0", 128, "bfloat16"), ("mCR", 128 * RO, "float16"), ("mC0", 128, "float16"),
    ("mD", 128, "bfloat16"), ("mV", 8, "bfloat16"), ("mL", 128, "float16"), ("mON", C, "bfloat16"), ("mOF", 128, "float32"),
    ("mRF", 16, "float16"), ("mTR", 64, "bfloat16"), ("mS", 2048, "bfloat16"), ("mW", 128, "bfloat16"), ("cX", 128, "bfloat16"), ("cY", 128, "bfloat16"), ("cZ", 136, "bfloat16"),
    ("cAG", 1024, "bfloat16"), ("c32", 136, "bfloat16"), ("c1", 128, "bfloat16"), ("cPA", 128, "bfloat16"), ("cK", 128, "bfloat16"),
    ("cBL", 128, "uint16"), ("cBR", 8 * RO, "uint16"),
]:
    SCRATCH[_n] = ("sbuf", [128, _w], _d)
for _t in range(RO + 1):
    SCRATCH["TB%d" % _t] = ("sbuf", [128, C], "float16")
for _b in range(8):
    SCRATCH["bk%d" % _b] = ("psum", [128, 512], "float32")
DMAS = 11
SEMAPHORES = ["v", "s", "p", "g", "snd"] + ["arr%d_%d" % (t, e) for t in range(1, RO + 1) for e in range(2)] + ["dma%d" % k for k in range(DMAS)]
AND, SHR = A.bitwise_and, A.arith_shift_right
ALL, LOW, HIGH = slice(0, 128), slice(0, 64), slice(64, 128)
HALF = (LOW, HIGH)


def arrange(calls):
    touch, before = {}, []
    for k, c in enumerate(calls):
        pre = {}
        for views, wr in ((c["reads"], False), (c["writes"], True)):
            for b, lo, hi in views:
                keep = []
                for e in touch.get(b, []):
                    j, l2, h2, w2 = e
                    if b.startswith("bk"):
                        hit = wr or w2 or calls[j]["q"] != c["q"]
                        gone = wr
                    else:
                        hit = (wr or w2) and l2 < hi and lo < h2
                        gone = wr and lo <= l2 and h2 <= hi
                    if hit and j != k:
                        free = b.startswith("bk") and c["q"] == "p" and calls[j]["q"] == "p"
                        pre[j] = max(pre.get(j, 0.0), 0.0 if free else HOP + calls[j]["late"])
                    if not gone:
                        keep.append(e)
                keep.append((k, lo, hi, wr))
                touch[b] = keep
        if c["q"] == "y":
            pre.update({j: pre.get(j, 0.0) for j in range(k) if calls[j]["q"] == "y"})
        before.append(pre)
    way = [c["time"] + c["late"] + (LEAD if c["writes"][0][0] in ("yc0", "yt0") else 0.0) for c in calls]
    after, left = [[] for c in calls], [len(pre) for pre in before]
    for k in range(len(calls) - 1, -1, -1):
        for j, gap in before[k].items():
            way[j] = max(way[j], calls[j]["time"] + gap + way[k])
            after[j].append(k)
    ready, free, start = {q: {} for q in "vspgy"}, {q: 0.0 for q in "vspgy"}, {}
    for k, c in enumerate(calls):
        if not left[k]:
            ready[c["q"]][k] = 0.0
    while len(start) < len(calls):
        t, q = min((max(free[q], min(r.values())), q) for q, r in ready.items() if r)
        rank = lambda k: (SHORT * calls[k]["time"] - way[k], k)
        k = min((k for k, x in ready[q].items() if x <= t), key=rank)
        soon = [m for m, x in ready[q].items() if t < x < t + calls[k]["time"] - FIT and way[m] > way[k] + AHEAD]
        if soon and AHEAD:
            m = min(soon, key=rank)
            k = min((n for n, x in ready[q].items() if max(x, t) + calls[n]["time"] <= ready[q][m] + FIT), key=rank, default=m)
            t = max(t, ready[q][k])
        del ready[q][k]
        start[k], free[q] = t, t + calls[k]["time"]
        for m in after[k]:
            left[m] -= 1
            if not left[m]:
                ready[calls[m]["q"]][m] = max(start[j] + calls[j]["time"] + gap for j, gap in before[m].items())

    def place(order, links, least):
        start, busy = {}, {}
        for k in order:
            d, line = calls[k]["time"], busy.setdefault(calls[k]["q"], [])
            t = max([start[j] + calls[j]["time"] + gap for j, gap in links[k].items()] + [least[k]])
            at = len(line)
            while at and line[at - 1][1] > t:
                at -= 1
            while at < len(line) and line[at][0] < t + d:
                t = max(t, line[at][1])
                at += 1
            line.insert(at, (t, t + d))
            start[k] = t
        return start
    every = range(len(calls))
    behind = [{m: before[m][k] for m in after[k]} for k in every]
    for turn in range(TURNS):
        late = [0.0 if after[k] else calls[k]["late"] for k in every]
        start = place(sorted(every, key=lambda k: (-start[k] - calls[k]["time"] - late[k], -k)), behind, late)
        start = place(sorted(every, key=lambda k: (-start[k] - calls[k]["time"], k)), before, [0.0] * len(calls))
    return sorted(every, key=lambda k: (start[k], k))


def rank_program(g, core, T, topo):
    rank = T.rank_of(core)
    if rank is None:
        return
    queue = {"v": g.vector, "s": g.scalar, "p": g.tensor, "g": g, "y": g.sync}
    calls = []

    def run(q, call, reads, writes, time, late=0.0, signal=None):
        spans = lambda views: [(x, 0, 1 << 20) if isinstance(x, str) else x for x in views]
        calls.append({"q": q, "call": call, "reads": spans(reads), "writes": spans(writes), "time": time, "late": late, "signal": signal})

    dmas = []

    def dma(q, out, in_, reads, writes, size):
        sem = "dma%d" % len(dmas)
        dmas.append(size)
        run(q, lambda e: e.dma_start(out, in_).then_inc(T.sem[sem], 16), reads, writes, 60.0, FAR + (sum(dmas) if size else 0) / RATE, (sem, 16))
        return sem

    def v(name, lo=0, hi=None, step=1, tag=None, rows=ALL):
        if hi is None:
            hi = T[name].shape[1]
        n = len(range(lo, hi, step))
        if name.startswith("bk"):
            return T[name][rows, lo:hi:step], [name], n, 0, False
        return T[name][rows, lo:hi:step], [(name if tag is None else name + "." + str(tag), lo, hi)], n, 2 if "16" in SCRATCH[name][2] else 4, False, rows

    def ind(win, off):
        return win[0].indirect(off[0]), win[1] + off[1], 16 * off[2], win[3], True

    def also(view, *names):
        return (view[0], view[1] + list(names)) + view[2:]

    def sc(x):
        return x if isinstance(x, tuple) else (x, [])

    def vtime(out, ins, rate=None):
        if out[4]:
            return 50 + out[2] * SCATTER * CYCLE
        if ins[0][4]:
            return 50 + out[2] * GATHER * CYCLE
        if rate is None:
            rate = 0.5 if all(x[3] == 2 for x in [out] + ins) else 1.0
        return max(64, ins[0][2] * rate) * CYCLE

    def ts(out, in0, s1, s2, op0, op1=None):
        s1, s2 = sc(s1), sc(s2)
        more = () if op1 is None else (op1,)
        run("v", lambda e: e.tensor_scalar(out[0], in0[0], s1[0], s2[0], op0, *more), in0[1] + s1[1] + s2[1], out[1], vtime(out, [in0]))

    def tt(out, a, b, op):
        run("v", lambda e: e.tensor_tensor(out[0], a[0], b[0], op), a[1] + b[1], out[1], vtime(out, [a, b], (BOTH if a[3] == b[3] == out[3] == 2 else 2.0) if a[3] and b[3] else 1.0))

    def cp(out, a):
        run("v", lambda e: e.tensor_copy(out[0], a[0]), a[1], out[1], vtime(out, [a]))

    def ms(out, x):
        run("v", lambda e: e.memset(out[0], x), [], out[1], vtime(out, [out]))

    def scan(out, d0, d1, op0, op1):
        run("v", lambda e: e.tensor_tensor_scan(out[0], d0[0], d1[0], 0.0, op0, op1), d0[1] + d1[1], out[1], vtime(out, [d0, d1]))

    def least(out, a):
        run("v", lambda e: e.tensor_reduce(out[0], a[0], AxisListType.X, A.min, apply_absolute_value=True), a[1], out[1], vtime(out, [a], 1.0))

    def S(out, in_, func=F.Identity, scale=1.0, bias=0.0, accum=None):
        scale, bias = sc(scale), sc(bias)
        k = {} if accum is None else {"accum_out": accum[0]}
        run("s", lambda e: e.activation(out[0], in_[0], func, bias=bias[0], scale=scale[0], **k),
            in_[1] + scale[1] + bias[1], out[1] + ([] if accum is None else accum[1]), 65 + out[2] * GATHER * CYCLE if in_[4] else SFIX + max(64, out[2]) * CYCLE)

    def put(out, x):
        S(out, v("cM", 0, out[2], rows=out[5]), scale=0.0, bias=x)

    def MM(out, lhsT, rhs, start=True, stop=True):
        run("p", lambda e: e.matmul(out[0], lhsT[0], rhs[0], start, stop), lhsT[1] + rhs[1], out[1], max(64, rhs[2]) * PE * (4 if rhs[3] == 4 else 1))

    def iota(out, pattern, base, cm):
        run("g", lambda e: e.iota(out[0], pattern, base, cm, allow_small_or_imprecise_dtypes=out[3] == 2), [], out[1], 130 + 2 * out[2] * CYCLE)

    def fill(out, src, pattern, base, cm, value, op=A.not_equal):
        run("g", lambda e: e.affine_select(out[0], src[0], pattern, op, value, base, cm), src[1], out[1], 170 + 2 * out[2] * CYCLE)

    def col(k, rows=ALL):
        return v("cF", k, k + 1, rows=rows)

    def blk(name, k, n=128, rows=ALL, tag=None):
        return v(name, n * k, n * k + n, rows=rows, tag=tag)

    dma("y", T.TI[:], T.tst[:], [], ["TI"], 131072)
    dma("s", T.P[:], T.pr[:], [], ["P"], 65536)
    for y in range(2):
        if y:
            dma("s", T.THI[0:8, :], T.th[:], [], ["THI"], 32)
        for e in range(2):
            dma("y", T["U%d" % y][HALF[e], 0:W], T.cov[HALF[y], :], [], ["U%d.%d" % (y, e)], 524288)

    iota(v("cD"), [[1, 128]], 256, -1)
    iota(v("cM"), [[1, 128]], 0, 0)
    iota(v("cP"), [[0, 1]], 0, 1)
    iota(v("cV", 0, 8), [[77, 8]], 0, 0)
    iota(v("cV", 8, 16), [[5, 8]], 0, 0)
    ms(v("mON"), 1.0)
    for k, (s1, op) in enumerate(((4, SHR), (15, AND), (31, AND), (3, SHR), (7, AND), (1, SHR))):
        ts(v("cI", k, k + 1), v("cP"), s1, None, op)
    ts(v("cH"), v("cM"), 4, None, SHR)
    ts(v("cT"), v("cD"), 15, None, AND)
    ts(v("cJ"), v("cM"), 15, None, AND)
    cp(v("cF", 0, 6), v("cI", 0, 6))
    ts(v("cB"), v("cT"), 1.0, None, A.mult)
    ts(v("cBM"), v("cH"), col(0), None, A.is_equal)
    ts(col(6), col(1), 613.0, None, A.mult)
    ts(v("cA"), v("cBM"), -100.0, 100.0, A.mult, A.add)
    ts(v("cW", 0, 8), v("cV", 0, 8), col(6), None, A.add)
    tt(v("cDD"), v("cB"), v("cA"), A.add)
    ts(v("cW", 0, 8), v("cW", 0, 8), W - 1, None, AND)
    ts(v("cW", 8, 16), v("cV", 8, 16), 15, None, AND)

    def eqm(out, val, scale):
        ts(out, v("cDD"), float(val), float(scale), A.is_equal, A.mult)
    ts(v("cF", 8, 16), v("cW", 0, 8), -0.5, None, A.add)
    eqm(v("mI"), 0, 1)
    cp(v("cBL"), v("cM"))
    S(v("VB"), v("TI"), scale=1.0 / 32, bias=1.0 / 64)
    S(v("ZN"), v("TI"), F.Relu, scale=NONE - 8, bias=-255.0 * (NONE - 8))
    for names, bank in ((("VB", "ZN"), "bk2"), (("P",), "bk3")):
        for y in range(2):
            for e in range(2):
                for name in names:
                    MM(blk(bank, y, rows=HALF[e]), blk("mI", y, 64), v(name, e, C, 2), name == names[0], name == names[-1])
    cp(v("TB0"), v("bk2", 0, C))
    S(v("P0"), v("bk3", 0, C), bias=-128.0)
    n = 32 * PLAN.count("S")
    for y in range(2):
        ms(v("U%d" % y, W, UW), -1.0)
        if n:
            put(v("P1", H * y, H * y + n), 0.0)
        S(v("P1", H * y + n, H * y + H), v("P0", H * y + n, H * y + H), F.Copy)
        n2 = 32 * (4 - PLAN.count("I"))
        S(v("PX", 2048 * y, 2048 * y + 16 * n2), ind(blk("P0", y), v("cBL", 0, n2)), F.Copy)
    ms(v("cAG", 0, 16 * PIECE), 1.0 / 16)
    put(v("cAG", 0, 16 * PIECE, 16), -32768.0)
    iota(v("cZ"), [[0, 136]], 0, 0)
    fill(v("mI17"), v("cZ"), [[-16, 8], [-1, 17]], 1, 1, 1.0)
    fill(v("mI17"), v("mI17"), [[0, 8], [1, 17]], 0, 0, 0.0)
    for name, x in (("mIG", 2048.0), ("mI16", 16.0), ("mN16", -16.0), ("mP", -32768.0)):
        S(v(name), v("mI17"), F.Copy, scale=x)
    for name, x in (("mN1", -1.0), ("mI32", 32.0), ("mIK", KEEP), ("mIN", NONE)):
        S(v(name), v("mI"), F.Copy, scale=x)
    put(v("mH"), -1.0 / 256)
    eqm(v("cC"), 15, -1.0 / 64)
    fill(v("cC"), v("cC"), [[0, 8], [1, 16]], -15, 0, 0.0)
    eqm(v("cE"), 0, 1.0 / 64)
    tt(v("mD"), v("cE"), v("cC"), A.add)
    ts(v("mV"), v("cM", 0, 8), col(0), 16.0, A.is_equal, A.mult)
    for name, x, n in (("c32", 32.0, 17), ("c1", 1.0, 16)):
        ms(v(name), x)
        put(v(name, 0, 8 * n, n), -2.0 ** 26)
    S(v("cPA"), v("cJ"), scale=-1.0, bias=15.0)
    top8 = slice(0, 8)
    put(v("mOF", rows=slice(0, 32)), 1.0)
    cp(v("THF", rows=top8), v("THI", rows=top8))
    iota(v("cG"), [[4, 2], [0, 2], [1, 4]], 0, 0)
    ts(v("TH8", rows=top8), v("cG", rows=top8), col(1, top8), v("THF", rows=top8), A.is_equal, A.mult)
    MM(v("bk7", 0, 16), v("mOF", rows=top8), v("TH8", rows=top8))
    quarter = [slice(32 * k, 32 * k + 32) for k in range(4)]
    ms(v("LR", rows=slice(0, 96), tag=0), 0.0)
    S(v("LR", 0, 272, 17, rows=quarter[0], tag=0), v("bk7", 0, 16, rows=quarter[0]), bias=-2048.0)
    for name in ("TH2", "L2"):
        S(v(name, 0, 16), v("bk7", 0, 16), F.Copy, scale=2048.0)
        S(v(name, 16, 32), v("bk7", 0, 16), scale=2048.0, bias=-512.0)
    ms(v("LR", rows=quarter[3], tag=3), 768.5)
    for k, (first, left) in enumerate(((None, 64.0), (64.0, 0.0), (64.0, 2048.0), (-48.0, 1.0))):
        if k:
            put(also(v("LR", 0, 272, 17, rows=quarter[k], tag=k), "LR.0"), first)
        ms(v("mL", rows=quarter[k], tag=k), left)
    ts(v("cF", 16, 24), v("cW", 8, 16), col(1), 8.0, A.is_equal, A.mult)
    ts(v("cF", 24, 32), v("cW", 8, 16), col(1), None, A.not_equal)
    ts(v("cF", 32, 40), v("cW", 8, 16), col(1), NONE, A.is_equal, A.mult)
    S(col(48), col(1), F.Square, bias=-15.0)
    ts(v("cA"), v("cD"), 256.0, 2.0, A.is_gt, A.mult)
    tt(v("cB"), v("cA"), v("cBM"), A.mult)
    eqm(v("cE"), 0, 2)
    tt(v("mF0"), v("cB"), v("cE"), A.subtract)
    put(v("mC0", rows=LOW, tag=0), 511.75)
    put(v("mC0", rows=HIGH, tag=1), 1.0 / 4096)
    for t in range(RO):
        eqm(blk("mPT", t), (-(1 + t)) % 16, 256)
        iota(blk("RN", t, C), [[0, C]], 0, 0)
        ts(blk("cBR", t, 8), v("cM", 0, 8), col(16 + t), None, A.add)
        fill(blk("mFN", t), v("mF0"), [[0, 8], [1, 16]], -RHO[t], 0, 0.0)
        fill(blk("mCR", t), also(v("mC0", tag=0), "mC0.1"), [[0, 8], [1, 16]], -RHO[t], 0, (7.5 + 1.0 / 64) / 128)
    ms(also(v("FT"), *["FT.%d%s" % (y, k) for y in range(2) for k in "abcdefghi"]), 0.0)
    ts(col(50), col(2), 2.0, None, A.is_equal)
    ts(col(51), col(2), 4.0, None, A.is_equal)
    for lo, x in ((4, -1.0), (5, -1.0), (28, -1.0), (29, -1.0), (6, 1.0)):
        put(also(v("FT", lo, 768, 32), "FT.0e", "FT.1e"), x)
    for y in range(2):
        ts(v("FA", 400 * y, 400 * y + 1), col(2), 6.0, None, A.is_equal)
        for k, x in ((1, 32.0), (2, -33.0)):
            S(v("FA", 400 * y + k, 400 * y + k + 1), col(51), scale=x, bias=col(50))
    ts(v("mTR"), v("cM", 0, 64), col(5), 16384.0, A.is_ge, A.mult)
    for e in range(2):
        ts(col(52 + e), v("cP"), 4.0, SPARE + 512.0 * e, A.mult, A.add)
        ts(blk("mRF", e, 8), v("cM", 0, 8), col(0), col(52 + e), A.is_equal, A.mult)
    ts(v("cK"), v("cJ"), col(1), -1.0, A.is_equal, A.add)
    fill(v("cX"), v("cZ", 0, 128), [[0, 2], [-32, 4], [0, 16]], -2, 1, 64.0)
    for k in range(16):
        fill(blk("mS", k), v("cX"), [[0, 8], [1, 16]], -k, 0, 0.0, A.is_equal)
    S(v("cY"), v("cPA"), F.Copy, scale=-2.0)
    fill(v("mW"), v("cY"), [[0, 2], [-32, 4], [0, 16]], -7, 1, 0.0, A.is_equal)
    fill(v("mW"), v("mW"), [[0, 2], [-32, 4], [0, 16]], -8, 1, 1.0)

    def codes(t, y):
        tb = blk("TB%d" % t, y)
        qf = blk("QF", y)
        turned = blk("bk%d" % (4 * y), 0)
        MM(turned, blk("mPT", t), tb)
        tt(qf, tb, turned, A.mult)
        ts(blk("FI", y), blk("QF", y), col(8 + t), BIG, A.add, A.min)
        ts(blk("XI", y), blk("FI", y), 0x7FFF8FFF, None, AND)
        ts(blk("OFF", y), blk("XI", y), float(VOID), None, A.min)
        if "C" in ONV:
            ts(blk("CM", y), blk("OFF", y), -2048.0, None, A.add)
        else:
            S(blk("CM", y), blk("OFF", y), bias=-2048.0)
        if "Z" in ONV:
            ts(blk("ZN", y), tb, -8.0, 0.0, A.add, A.max)
        else:
            S(blk("ZN", y), tb, F.Relu, bias=-8.0)
        if "T" in ONV:
            ts(blk("TR", y), tb, col(32 + t), None, A.max)
        else:
            S(blk("TR", y), tb, scale=col(24 + t), bias=col(32 + t))

    sent = [0]

    def visit(t, y):
        more = t < RO - 1
        bx, by, bz, bw = ("bk%d" % (k + 4 * y) for k in range(4))
        U = also(v("U%d" % y), "U%d.0" % y, "U%d.1" % y)
        w = lambda name: blk(name, y, 8)
        b = lambda name: blk(name, y)
        top = lambda name: v(name, 128 * y + 15, 128 * y + 128, 16)
        mi = lambda i, n=1: v("M", 2048 * y + 128 * i, 2048 * y + 128 * (i + n))
        ri = lambda i: v("R", 2048 * y + i, 2048 * y + 2048, 16)
        key = v(bx, 256, 392)
        for c0 in range(H * y, H * y + H, PIECE):
            r = v("R", 16 * c0, 16 * (c0 + PIECE))
            S(r, ind(U, v("OFF", c0, c0 + PIECE)), bias=-128.0)
            scan(v("KP", 16 * c0, 16 * (c0 + PIECE)), v("cAG", 0, 16 * PIECE), r, A.add, A.max)
        for i in range(16):
            MM(v(bz, i, 128, 16), ri(i), v("mV"))
        scan(b("S2"), v("c1"), blk(bz, 0), A.add, A.max)
        S(w("PV"), top("S2"), F.Relu, scale=-4.0, bias=-4.0 * 32881)
        ts(w("AV"), top("S2"), 15, None, AND)
        S(w("AB"), w("AV"), F.Copy)
        kp = v("KP", 2048 * y + 15, 2048 * y + 2048, 16)
        if "W" in ONV:
            ts(b("WP"), kp, 1536.0, None, A.add)
        else:
            S(b("WP"), kp, bias=1536.0)
        MM(key, b("P1"), v("mP"), True, False)
        MM(key, also(v("mL", tag=0), "mL.1", "mL.2", "mL.3"), also(blk("LR", y, 136, tag=0), "LR.1", "LR.2", "LR.3"), False, False)
        for k, how in enumerate(PLAN):
            if how == "S":
                bank = (by, bw)[k % 2]
                MM(v(bank), v("mI"), blk("R", 4 * y + k, 512), True, False)
                MM(v(bank), v("mN1"), blk("PX", 4 * y + k, 512), False, True)
                S(blk("M", 4 * y + k, 512), v(bank), F.Relu)
            elif how == "N":
                tt(blk("M", 4 * y + k, 512), blk("R", 4 * y + k, 512), blk("PX", 4 * y + k, 512), A.max)
        lo = 32 * (4 - PLAN.count("I"))
        for i in range(16 if lo < H else 0):
            tt(v("M", 2048 * y + 16 * lo + i, 2048 * y + 2048, 16, tag="%d.%d" % (y, i)), v("R", 2048 * y + 16 * lo + i, 2048 * y + 2048, 16),
               v("P0", 128 * y + lo, 128 * y + 128), A.max)
        MM(key, kp, v("mI16"), False, False)
        for i in range(16):
            MM(key, also(v("M", 2048 * y + i, 2048 * y + 2048, 16), "M.%d.%d" % (y, i)), v("mIG"), False, False)
        MM(v(bx, 256, 392, 17), v("mI"), w("PV"), False, False)
        MM(v(bx, 256, 392, 17), v("mI"), w("AB"), False, False)
        MM(key, b("WP"), v("mN16"), False, True)
        k1 = v("S1", 136 * y + 16, 136 * y + 136, 17)
        scan(blk("S1", y, 136), v("c32"), key, A.add, A.max)
        ts(w("AG"), k1, 15, None, AND)
        tt(w("PU"), k1, blk("L2", 2 + y, 8), A.is_ge)
        MM(blk(bx, 0), b("CM"), v("mD"), True, False)
        MM(v(bx, 15, 128, 16), v("mIK"), w("PU"), False, True)
        tt(b("ST"), ind(w("AG"), v("cBL", 0, 8)), v("cPA"), A.is_gt)
        scan(b("S3"), b("ST"), blk(bx, 0), A.mult, A.add)
        ft = lambda tag, lo, hi: v("FT", 384 * y + lo, 384 * y + hi, 32, tag="%d%s" % (y, tag))
        x, x0, x1, pr = ft("a", 2, 256), ft("a", 2, 128), ft("a", 130, 256), v("PR", 16 * y, 16 * y + 12)
        ts(blk("WN", 2 * y, 8), top("S3"), 4.0, 128.0 - 7.5 / 16, A.mult, A.add)
        ts(x, top("S3"), -KEEP, -33.0, A.add, A.max)
        if "q" in ONV:
            tt(v("PR", 16 * y, 16 * y + 8), x, x, A.mult)
        else:
            S(v("PR", 16 * y, 16 * y + 8), x, F.Square)
        tt(v("PR", 16 * y + 8, 16 * y + 12), x0, x1, A.mult)
        for tag, lo, hi, a in (("b", 3, 256, x), ("c", 254, 380, x0), ("d", 255, 380, x1)):
            if tag in ONV:
                cp(ft(tag, lo, hi), a)
            else:
                S(ft(tag, lo, hi), a, F.Copy)
        tt(ft("e", 134, 256), x1, x0, A.subtract)
        if "p" in ONV:
            tt(ft("f", 0, 256), x, x, A.mult)
            tt(ft("f", 256, 384), x0, x1, A.mult)
        elif "P" in ONV:
            S(ft("f", 0, 256), x, F.Square)
            tt(ft("f", 256, 384), x0, x1, A.mult)
        else:
            cp(ft("f", 0, 384), pr)
        tt(ft("g", 1, 384), pr, ft("f", 0, 384), A.subtract)
        ts(w("H2"), k1, 1, 0xF0, SHR, AND)
        S(ft("h", 7, 256), w("H2"), F.Copy, scale=1.0 / 16)
        S(ft("i", 8, 256), w("H2"), F.Square, scale=1.0 / 16)
        rows = ["FT.%d%s" % (y, k) for k in "abcdefghi"]
        for e in range(2):
            MM(v(by, 128 + e, 384, 2), also(blk("FT", 3 * y + e), *rows), v("mI"))
        MM(blk(bx if "F" in ONV else by, 0), also(v("FT", 384 * y + 252, 384 * y + 380), *rows), v("mI"))
        if "F" in ONV:
            S(v("FA", 400 * y + 131, 400 * y + 387), v(by, 128, 384), F.Copy)
            cp(v("FA", 400 * y + 3, 400 * y + 131), v(bx, 0, 128))
        elif "A" in ONV:
            cp(v("FA", 400 * y + 3, 400 * y + 387), v(by, 0, 384))
        else:
            S(v("FA", 400 * y + 3, 400 * y + 387), v(by, 0, 384), F.Copy)
        useless = lambda z: v("RN", 128 * (2 * t + z) + RHO[t], 128 * (2 * t + z) + 128, 16)
        ts(w("GM"), k1, 11, 15, SHR, AND)
        tt(useless(y), k1, w("L2"), A.is_lt)
        tt(blk("WN", 2 * y + 1, 8), w("GM"), w("H2"), A.subtract)
        yield
        if more and y == 1:
            for z in range(2):
                MM(blk(bw, z, 8), blk("mON", 0), useless(z))
            S(v("MJ"), v(bw, 0, 16), bias=3072.0, accum=v("MC", 0, 1))
            S(v("MW"), v("MC", 0, 1), scale=1.0 / 256, bias=-127.5 / 256)
            S(v("MC", 1, 2), v("MW"), scale=-256.0, bias=v("MC", 0, 1))
            S(v("mL", rows=quarter[1], tag=1), v("mI", rows=quarter[1]), scale=0.0, bias=v("MC", 1, 2, rows=quarter[1]))
            S(v("MC", 2, 3), v("MC", 1, 2), scale=2048.0)
            S(v("L2"), v("TH2"), bias=v("MC", 2, 3))
        if "B" in ONV:
            ts(b("VB"), ind(blk("WN", y, 16), blk("cBR", t, 8)), 1.0 / 32, None, A.mult)
        else:
            S(b("VB"), ind(blk("WN", y, 16), blk("cBR", t, 8)), scale=1.0 / 32)
        MM(blk(bz, 0), blk("mCR", t), blk("mON", 0), True, False)
        MM(blk(bz, 0), blk("mFN", t), b("ZN"), False, False)
        MM(blk(bz, 0), blk("RN", 2 * t + y), v("mIN"), False, False)
        MM(blk(bz, 0), b("VB"), v("mI"), False, True)
        out, land = blk("TS", 2 * t + y), blk("TB%d" % (t + 1), y)
        tt(out, b("TR"), blk(bz, 0), A.min)
        step = 1 if more else -(RO - 1)
        dst, src = T.cores[(rank + step) % N], T.cores[(rank - step) % N]
        rid, pid, _se = topo.addr(dst)
        arr = "arr%d_%d" % (t + 1, y)
        run("g", lambda e: e.remote_dma(land[0], out[0], T.sem[arr], T.sem["snd"], pid, rid, topo.mask(core, dst)), out[1], land[1], 100.0, FAR if sent[0] else FAR + FIRST,
            (arr, len(topo.engines(src, core))))
        sent[0] += len(topo.engines(core, dst))
        fa = lambda lo, hi, step=1, rows=ALL: v("FA", 400 * y + lo, 400 * y + hi, step, rows=rows)
        for gr, bank in enumerate((by, bx, bz, by)):
            rows = slice(32 * gr, 32 * gr + 7)
            for be in range(2):
                c0, n = 67 * be, 64 * be + 67
                MM(v(bank, c0, c0 + n), fa(131 + 128 * be, 259 + 128 * be, rows=rows), fa(0, n, rows=rows), True, False)
                MM(v(bank, c0 + n - 64, c0 + n), v("mI"), v("mTR"), False, True)
            for be in range(2):
                c0, n = 67 * be, 64 * be + 67
                least(v("RD", 8 * y + 4 * be + gr, 8 * y + 4 * be + gr + 1), v(bank, c0, c0 + n))
        l16 = lambda name: blk(name, y, 16)
        for k in range(16):
            MM(v(bw, 0, 16), blk("mS", k), fa(131 + k, 387, 16), k == 0, k == 15)
        MM(blk(bw, 1, C), v("mW"), fa(131, 387))
        if "O" in ONV:
            ts(l16("OL0"), v(bw, 0, 16), 2048.0, 0.0, A.add, A.max)
        else:
            S(l16("OL0"), v(bw, 0, 16), F.Relu, bias=2048.0)
        S(blk("UG", y, C), ind(U, l16("OL0")), F.Copy)
        S(blk("W1", y, C), blk(bw, 1, C), F.Sign, bias=col(48))
        tt(b("FE"), ind(w("RD"), v("cBL", 0, 8)), v("cK"), A.is_le)
        for half in HALF:
            for be in range(2):
                MM(v(bz, 8 * be, 8 * be + 8, rows=half), blk("FE", 2 * y + be, 64), blk("mRF", be, 8))
        tt(l16("OL"), l16("OL0"), v(bz, 0, 16), A.max)
        run("v", lambda e: e.tensor_tensor(U[0].indirect(l16("OL")[0]), blk("UG", y, C)[0], blk("W1", y, C)[0], A.mult),
            l16("OL")[1] + blk("UG", y, C)[1] + blk("W1", y, C)[1], U[1], 50 + C * SCATTER * CYCLE)
        if more:
            codes(t + 1, y)

    codes(0, 0)
    codes(0, 1)
    for t in range(RO):
        parts = [visit(t, 0), visit(t, 1)]
        for part in [parts[k] for k in TURN]:
            next(part, None)

    ends = []
    for y in range(2):
        bx, by, half = "bk%d" % (4 * y), "bk%d" % (4 * y + 1), HALF[y]
        MM(v(by, 0, C, rows=half), v("mH", 0, 64), v("mON"), True, False)
        for e in range(2):
            MM(v(by, e, C, 2, rows=half), blk("mI32", e, 64), blk("TB%d" % RO, y), False, e == 1)
        ts(v("OUTT", rows=half, tag=y), v(by, 0, C, rows=half), 256.0, None, A.min)
        ends.append(dma("s", T.yt[half, :], T.OUTT[half, :], ["OUTT.%d" % y], ["yt%d" % y], 0))
        for i in range(16):
            MM(v(bx, 0, C, rows=half), v("mI", 0, 64), v("U%d" % y, i, W, 16), i == 0, i == 15)
        cp(v("OUTC", rows=half, tag=y), v(bx, 0, C, rows=half))
        ends.append(dma("y", T.yc[half, :], T.OUTC[half, :], ["OUTC.%d" % y], ["yc%d" % y], 0))

    count = {}
    known = {q: {} for q in queue}
    done = {}
    last = {}

    def need(q, sem, val):
        if known[q].get(sem, 0) >= val:
            return
        queue[q].wait_ge(T.sem[sem], val)
        known[q][sem] = val
        for k, x in done.get((sem, val), {}).items():
            if known[q].get(k, 0) < x:
                known[q][k] = x

    for k in arrange(calls):
        c = calls[k]
        q = c["q"]
        todo = {}
        for views, wr in ((c["reads"], False), (c["writes"], True)):
            for b, lo, hi in views:
                for l2, h2, w2, q2, s2, v2 in last.get(b, []):
                    if b.startswith("bk"):
                        hit = q2 != q or (w2 and q != "p")
                    else:
                        hit = (wr or w2) and l2 < hi and lo < h2
                    if hit and todo.get(s2, 0) < v2:
                        todo[s2] = v2
        for s2, v2 in sorted(todo.items(), key=lambda kv: -sum(done.get(kv, {}).values())):
            need(q, s2, v2)
        if c["signal"] is None:
            c["call"](queue[q]).then_inc(T.sem[q], 1)
            count[q] = count.get(q, 0) + 1
            sem, val = q, count[q]
        else:
            c["call"](queue[q])
            sem, val = c["signal"]
        far = sem.startswith("arr")
        for views, wr in (([] if far else c["reads"], False), (c["writes"], True)):
            for b, lo, hi in views:
                keep = []
                for e in last.get(b, []):
                    if b.startswith("bk"):
                        if e[3] != q or wr or not e[2]:
                            continue
                    elif wr and lo <= e[0] and e[1] <= hi:
                        continue
                    elif not wr and not e[2] and e[3] == q and lo <= e[0] and e[1] <= hi:
                        continue
                    keep.append(e)
                keep.append((lo, hi, wr, q, sem, val))
                last[b] = keep
        done[(sem, val)] = {sem: val} if far else dict(known[q], **{sem: val})
    for sem in ends:
        need("y", sem, 16)
    g.wait_ge(T.sem["snd"], sent[0])
